import numpy as np
import ml_dtypes


def mxq(x, axis, fmt="e4m3"):
    dtype, down = {"e4m3": (ml_dtypes.float8_e4m3fn, 7), "e5m2": (ml_dtypes.float8_e5m2, 14)}[fmt]
    v = np.moveaxis(np.asarray(x, np.float32).astype(ml_dtypes.bfloat16).astype(np.float64), axis, -1)
    blocks = v.reshape(v.shape[:-1] + (-1, 32))
    amax = np.abs(blocks).max(-1, keepdims=True)
    byte = np.maximum(np.where(amax > 0, np.frexp(amax)[1] - 1 + 127, 0) - down, 1)
    scale = np.exp2(byte - 127.0)
    codes = (blocks / scale).astype(np.float32).astype(dtype).astype(np.float64)
    return np.moveaxis((codes * scale).reshape(v.shape), -1, axis)


WIDE = False


def mx_kscale(k):
    if not WIDE:
        return np.ones(k)
    levels = np.array([18, -18])
    if k % 512:
        return np.exp2(np.random.permutation(np.resize(levels, k // 32))).repeat(32)
    a = np.empty((k // 512, 16))
    for p in range(k // 512):
        a[p, :8] = np.random.permutation(np.resize(levels, 8))
        for g in range(8):
            far = levels[np.abs(levels - a[p, g]) >= 10]
            a[p, g + 8] = far[np.random.randint(len(far))]
    return np.exp2(a.ravel()).repeat(32)


def f64(x):
    return np.asarray(x).astype(np.float64)


def striped(idx):
    return np.tile(np.asarray(idx).reshape(-1, 16).T, (8, 1)).astype(np.uint16)


def unstriped(offs):
    return offs[:16].T.reshape(-1).astype(np.int64)


def setup_inputs():
    n = np.random.standard_normal
    uni = np.random.uniform
    idx = np.random.permutation(2048)[:512]
    soft = np.exp(0.4 * n((512, 512)))
    f_d = mx_kscale(512)
    f_r = mx_kscale(512)
    return {
        "cT": (n((512, 2048)) / np.sqrt(512) * f_d[:, None]).astype(np.float32),
        "dvT": (n((512, 512)) / f_d[:, None] * f_r[None, :]).astype(np.float32),
        "pm": (soft / soft.sum(-1, keepdims=True)).astype(np.float32),
        "pw": (soft / soft.sum(-1, keepdims=True) / f_r[:, None]).astype(np.float32),
        "offs": striped(idx),
    }


def reference(cT, dvT, pm, pw, offs):
    idx = unstriped(offs)
    cT_i = f64(cT)[:, idx]
    dp = mxq(f64(dvT), 0, "e5m2").T @ mxq(cT_i, 0, "e4m3")
    s = (f64(pm) * dp).sum(-1, keepdims=True)
    out_0 = f64(pm) * (dp - s)
    dc = mxq(f64(dvT), 1, "e5m2") @ mxq(f64(pw), 0, "e4m3")
    out_1 = np.zeros((512, 2048))
    out_1[:, idx] = dc
    return out_0, out_1

@@ -1,0 +1,162 @@
+from contextlib import ExitStack
+
+import concourse.mybir as mybir
+from concourse.masks import make_identity
+
+D, R, SLOTS, T = 512, 512, 512, 2048
+FLOPS = 2 * 2 * D * R * SLOTS
+
+F32 = mybir.dt.float32
+BF16 = mybir.dt.bfloat16
+I32 = mybir.dt.int32
+U32 = mybir.dt.uint32
+U16 = mybir.dt.uint16
+U8 = mybir.dt.uint8
+E4M3 = mybir.dt.float8_e4m3fn_x4
+E5M2 = mybir.dt.float8_e5m2_x4
+COPY = mybir.ActivationFunctionType.Copy
+MULT = mybir.AluOpType.mult
+SUBTRACT = mybir.AluOpType.subtract
+
+P = 128
+PACK = 4
+HALF = SLOTS // 2
+HALF_T = T // 2
+VECTOR_SHARE = 160
+
+
+def weave_views(dst, src):
+    return dst.rearrange("p (c i) t -> p c t i", i=4), src.rearrange("p t (c i) -> p c t i", i=4)
+
+
+def tile_attend_gsoftc_kernel(tc, cT, dvT, pm, pw, offs, out_0, out_1):
+    nc = tc.nc
+    with ExitStack() as ctx:
+        sb = ctx.enter_context(tc.tile_pool(name="sb", bufs=1))
+        ring = ctx.enter_context(tc.tile_pool(name="ring", bufs=4))
+        psum1 = ctx.enter_context(tc.psum_pool(name="psum1", bufs=1))
+        psum2 = ctx.enter_context(tc.psum_pool(name="psum2", bufs=2))
+
+        offsets = sb.tile([P, SLOTS // 16], U16, name="offsets")
+        dv = sb.tile([P, PACK * R], F32, name="dv")
+        pw_raw = [sb.tile([P, PACK, HALF], F32, name="pw_raw%d" % h) for h in range(2)]
+        c_raw = [[sb.tile([P, 2, HALF_T], F32, name="c_raw%d%d" % (u, h)) for h in range(2)] for u in range(2)]
+        pm_sb = sb.tile([P, PACK, SLOTS], F32, name="pm_sb")
+
+        dv_rows = dvT.rearrange("(p j) r -> p (j r)", j=PACK)
+        pw_rows = pw.rearrange("(p t) i -> p t i", t=PACK)
+        c_rows = cT.rearrange("(p j) t -> p j t", j=PACK)
+        for u in range(2):
+            nc.sync.dma_start(dv[:, 2 * u * R : 2 * (u + 1) * R], dv_rows[:, 2 * u * R : 2 * (u + 1) * R])
+        for h in range(2):
+            nc.sync.dma_start(pw_raw[h][:], pw_rows[:, :, h * HALF : (h + 1) * HALF])
+        nc.sync.dma_start(offsets[:], offs)
+        for u in range(2):
+            for h in range(2):
+                nc.sync.dma_start(c_raw[u][h][:], c_rows[:, 2 * u : 2 * u + 2, h * HALF_T : (h + 1) * HALF_T])
+        nc.sync.dma_start(pm_sb[:], pm.rearrange("(m p) i -> p m i", p=P))
+
+        ident = sb.tile([P, P], F32, name="ident")
+        make_identity(nc, ident[:])
+        windows = [sb.tile([P, T], F32, name="window%d" % w) for w in range(3)]
+        for window in windows:
+            nc.vector.memset(window[:].bitcast(I32), 0)
+
+        def turn_dv(j):
+            bank = psum2.tile([P, PACK, P], F32, name="turned")
+            for t in range(PACK):
+                nc.tensor.transpose(bank[:, t, :], dv[:, j * R + t : (j + 1) * R : PACK], ident[:])
+            woven = ring.tile([P, P, PACK], BF16, name="dvr_woven", align_bytes=64)
+            nc.scalar.activation(woven[:], bank[:].rearrange("q t p -> q p t"), COPY)
+            return woven
+
+        def quantize_dvr(j, woven):
+            codes = sb.tile([P, P], U32, name="dvr_codes%d" % j, tag="pairs0" if j == 2 else "dvr_codes%d" % j, align_bytes=64)
+            scales = sb.tile([P, P], U8, name="dvr_scales%d" % j, align_bytes=64)
+            nc.vector.quantize_mx(out=codes[:].bitcast(E5M2), scales=scales[:], in_=woven[:].rearrange("q p t -> q (p t)"))
+            return codes, scales
+
+        pw_codes = sb.tile([P, SLOTS], U32, name="pw_codes", align_bytes=64)
+        pw_scales = sb.tile([P, SLOTS], U8, name="pw_scales", align_bytes=64)
+
+        def product_dc(codes, scales, dc):
+            bank = psum2.tile([P, SLOTS], F32, name="dc_bank")
+            nc.tensor.matmul_mx(out=bank[:], lhsT=codes[:].bitcast(E5M2), lhsT_scale=scales[:],
+                                rhs=pw_codes[:].bitcast(E4M3), rhs_scale=pw_scales[:], start=True, stop=True)
+            nc.scalar.copy(dc, bank[:])
+
+        out1_rows = out_1.rearrange("(p j) t -> p j t", j=PACK)
+
+        def scatter_dc(j, dc):
+            window = windows[j % 3]
+            nc.vector.tensor_copy(window[:].indirect(offsets[:]), dc)
+            nc.sync.dma_start(out1_rows[:, j, :], window[:])
+
+        dvr_woven = [turn_dv(j) for j in range(2)]
+        dvd_woven = sb.tile([P, R, PACK], BF16, name="dvd_woven", align_bytes=64)
+        dst, src = weave_views(dvd_woven[:], dv[:].rearrange("p (j r) -> p j r", j=PACK))
+        nc.vector.tensor_copy(dst, src)
+
+        pw_woven = [sb.tile([P, HALF, PACK], BF16, name="pw_woven%d" % h, align_bytes=64) for h in range(2)]
+        dst, src = weave_views(pw_woven[0][:], pw_raw[0][:])
+        nc.vector.tensor_copy(dst, src)
+        dvr = [quantize_dvr(0, dvr_woven[0])]
+        for h in range(2):
+            if h == 1:
+                dst, src = weave_views(pw_woven[1][:, :VECTOR_SHARE, :], pw_raw[1][:, :, :VECTOR_SHARE])
+                nc.vector.tensor_copy(dst, src)
+                dst, src = weave_views(pw_woven[1][:, VECTOR_SHARE:, :], pw_raw[1][:, :, VECTOR_SHARE:])
+                nc.scalar.activation(dst, src, COPY)
+            cols = slice(h * HALF, (h + 1) * HALF)
+            nc.vector.quantize_mx(out=pw_codes[:, cols].bitcast(E4M3), scales=pw_scales[:, cols],
+                                  in_=pw_woven[h][:].rearrange("p c t -> p (c t)"))
+        dvr_woven.extend(turn_dv(j) for j in range(2, PACK))
+        dvr.extend(quantize_dvr(j, dvr_woven[j]) for j in range(1, PACK))
+
+        dvd_codes = sb.tile([P, R], U32, name="dvd_codes", align_bytes=64)
+        dvd_scales = sb.tile([P, R], U8, name="dvd_scales", align_bytes=64)
+        nc.vector.quantize_mx(out=dvd_codes[:].bitcast(E5M2), scales=dvd_scales[:], in_=dvd_woven[:].rearrange("p r j -> p (r j)"))
+
+        for j in range(3):
+            dc = sb.tile([P, SLOTS], F32, name="dc%d" % j)
+            product_dc(*dvr[j], dc[:])
+            scatter_dc(j, dc[:])
+
+        picked = sb.tile([P, 2, SLOTS], U32, name="picked", tag="picked")
+        for u in range(2):
+            pairs = sb.tile([P, T], U32, name="pairs%d" % u, tag="pairs%d" % u, align_bytes=64)
+            halves = pairs[:].bitcast(BF16).rearrange("p (t e) -> p t e", e=2)
+            for h in range(2):
+                nc.scalar.activation(halves[:, h * HALF_T : (h + 1) * HALF_T, :], c_raw[u][h][:].rearrange("p e t -> p t e"), COPY)
+            nc.vector.tensor_copy(picked[:, u, :], pairs[:].indirect(offsets[:]))
+        c_woven = sb.tile([P, SLOTS * PACK], BF16, name="c_woven", align_bytes=64)
+        nc.vector.tensor_copy(c_woven[:].bitcast(I32).rearrange("p (i u) -> p i u", u=2),
+                              picked[:].bitcast(I32).rearrange("p u i -> p i u"))
+        dc_last = sb.tile([P, SLOTS], F32, name="dc_last", tag="picked")
+        product_dc(*dvr[3], dc_last[:])
+        c_codes = sb.tile([P, SLOTS], U32, name="c_codes", align_bytes=64)
+        c_scales = sb.tile([P, SLOTS], U8, name="c_scales", align_bytes=64)
+        nc.vector.quantize_mx(out=c_codes[:].bitcast(E4M3), scales=c_scales[:], in_=c_woven[:])
+        scatter_dc(3, dc_last[:])
+
+        dp = [psum1.tile([P, SLOTS], F32, name="dp%d" % m) for m in range(PACK)]
+        weighted = [sb.tile([P, SLOTS], F32, name="weighted%d" % m) for m in range(PACK)]
+        minus_s = [sb.tile([P, 1], F32, name="minus_s%d" % m) for m in range(PACK)]
+        result = [sb.tile([P, SLOTS], F32, name="result%d" % m) for m in range(PACK)]
+        for m in range(PACK):
+            rows = slice(m * P, (m + 1) * P)
+            nc.tensor.matmul_mx(out=dp[m][:], lhsT=dvd_codes[:, rows].bitcast(E5M2), lhsT_scale=dvd_scales[:, rows],
+                                rhs=c_codes[:].bitcast(E4M3), rhs_scale=c_scales[:], start=True, stop=True)
+
+        def row_sums(m):
+            nc.vector.scalar_tensor_tensor(weighted[m][:], dp[m][:], -1.0, pm_sb[:, m, :], MULT, MULT, accum_out=minus_s[m][:])
+
+        def finish(m):
+            nc.vector.scalar_tensor_tensor(result[m][:], pm_sb[:, m, :], minus_s[m][:], weighted[m][:], MULT, SUBTRACT)
+            nc.sync.dma_start(out_0[m * P : (m + 1) * P, :], result[m][:])
+
+        row_sums(0)
+        for m in range(1, PACK):
+            row_sums(m)
+            finish(m - 1)
+        finish(PACK - 1)

@@ -16,13 +16,15 @@ E4M3 = mybir.dt.float8_e4m3fn_x4
 E5M2 = mybir.dt.float8_e5m2_x4
 COPY = mybir.ActivationFunctionType.Copy
 MULT = mybir.AluOpType.mult
-SUBTRACT = mybir.AluOpType.subtract
+ADD = mybir.AluOpType.add
+IDENTITY = mybir.ActivationFunctionType.Identity
 
 P = 128
 PACK = 4
 HALF = SLOTS // 2
 HALF_T = T // 2
 VECTOR_SHARE = 160
+GPSIMD_COLUMNS = (512, 320, 0, 0)
 
 
 def weave_views(dst, src):
@@ -40,7 +42,7 @@ def tile_attend_gsoftc_kernel(tc, cT, dvT, pm, pw, offs, out_0, out_1):
         offsets = sb.tile([P, SLOTS // 16], U16, name="offsets")
         dv = sb.tile([P, PACK * R], F32, name="dv")
         pw_raw = [sb.tile([P, PACK, HALF], F32, name="pw_raw%d" % h) for h in range(2)]
-        c_raw = [[sb.tile([P, 2, HALF_T], F32, name="c_raw%d%d" % (u, h)) for h in range(2)] for u in range(2)]
+        c_raw = [[sb.tile([P, 2, HALF_T], F32, name="c_raw%d%d" % (u, h), tag="c_raw%d%d" % (u, h), align_bytes=64) for h in range(2)] for u in range(2)]
         pm_sb = sb.tile([P, PACK, SLOTS], F32, name="pm_sb")
 
         dv_rows = dvT.rearrange("(p j) r -> p (j r)", j=PACK)
@@ -62,26 +64,29 @@ def tile_attend_gsoftc_kernel(tc, cT, dvT, pm, pw, offs, out_0, out_1):
         for window in windows:
             nc.vector.memset(window[:].bitcast(I32), 0)
 
-        def turn_dv(j):
-            bank = psum2.tile([P, PACK, P], F32, name="turned")
-            for t in range(PACK):
-                nc.tensor.transpose(bank[:, t, :], dv[:, j * R + t : (j + 1) * R : PACK], ident[:])
-            woven = ring.tile([P, P, PACK], BF16, name="dvr_woven", align_bytes=64)
-            nc.scalar.activation(woven[:], bank[:].rearrange("q t p -> q p t"), COPY)
-            return woven
+        def turn_dv(j, woven):
+            rounded = ring.tile([P, R], BF16, name="dv_rounded")
+            nc.scalar.activation(rounded[:].rearrange("p (u q e) -> p u q e", u=2, e=2),
+                                 dv[:, j * R : (j + 1) * R].rearrange("p (q u e) -> p u q e", u=2, e=2), COPY)
+            words = rounded[:].bitcast(F32)
+            bank = psum2.tile([P, 2, P], F32, name="turned")
+            for u in range(2):
+                nc.tensor.transpose(bank[:, u, :], words[:, u * P : (u + 1) * P], ident[:])
+            nc.scalar.copy(woven.bitcast(F32).rearrange("q (p u) -> q p u", u=2), bank[:].rearrange("q u p -> q p u"))
 
-        def quantize_dvr(j, woven):
-            codes = sb.tile([P, P], U32, name="dvr_codes%d" % j, tag="pairs0" if j == 2 else "dvr_codes%d" % j, align_bytes=64)
-            scales = sb.tile([P, P], U8, name="dvr_scales%d" % j, align_bytes=64)
-            nc.vector.quantize_mx(out=codes[:].bitcast(E5M2), scales=scales[:], in_=woven[:].rearrange("q p t -> q (p t)"))
-            return codes, scales
+        def quantize_dvr(name, woven, codes_tag, scales_tag):
+            width = woven.shape[1] // PACK
+            codes = sb.tile([P, width], U32, name=name + "_codes", tag=codes_tag, align_bytes=64)
+            scales = sb.tile([P, width], U8, name=name + "_scales", tag=scales_tag, align_bytes=64)
+            nc.vector.quantize_mx(out=codes[:].bitcast(E5M2), scales=scales[:], in_=woven)
+            return [(codes[:, c : c + P], scales[:, c : c + P]) for c in range(0, width, P)]
 
         pw_codes = sb.tile([P, SLOTS], U32, name="pw_codes", align_bytes=64)
         pw_scales = sb.tile([P, SLOTS], U8, name="pw_scales", align_bytes=64)
 
         def product_dc(codes, scales, dc):
             bank = psum2.tile([P, SLOTS], F32, name="dc_bank")
-            nc.tensor.matmul_mx(out=bank[:], lhsT=codes[:].bitcast(E5M2), lhsT_scale=scales[:],
+            nc.tensor.matmul_mx(out=bank[:], lhsT=codes.bitcast(E5M2), lhsT_scale=scales,
                                 rhs=pw_codes[:].bitcast(E4M3), rhs_scale=pw_scales[:], start=True, stop=True)
             nc.scalar.copy(dc, bank[:])
 
@@ -92,15 +97,19 @@ def tile_attend_gsoftc_kernel(tc, cT, dvT, pm, pw, offs, out_0, out_1):
             nc.vector.tensor_copy(window[:].indirect(offsets[:]), dc)
             nc.sync.dma_start(out1_rows[:, j, :], window[:])
 
-        dvr_woven = [turn_dv(j) for j in range(2)]
+        woven_first = sb.tile([P, R], BF16, name="woven_first", align_bytes=64)
+        woven_middle = sb.tile([P, 2 * R], BF16, name="woven_middle", tag="woven_middle", align_bytes=64)
+        woven_last = sb.tile([P, R], BF16, name="woven_last", align_bytes=64)
+        turn_dv(0, woven_first[:])
+        turn_dv(1, woven_middle[:, :R])
         dvd_woven = sb.tile([P, R, PACK], BF16, name="dvd_woven", align_bytes=64)
         dst, src = weave_views(dvd_woven[:], dv[:].rearrange("p (j r) -> p j r", j=PACK))
         nc.vector.tensor_copy(dst, src)
 
-        pw_woven = [sb.tile([P, HALF, PACK], BF16, name="pw_woven%d" % h, align_bytes=64) for h in range(2)]
+        pw_woven = [sb.tile([P, HALF, PACK], BF16, name="pw_woven%d" % h, tag="pw_woven%d" % h, align_bytes=64) for h in range(2)]
         dst, src = weave_views(pw_woven[0][:], pw_raw[0][:])
         nc.vector.tensor_copy(dst, src)
-        dvr = [quantize_dvr(0, dvr_woven[0])]
+        dvr = quantize_dvr("first", woven_first[:], "first_codes", "first_scales")
         for h in range(2):
             if h == 1:
                 dst, src = weave_views(pw_woven[1][:, :VECTOR_SHARE, :], pw_raw[1][:, :, :VECTOR_SHARE])
@@ -110,12 +119,14 @@ def tile_attend_gsoftc_kernel(tc, cT, dvT, pm, pw, offs, out_0, out_1):
             cols = slice(h * HALF, (h + 1) * HALF)
             nc.vector.quantize_mx(out=pw_codes[:, cols].bitcast(E4M3), scales=pw_scales[:, cols],
                                   in_=pw_woven[h][:].rearrange("p c t -> p (c t)"))
-        dvr_woven.extend(turn_dv(j) for j in range(2, PACK))
-        dvr.extend(quantize_dvr(j, dvr_woven[j]) for j in range(1, PACK))
+        turn_dv(2, woven_middle[:, R:])
+        turn_dv(3, woven_last[:])
+        dvr.extend(quantize_dvr("middle", woven_middle[:], "pw_woven1", "pairs0"))
 
-        dvd_codes = sb.tile([P, R], U32, name="dvd_codes", align_bytes=64)
+        dvd_codes = sb.tile([P, R], U32, name="dvd_codes", tag="woven_middle", align_bytes=64)
         dvd_scales = sb.tile([P, R], U8, name="dvd_scales", align_bytes=64)
         nc.vector.quantize_mx(out=dvd_codes[:].bitcast(E5M2), scales=dvd_scales[:], in_=dvd_woven[:].rearrange("p r j -> p (r j)"))
+        dvr.extend(quantize_dvr("last", woven_last[:], "last_codes", "last_scales"))
 
         for j in range(3):
             dc = sb.tile([P, SLOTS], F32, name="dc%d" % j)
@@ -124,20 +135,27 @@ def tile_attend_gsoftc_kernel(tc, cT, dvT, pm, pw, offs, out_0, out_1):
 
         picked = sb.tile([P, 2, SLOTS], U32, name="picked", tag="picked")
         for u in range(2):
-            pairs = sb.tile([P, T], U32, name="pairs%d" % u, tag="pairs%d" % u, align_bytes=64)
+            pairs = sb.tile([P, T], U32, name="pairs%d" % u, tag=("pairs0", "c_raw00")[u], align_bytes=64)
             halves = pairs[:].bitcast(BF16).rearrange("p (t e) -> p t e", e=2)
             for h in range(2):
                 nc.scalar.activation(halves[:, h * HALF_T : (h + 1) * HALF_T, :], c_raw[u][h][:].rearrange("p e t -> p t e"), COPY)
             nc.vector.tensor_copy(picked[:, u, :], pairs[:].indirect(offsets[:]))
+        bank = psum2.tile([P, SLOTS], F32, name="dc_bank")
+        nc.tensor.matmul_mx(out=bank[:], lhsT=dvr[3][0].bitcast(E5M2), lhsT_scale=dvr[3][1],
+                            rhs=pw_codes[:].bitcast(E4M3), rhs_scale=pw_scales[:], start=True, stop=True)
+        half_cols = SLOTS // 32
+        dc_a = sb.tile([P, HALF], F32, name="dc_a", tag="c_raw11", align_bytes=64)
+        nc.scalar.copy(dc_a[:], bank[:, :HALF])
+        nc.vector.tensor_copy(windows[0][:].indirect(offsets[:, :half_cols]), dc_a[:])
         c_woven = sb.tile([P, SLOTS * PACK], BF16, name="c_woven", align_bytes=64)
-        nc.vector.tensor_copy(c_woven[:].bitcast(I32).rearrange("p (i u) -> p i u", u=2),
-                              picked[:].bitcast(I32).rearrange("p u i -> p i u"))
-        dc_last = sb.tile([P, SLOTS], F32, name="dc_last", tag="picked")
-        product_dc(*dvr[3], dc_last[:])
-        c_codes = sb.tile([P, SLOTS], U32, name="c_codes", align_bytes=64)
+        nc.scalar.copy(c_woven[:].bitcast(U32).rearrange("p (i u) -> p i u", u=2), picked[:].rearrange("p u i -> p i u"))
+        c_codes = sb.tile([P, SLOTS], U32, name="c_codes", tag="c_raw11", align_bytes=64)
         c_scales = sb.tile([P, SLOTS], U8, name="c_scales", align_bytes=64)
         nc.vector.quantize_mx(out=c_codes[:].bitcast(E4M3), scales=c_scales[:], in_=c_woven[:])
-        scatter_dc(3, dc_last[:])
+        dc_b = sb.tile([P, HALF], F32, name="dc_b", tag="picked")
+        nc.scalar.copy(dc_b[:], bank[:, HALF:])
+        nc.vector.tensor_copy(windows[0][:].indirect(offsets[:, half_cols:]), dc_b[:])
+        nc.sync.dma_start(out1_rows[:, 3, :], windows[0][:])
 
         dp = [psum1.tile([P, SLOTS], F32, name="dp%d" % m) for m in range(PACK)]
         weighted = [sb.tile([P, SLOTS], F32, name="weighted%d" % m) for m in range(PACK)]
@@ -152,11 +170,17 @@ def tile_attend_gsoftc_kernel(tc, cT, dvT, pm, pw, offs, out_0, out_1):
             nc.vector.scalar_tensor_tensor(weighted[m][:], dp[m][:], -1.0, pm_sb[:, m, :], MULT, MULT, accum_out=minus_s[m][:])
 
         def finish(m):
-            nc.vector.scalar_tensor_tensor(result[m][:], pm_sb[:, m, :], minus_s[m][:], weighted[m][:], MULT, SUBTRACT)
-            nc.sync.dma_start(out_0[m * P : (m + 1) * P, :], result[m][:])
+            split = GPSIMD_COLUMNS[m]
+            if split:
+                centred = sb.tile([P, split], F32, name="centred%d" % m)
+                nc.scalar.activation(centred[:], dp[m][:, :split], IDENTITY, bias=minus_s[m][:])
+                nc.gpsimd.tensor_tensor(result[m][:, :split], centred[:], pm_sb[:, m, :split], MULT)
+            if split < SLOTS:
+                nc.vector.scalar_tensor_tensor(result[m][:, split:], dp[m][:, split:], minus_s[m][:], pm_sb[:, m, split:], ADD, MULT)
+            queue = nc.sync if split else nc.scalar
+            queue.dma_start(out_0[m * P : (m + 1) * P, :], result[m][:])
 
-        row_sums(0)
-        for m in range(1, PACK):
+        for m in range(PACK):
             row_sums(m)
-            finish(m - 1)
-        finish(PACK - 1)
+        for m in (0, 2, 3, 1):
+            finish(m)

@@ -23,7 +23,6 @@ P = 128
 PACK = 4
 HALF = SLOTS // 2
 HALF_T = T // 2
-VECTOR_SHARE = 160
 GPSIMD_COLUMNS = (512, 320, 0, 0)
 
 
@@ -35,13 +34,11 @@ def tile_attend_gsoftc_kernel(tc, cT, dvT, pm, pw, offs, out_0, out_1):
     nc = tc.nc
     with ExitStack() as ctx:
         sb = ctx.enter_context(tc.tile_pool(name="sb", bufs=1))
-        ring = ctx.enter_context(tc.tile_pool(name="ring", bufs=4))
-        psum1 = ctx.enter_context(tc.psum_pool(name="psum1", bufs=1))
-        psum2 = ctx.enter_context(tc.psum_pool(name="psum2", bufs=2))
+        psum = ctx.enter_context(tc.psum_pool(name="psum", bufs=1))
 
         offsets = sb.tile([P, SLOTS // 16], U16, name="offsets")
         dv = sb.tile([P, PACK * R], F32, name="dv")
-        pw_raw = [sb.tile([P, PACK, HALF], F32, name="pw_raw%d" % h) for h in range(2)]
+        pw_raw = [sb.tile([P, PACK, HALF], F32, name="pw_raw%d" % h, tag="pw_raw%d" % h, align_bytes=64) for h in range(2)]
         c_raw = [[sb.tile([P, 2, HALF_T], F32, name="c_raw%d%d" % (u, h), tag="c_raw%d%d" % (u, h), align_bytes=64) for h in range(2)] for u in range(2)]
         pm_sb = sb.tile([P, PACK, SLOTS], F32, name="pm_sb")
 
@@ -61,18 +58,22 @@ def tile_attend_gsoftc_kernel(tc, cT, dvT, pm, pw, offs, out_0, out_1):
         ident = sb.tile([P, P], F32, name="ident")
         make_identity(nc, ident[:])
         windows = [sb.tile([P, T], F32, name="window%d" % w) for w in range(3)]
-        for window in windows:
+        for window in windows[:2]:
             nc.vector.memset(window[:].bitcast(I32), 0)
 
-        def turn_dv(j, woven):
-            rounded = ring.tile([P, R], BF16, name="dv_rounded")
-            nc.scalar.activation(rounded[:].rearrange("p (u q e) -> p u q e", u=2, e=2),
-                                 dv[:, j * R : (j + 1) * R].rearrange("p (q u e) -> p u q e", u=2, e=2), COPY)
+        def turn_dv(u):
+            rounded = sb.tile([P, 2 * R], BF16, name="dv_rounded%d" % u)
+            nc.scalar.copy(rounded[:].rearrange("p (j w q e) -> p j w q e", j=2, w=2, e=2),
+                           dv[:, 2 * u * R : 2 * (u + 1) * R].rearrange("p (j q w e) -> p j w q e", j=2, w=2, e=2))
             words = rounded[:].bitcast(F32)
-            bank = psum2.tile([P, 2, P], F32, name="turned")
-            for u in range(2):
-                nc.tensor.transpose(bank[:, u, :], words[:, u * P : (u + 1) * P], ident[:])
-            nc.scalar.copy(woven.bitcast(F32).rearrange("q (p u) -> q p u", u=2), bank[:].rearrange("q u p -> q p u"))
+            bank = psum.tile([P, 2, 2, P], F32, name="turned%d" % u, tag="bank%d" % u)
+            for j in range(2):
+                for w in range(2):
+                    first = (2 * j + w) * P
+                    nc.tensor.transpose(bank[:, j, w, :], words[:, first : first + P], ident[:])
+            woven = sb.tile([P, 2 * R], BF16, name="dvr_woven%d" % u, tag="dvr_woven%d" % u, align_bytes=64)
+            nc.scalar.copy(woven[:].bitcast(F32).rearrange("q (j p w) -> q j p w", j=2, w=2), bank[:].rearrange("q j w p -> q j p w"))
+            return woven
 
         def quantize_dvr(name, woven, codes_tag, scales_tag):
             width = woven.shape[1] // PACK
@@ -81,83 +82,76 @@ def tile_attend_gsoftc_kernel(tc, cT, dvT, pm, pw, offs, out_0, out_1):
             nc.vector.quantize_mx(out=codes[:].bitcast(E5M2), scales=scales[:], in_=woven)
             return [(codes[:, c : c + P], scales[:, c : c + P]) for c in range(0, width, P)]
 
-        pw_codes = sb.tile([P, SLOTS], U32, name="pw_codes", align_bytes=64)
-        pw_scales = sb.tile([P, SLOTS], U8, name="pw_scales", align_bytes=64)
+        pw_codes = sb.tile([P, HALF + SLOTS], U32, name="pw_codes", align_bytes=64)
+        pw_scales = sb.tile([P, HALF + SLOTS], U8, name="pw_scales", align_bytes=64)
+        nc.gpsimd.memset(pw_codes[:, :HALF], 0)
+        nc.gpsimd.memset(pw_scales[:, :HALF], 0)
+        nc.gpsimd.memset(windows[2][:].bitcast(I32), 0)
 
-        def product_dc(codes, scales, dc):
-            bank = psum2.tile([P, SLOTS], F32, name="dc_bank")
+        def product_dc(operand, first, bank_nr):
+            codes, scales = operand
+            bank = psum.tile([P, SLOTS], F32, name="dc_bank", tag="bank%d" % bank_nr)
             nc.tensor.matmul_mx(out=bank[:], lhsT=codes.bitcast(E5M2), lhsT_scale=scales,
-                                rhs=pw_codes[:].bitcast(E4M3), rhs_scale=pw_scales[:], start=True, stop=True)
-            nc.scalar.copy(dc, bank[:])
+                                rhs=pw_codes[:, first : first + SLOTS].bitcast(E4M3), rhs_scale=pw_scales[:, first : first + SLOTS],
+                                start=True, stop=True)
+            return bank
 
         out1_rows = out_1.rearrange("(p j) t -> p j t", j=PACK)
 
-        def scatter_dc(j, dc):
-            window = windows[j % 3]
-            nc.vector.tensor_copy(window[:].indirect(offsets[:]), dc)
-            nc.sync.dma_start(out1_rows[:, j, :], window[:])
-
-        woven_first = sb.tile([P, R], BF16, name="woven_first", align_bytes=64)
-        woven_middle = sb.tile([P, 2 * R], BF16, name="woven_middle", tag="woven_middle", align_bytes=64)
-        woven_last = sb.tile([P, R], BF16, name="woven_last", align_bytes=64)
-        turn_dv(0, woven_first[:])
-        turn_dv(1, woven_middle[:, :R])
-        dvd_woven = sb.tile([P, R, PACK], BF16, name="dvd_woven", align_bytes=64)
-        dst, src = weave_views(dvd_woven[:], dv[:].rearrange("p (j r) -> p j r", j=PACK))
-        nc.vector.tensor_copy(dst, src)
+        def scatter(window, source, first, count, name, tag):
+            dc = sb.tile([P, count], F32, name=name, tag=tag, align_bytes=64)
+            nc.scalar.copy(dc[:], source)
+            nc.vector.tensor_copy(window[:].indirect(offsets[:, first // 16 : (first + count) // 16]), dc[:])
 
         pw_woven = [sb.tile([P, HALF, PACK], BF16, name="pw_woven%d" % h, tag="pw_woven%d" % h, align_bytes=64) for h in range(2)]
-        dst, src = weave_views(pw_woven[0][:], pw_raw[0][:])
-        nc.vector.tensor_copy(dst, src)
-        dvr = quantize_dvr("first", woven_first[:], "first_codes", "first_scales")
-        for h in range(2):
-            if h == 1:
-                dst, src = weave_views(pw_woven[1][:, :VECTOR_SHARE, :], pw_raw[1][:, :, :VECTOR_SHARE])
-                nc.vector.tensor_copy(dst, src)
-                dst, src = weave_views(pw_woven[1][:, VECTOR_SHARE:, :], pw_raw[1][:, :, VECTOR_SHARE:])
-                nc.scalar.activation(dst, src, COPY)
-            cols = slice(h * HALF, (h + 1) * HALF)
+
+        def weave_pw(h):
+            nc.vector.tensor_copy(*weave_views(pw_woven[h][:], pw_raw[h][:]))
+
+        def quantize_pw(h):
+            cols = slice((h + 1) * HALF, (h + 2) * HALF)
             nc.vector.quantize_mx(out=pw_codes[:, cols].bitcast(E4M3), scales=pw_scales[:, cols],
                                   in_=pw_woven[h][:].rearrange("p c t -> p (c t)"))
-        turn_dv(2, woven_middle[:, R:])
-        turn_dv(3, woven_last[:])
-        dvr.extend(quantize_dvr("middle", woven_middle[:], "pw_woven1", "pairs0"))
 
-        dvd_codes = sb.tile([P, R], U32, name="dvd_codes", tag="woven_middle", align_bytes=64)
+        dvr_woven = [turn_dv(u) for u in range(2)]
+        dvd_woven = sb.tile([P, R, PACK], BF16, name="dvd_woven", align_bytes=64)
+        nc.vector.tensor_copy(*weave_views(dvd_woven[:], dv[:].rearrange("p (j r) -> p j r", j=PACK)))
+        weave_pw(0)
+        dvr = quantize_dvr("first", dvr_woven[0][:], "first_codes", "first_scales")
+        quantize_pw(0)
+        early = product_dc(dvr[0], 0, 2)
+        weave_pw(1)
+        quantize_pw(1)
+        dvr.extend(quantize_dvr("second", dvr_woven[1][:], "pw_woven1", "pairs0"))
+        dvd_codes = sb.tile([P, R], U32, name="dvd_codes", tag="dvr_woven1", align_bytes=64)
         dvd_scales = sb.tile([P, R], U8, name="dvd_scales", align_bytes=64)
         nc.vector.quantize_mx(out=dvd_codes[:].bitcast(E5M2), scales=dvd_scales[:], in_=dvd_woven[:].rearrange("p r j -> p (r j)"))
-        dvr.extend(quantize_dvr("last", woven_last[:], "last_codes", "last_scales"))
 
-        for j in range(3):
-            dc = sb.tile([P, SLOTS], F32, name="dc%d" % j)
-            product_dc(*dvr[j], dc[:])
-            scatter_dc(j, dc[:])
+        scatter(windows[0], early[:, HALF:], 0, HALF, "dc0a", "pw_raw1")
+        scatter(windows[0], product_dc(dvr[0], HALF, 3)[:, HALF:], HALF, HALF, "dc0b", "dc0b")
+        nc.sync.dma_start(out1_rows[:, 0, :], windows[0][:])
+        for j in (1, 2):
+            scatter(windows[j], product_dc(dvr[j], HALF, (4, 3)[j - 1])[:], 0, SLOTS, "dc%d" % j, "dc%d" % j)
+            nc.sync.dma_start(out1_rows[:, j, :], windows[j][:])
+        last = product_dc(dvr[3], HALF, 5)
 
-        picked = sb.tile([P, 2, SLOTS], U32, name="picked", tag="picked")
+        picked = sb.tile([P, 2, SLOTS], U32, name="picked", tag="picked", align_bytes=64)
         for u in range(2):
             pairs = sb.tile([P, T], U32, name="pairs%d" % u, tag=("pairs0", "c_raw00")[u], align_bytes=64)
             halves = pairs[:].bitcast(BF16).rearrange("p (t e) -> p t e", e=2)
             for h in range(2):
                 nc.scalar.activation(halves[:, h * HALF_T : (h + 1) * HALF_T, :], c_raw[u][h][:].rearrange("p e t -> p t e"), COPY)
             nc.vector.tensor_copy(picked[:, u, :], pairs[:].indirect(offsets[:]))
-        bank = psum2.tile([P, SLOTS], F32, name="dc_bank")
-        nc.tensor.matmul_mx(out=bank[:], lhsT=dvr[3][0].bitcast(E5M2), lhsT_scale=dvr[3][1],
-                            rhs=pw_codes[:].bitcast(E4M3), rhs_scale=pw_scales[:], start=True, stop=True)
-        half_cols = SLOTS // 32
-        dc_a = sb.tile([P, HALF], F32, name="dc_a", tag="c_raw11", align_bytes=64)
-        nc.scalar.copy(dc_a[:], bank[:, :HALF])
-        nc.vector.tensor_copy(windows[0][:].indirect(offsets[:, :half_cols]), dc_a[:])
+        scatter(windows[0], last[:, :HALF], 0, HALF, "dc3a", "c_raw11")
         c_woven = sb.tile([P, SLOTS * PACK], BF16, name="c_woven", align_bytes=64)
         nc.scalar.copy(c_woven[:].bitcast(U32).rearrange("p (i u) -> p i u", u=2), picked[:].rearrange("p u i -> p i u"))
         c_codes = sb.tile([P, SLOTS], U32, name="c_codes", tag="c_raw11", align_bytes=64)
         c_scales = sb.tile([P, SLOTS], U8, name="c_scales", align_bytes=64)
         nc.vector.quantize_mx(out=c_codes[:].bitcast(E4M3), scales=c_scales[:], in_=c_woven[:])
-        dc_b = sb.tile([P, HALF], F32, name="dc_b", tag="picked")
-        nc.scalar.copy(dc_b[:], bank[:, HALF:])
-        nc.vector.tensor_copy(windows[0][:].indirect(offsets[:, half_cols:]), dc_b[:])
+        scatter(windows[0], last[:, HALF:], HALF, HALF, "dc3b", "picked")
         nc.sync.dma_start(out1_rows[:, 3, :], windows[0][:])
 
-        dp = [psum1.tile([P, SLOTS], F32, name="dp%d" % m) for m in range(PACK)]
+        dp = [psum.tile([P, SLOTS], F32, name="dp%d" % m, tag="bank%d" % m) for m in range(PACK)]
         weighted = [sb.tile([P, SLOTS], F32, name="weighted%d" % m) for m in range(PACK)]
         minus_s = [sb.tile([P, 1], F32, name="minus_s%d" % m) for m in range(PACK)]
         result = [sb.tile([P, SLOTS], F32, name="result%d" % m) for m in range(PACK)]

@@ -58,7 +58,7 @@ def tile_attend_gsoftc_kernel(tc, cT, dvT, pm, pw, offs, out_0, out_1):
         ident = sb.tile([P, P], F32, name="ident")
         make_identity(nc, ident[:])
         windows = [sb.tile([P, T], F32, name="window%d" % w) for w in range(3)]
-        for window in windows[:2]:
+        for window in windows:
             nc.vector.memset(window[:].bitcast(I32), 0)
 
         def turn_dv(u):
@@ -84,9 +84,8 @@ def tile_attend_gsoftc_kernel(tc, cT, dvT, pm, pw, offs, out_0, out_1):
 
         pw_codes = sb.tile([P, HALF + SLOTS], U32, name="pw_codes", align_bytes=64)
         pw_scales = sb.tile([P, HALF + SLOTS], U8, name="pw_scales", align_bytes=64)
-        nc.gpsimd.memset(pw_codes[:, :HALF], 0)
-        nc.gpsimd.memset(pw_scales[:, :HALF], 0)
-        nc.gpsimd.memset(windows[2][:].bitcast(I32), 0)
+        nc.vector.memset(pw_codes[:, :HALF], 0)
+        nc.vector.memset(pw_scales[:, :HALF].bitcast(I32), 0)
 
         def product_dc(operand, first, bank_nr):
             codes, scales = operand
@@ -140,11 +139,11 @@ def tile_attend_gsoftc_kernel(tc, cT, dvT, pm, pw, offs, out_0, out_1):
             pairs = sb.tile([P, T], U32, name="pairs%d" % u, tag=("pairs0", "c_raw00")[u], align_bytes=64)
             halves = pairs[:].bitcast(BF16).rearrange("p (t e) -> p t e", e=2)
             for h in range(2):
-                nc.scalar.activation(halves[:, h * HALF_T : (h + 1) * HALF_T, :], c_raw[u][h][:].rearrange("p e t -> p t e"), COPY)
+                nc.scalar.activation(*weave_views(halves[:, h * HALF_T : (h + 1) * HALF_T, :], c_raw[u][h][:]), COPY)
             nc.vector.tensor_copy(picked[:, u, :], pairs[:].indirect(offsets[:]))
         scatter(windows[0], last[:, :HALF], 0, HALF, "dc3a", "c_raw11")
         c_woven = sb.tile([P, SLOTS * PACK], BF16, name="c_woven", align_bytes=64)
-        nc.scalar.copy(c_woven[:].bitcast(U32).rearrange("p (i u) -> p i u", u=2), picked[:].rearrange("p u i -> p i u"))
+        nc.scalar.copy(*weave_views(c_woven[:].bitcast(U32).rearrange("p (i u) -> p i u", u=2), picked[:]))
         c_codes = sb.tile([P, SLOTS], U32, name="c_codes", tag="c_raw11", align_bytes=64)
         c_scales = sb.tile([P, SLOTS], U8, name="c_scales", align_bytes=64)
         nc.vector.quantize_mx(out=c_codes[:].bitcast(E4M3), scales=c_scales[:], in_=c_woven[:])

@@ -36,144 +36,168 @@ def tile_attend_gsoftc_kernel(tc, cT, dvT, pm, pw, offs, out_0, out_1):
         sb = ctx.enter_context(tc.tile_pool(name="sb", bufs=1))
         psum = ctx.enter_context(tc.psum_pool(name="psum", bufs=1))
 
+        def tile(shape, dtype, name, tag=None):
+            return sb.tile(shape, dtype, name=name, tag=tag or name, align_bytes=64)
+
         offsets = sb.tile([P, SLOTS // 16], U16, name="offsets")
-        dv = sb.tile([P, PACK * R], F32, name="dv")
-        pw_raw = [sb.tile([P, PACK, HALF], F32, name="pw_raw%d" % h, tag="pw_raw%d" % h, align_bytes=64) for h in range(2)]
-        c_raw = [[sb.tile([P, 2, HALF_T], F32, name="c_raw%d%d" % (u, h), tag="c_raw%d%d" % (u, h), align_bytes=64) for h in range(2)] for u in range(2)]
-        pm_sb = sb.tile([P, PACK, SLOTS], F32, name="pm_sb")
+        dv_raw = [tile([P, 2 * R], F32, "dv_raw%d" % u) for u in range(2)]
+        pw_raw = [tile([P, PACK, HALF], F32, "pw_raw%d" % h) for h in range(2)]
+        c_raw = [[tile([P, 2, HALF_T], F32, "c_raw%d%d" % (u, h)) for h in range(2)] for u in range(2)]
 
         dv_rows = dvT.rearrange("(p j) r -> p (j r)", j=PACK)
         pw_rows = pw.rearrange("(p t) i -> p t i", t=PACK)
         c_rows = cT.rearrange("(p j) t -> p j t", j=PACK)
         for u in range(2):
-            nc.sync.dma_start(dv[:, 2 * u * R : 2 * (u + 1) * R], dv_rows[:, 2 * u * R : 2 * (u + 1) * R])
+            nc.sync.dma_start(dv_raw[u][:], dv_rows[:, 2 * u * R : 2 * (u + 1) * R])
         for h in range(2):
             nc.sync.dma_start(pw_raw[h][:], pw_rows[:, :, h * HALF : (h + 1) * HALF])
         nc.sync.dma_start(offsets[:], offs)
         for u in range(2):
             for h in range(2):
                 nc.sync.dma_start(c_raw[u][h][:], c_rows[:, 2 * u : 2 * u + 2, h * HALF_T : (h + 1) * HALF_T])
-        nc.sync.dma_start(pm_sb[:], pm.rearrange("(m p) i -> p m i", p=P))
 
-        ident = sb.tile([P, P], F32, name="ident")
+        ident = tile([P, P], F32, "ident")
         make_identity(nc, ident[:])
-        windows = [sb.tile([P, T], F32, name="window%d" % w) for w in range(3)]
+        windows = [tile([P, T], F32, "window%d" % w) for w in range(3)]
         for window in windows:
             nc.vector.memset(window[:].bitcast(I32), 0)
+        pw_codes = tile([P, HALF + SLOTS], U32, "pw_codes")
+        pw_scales = tile([P, HALF + SLOTS], U8, "pw_scales")
+        nc.vector.memset(pw_codes[:, :HALF], 0)
+        nc.vector.memset(pw_scales[:, :HALF].bitcast(I32), 0)
 
-        def turn_dv(u):
-            rounded = sb.tile([P, 2 * R], BF16, name="dv_rounded%d" % u)
-            nc.scalar.copy(rounded[:].rearrange("p (j w q e) -> p j w q e", j=2, w=2, e=2),
-                           dv[:, 2 * u * R : 2 * (u + 1) * R].rearrange("p (j q w e) -> p j w q e", j=2, w=2, e=2))
-            words = rounded[:].bitcast(F32)
+        rounded = tile([P, PACK * R], BF16, "dv_rounded")
+
+        def turn(u):
+            part = rounded[:, 2 * u * R : 2 * (u + 1) * R]
+            nc.vector.tensor_copy(part.rearrange("p (j w q e) -> p j w q e", j=2, w=2, e=2),
+                                  dv_raw[u][:].rearrange("p (j q w e) -> p j w q e", j=2, w=2, e=2))
+            words = part.bitcast(F32)
             bank = psum.tile([P, 2, 2, P], F32, name="turned%d" % u, tag="bank%d" % u)
             for j in range(2):
                 for w in range(2):
                     first = (2 * j + w) * P
                     nc.tensor.transpose(bank[:, j, w, :], words[:, first : first + P], ident[:])
-            woven = sb.tile([P, 2 * R], BF16, name="dvr_woven%d" % u, tag="dvr_woven%d" % u, align_bytes=64)
+            return bank
+
+        def weave_turned(u, bank):
+            woven = tile([P, 2 * R], BF16, "dvr_woven%d" % u)
             nc.scalar.copy(woven[:].bitcast(F32).rearrange("q (j p w) -> q j p w", j=2, w=2), bank[:].rearrange("q j w p -> q j p w"))
             return woven
 
-        def quantize_dvr(name, woven, codes_tag, scales_tag):
+        def quantize_dv(name, woven, codes_tag=None):
             width = woven.shape[1] // PACK
-            codes = sb.tile([P, width], U32, name=name + "_codes", tag=codes_tag, align_bytes=64)
-            scales = sb.tile([P, width], U8, name=name + "_scales", tag=scales_tag, align_bytes=64)
+            codes = tile([P, width], U32, name + "_codes", codes_tag)
+            scales = tile([P, width], U8, name + "_scales")
             nc.vector.quantize_mx(out=codes[:].bitcast(E5M2), scales=scales[:], in_=woven)
             return [(codes[:, c : c + P], scales[:, c : c + P]) for c in range(0, width, P)]
 
-        pw_codes = sb.tile([P, HALF + SLOTS], U32, name="pw_codes", align_bytes=64)
-        pw_scales = sb.tile([P, HALF + SLOTS], U8, name="pw_scales", align_bytes=64)
-        nc.vector.memset(pw_codes[:, :HALF], 0)
-        nc.vector.memset(pw_scales[:, :HALF].bitcast(I32), 0)
+        def weave_dvd(h, woven):
+            nc.scalar.copy(woven.rearrange("p (e q j) -> p q j e", e=2, j=PACK),
+                           rounded[:].rearrange("p (j w q e) -> p w q j e", j=PACK, w=2, e=2)[:, h, :, :, :])
 
-        def product_dc(operand, first, bank_nr):
+        def product_dc(operand, first, bank_tag):
             codes, scales = operand
-            bank = psum.tile([P, SLOTS], F32, name="dc_bank", tag="bank%d" % bank_nr)
+            bank = psum.tile([P, SLOTS], F32, name="dc_bank", tag=bank_tag)
             nc.tensor.matmul_mx(out=bank[:], lhsT=codes.bitcast(E5M2), lhsT_scale=scales,
                                 rhs=pw_codes[:, first : first + SLOTS].bitcast(E4M3), rhs_scale=pw_scales[:, first : first + SLOTS],
                                 start=True, stop=True)
             return bank
 
+        def quantize_pw(h, woven):
+            cols = slice((h + 1) * HALF, (h + 2) * HALF)
+            nc.vector.quantize_mx(out=pw_codes[:, cols].bitcast(E4M3), scales=pw_scales[:, cols], in_=woven)
+
+        def weave_pw(h, woven):
+            nc.vector.tensor_copy(*weave_views(woven.rearrange("p (c t) -> p c t", t=PACK), pw_raw[h][:]))
+
+        def scatter(window, dc, first, count):
+            nc.vector.tensor_copy(window[:].indirect(offsets[:, first // 16 : (first + count) // 16]), dc)
+
+        def copy_out(source, name):
+            dc = tile([P, source.shape[1]], F32, name)
+            nc.scalar.copy(dc[:], source)
+            return dc
+
         out1_rows = out_1.rearrange("(p j) t -> p j t", j=PACK)
 
-        def scatter(window, source, first, count, name, tag):
-            dc = sb.tile([P, count], F32, name=name, tag=tag, align_bytes=64)
-            nc.scalar.copy(dc[:], source)
-            nc.vector.tensor_copy(window[:].indirect(offsets[:, first // 16 : (first + count) // 16]), dc[:])
+        banks = [turn(u) for u in range(2)]
+        woven = [weave_turned(u, banks[u]) for u in range(2)]
+        pw_woven0 = tile([P, PACK * HALF], BF16, "pw_woven0")
+        weave_pw(0, pw_woven0[:])
+        dvr = quantize_dv("dvr0", woven[0][:])
+        quantize_pw(0, pw_woven0[:])
+        early = product_dc(dvr[0], 0, "bank2")
+        pw_woven1 = tile([P, PACK * HALF], BF16, "pw_woven1", "dvr_woven0")
+        weave_pw(1, pw_woven1[:])
+        dvr.extend(quantize_dv("dvr1", woven[1][:]))
+        quantize_pw(1, pw_woven1[:])
+        dvd_woven0 = tile([P, 2 * R], BF16, "dvd_woven0", "dvr_woven0")
+        weave_dvd(0, dvd_woven0[:])
+        dvd = quantize_dv("dvd0", dvd_woven0[:])
 
-        pw_woven = [sb.tile([P, HALF, PACK], BF16, name="pw_woven%d" % h, tag="pw_woven%d" % h, align_bytes=64) for h in range(2)]
-
-        def weave_pw(h):
-            nc.vector.tensor_copy(*weave_views(pw_woven[h][:], pw_raw[h][:]))
-
-        def quantize_pw(h):
-            cols = slice((h + 1) * HALF, (h + 2) * HALF)
-            nc.vector.quantize_mx(out=pw_codes[:, cols].bitcast(E4M3), scales=pw_scales[:, cols],
-                                  in_=pw_woven[h][:].rearrange("p c t -> p (c t)"))
-
-        dvr_woven = [turn_dv(u) for u in range(2)]
-        dvd_woven = sb.tile([P, R, PACK], BF16, name="dvd_woven", align_bytes=64)
-        nc.vector.tensor_copy(*weave_views(dvd_woven[:], dv[:].rearrange("p (j r) -> p j r", j=PACK)))
-        weave_pw(0)
-        dvr = quantize_dvr("first", dvr_woven[0][:], "first_codes", "first_scales")
-        quantize_pw(0)
-        early = product_dc(dvr[0], 0, 2)
-        weave_pw(1)
-        quantize_pw(1)
-        dvr.extend(quantize_dvr("second", dvr_woven[1][:], "pw_woven1", "pairs0"))
-        dvd_codes = sb.tile([P, R], U32, name="dvd_codes", tag="dvr_woven1", align_bytes=64)
-        dvd_scales = sb.tile([P, R], U8, name="dvd_scales", align_bytes=64)
-        nc.vector.quantize_mx(out=dvd_codes[:].bitcast(E5M2), scales=dvd_scales[:], in_=dvd_woven[:].rearrange("p r j -> p (r j)"))
-
-        scatter(windows[0], early[:, HALF:], 0, HALF, "dc0a", "pw_raw1")
-        scatter(windows[0], product_dc(dvr[0], HALF, 3)[:, HALF:], HALF, HALF, "dc0b", "dc0b")
+        dc0a = copy_out(early[:, HALF:], "dc0a")
+        scatter(windows[0], dc0a[:], 0, HALF)
+        dc0b = copy_out(product_dc(dvr[0], HALF, "bank3")[:, HALF:], "dc0b")
+        scatter(windows[0], dc0b[:], HALF, HALF)
         nc.sync.dma_start(out1_rows[:, 0, :], windows[0][:])
+        pm_sb = tile([P, PACK, SLOTS], F32, "pm_sb", "dc0b")
+        nc.sync.dma_start(pm_sb[:], pm.rearrange("(q t) i -> q t i", t=PACK))
         for j in (1, 2):
-            scatter(windows[j], product_dc(dvr[j], HALF, (4, 3)[j - 1])[:], 0, SLOTS, "dc%d" % j, "dc%d" % j)
+            dc = copy_out(product_dc(dvr[j], HALF, "bank%d" % (3 + j))[:], "dc%d" % j)
+            scatter(windows[j], dc[:], 0, SLOTS)
             nc.sync.dma_start(out1_rows[:, j, :], windows[j][:])
-        last = product_dc(dvr[3], HALF, 5)
+        last = product_dc(dvr[3], HALF, "bank6")
+        dc3a = copy_out(last[:, :HALF], "dc3a")
 
-        picked = sb.tile([P, 2, SLOTS], U32, name="picked", tag="picked", align_bytes=64)
-        for u in range(2):
-            pairs = sb.tile([P, T], U32, name="pairs%d" % u, tag=("pairs0", "c_raw00")[u], align_bytes=64)
+        picked = tile([P, 2, SLOTS], U32, "picked")
+
+        def gather(u, tag):
+            pairs = tile([P, T], U32, "c_pairs%d" % u, tag)
             halves = pairs[:].bitcast(BF16).rearrange("p (t e) -> p t e", e=2)
             for h in range(2):
                 nc.scalar.activation(*weave_views(halves[:, h * HALF_T : (h + 1) * HALF_T, :], c_raw[u][h][:]), COPY)
             nc.vector.tensor_copy(picked[:, u, :], pairs[:].indirect(offsets[:]))
-        scatter(windows[0], last[:, :HALF], 0, HALF, "dc3a", "c_raw11")
-        c_woven = sb.tile([P, SLOTS * PACK], BF16, name="c_woven", align_bytes=64)
-        nc.scalar.copy(*weave_views(c_woven[:].bitcast(U32).rearrange("p (i u) -> p i u", u=2), picked[:]))
-        c_codes = sb.tile([P, SLOTS], U32, name="c_codes", tag="c_raw11", align_bytes=64)
-        c_scales = sb.tile([P, SLOTS], U8, name="c_scales", align_bytes=64)
-        nc.vector.quantize_mx(out=c_codes[:].bitcast(E4M3), scales=c_scales[:], in_=c_woven[:])
-        scatter(windows[0], last[:, HALF:], HALF, HALF, "dc3b", "picked")
-        nc.sync.dma_start(out1_rows[:, 3, :], windows[0][:])
 
-        dp = [psum.tile([P, SLOTS], F32, name="dp%d" % m, tag="bank%d" % m) for m in range(PACK)]
-        weighted = [sb.tile([P, SLOTS], F32, name="weighted%d" % m) for m in range(PACK)]
-        minus_s = [sb.tile([P, 1], F32, name="minus_s%d" % m) for m in range(PACK)]
-        result = [sb.tile([P, SLOTS], F32, name="result%d" % m) for m in range(PACK)]
-        for m in range(PACK):
-            rows = slice(m * P, (m + 1) * P)
-            nc.tensor.matmul_mx(out=dp[m][:], lhsT=dvd_codes[:, rows].bitcast(E5M2), lhsT_scale=dvd_scales[:, rows],
+        gather(0, "dvr1_codes")
+        scatter(windows[0], dc3a[:], 0, HALF)
+        gather(1, "c_raw01")
+        late = tile([P, HALF + R], F32, "late", "c_raw11")
+        nc.scalar.copy(late[:, :HALF], last[:, HALF:])
+        scatter(windows[0], late[:, :HALF], HALF, HALF)
+        nc.sync.dma_start(out1_rows[:, 3, :], windows[0][:])
+        weave_dvd(1, late[:, HALF:].bitcast(BF16))
+        c_woven = tile([P, SLOTS * PACK], BF16, "c_woven")
+        nc.scalar.copy(*weave_views(c_woven[:].bitcast(U32).rearrange("p (i u) -> p i u", u=2), picked[:]))
+        c_codes = tile([P, SLOTS], U32, "c_codes")
+        c_scales = tile([P, SLOTS], U8, "c_scales")
+        nc.vector.quantize_mx(out=c_codes[:].bitcast(E4M3), scales=c_scales[:], in_=c_woven[:])
+        dvd.extend(quantize_dv("dvd1", late[:, HALF:].bitcast(BF16), "c_woven"))
+
+        dp = [psum.tile([P, SLOTS], F32, name="dp%d" % t, tag="bank%d" % t) for t in range(PACK)]
+        weighted = [tile([P, SLOTS], F32, "weighted%d" % t) for t in range(PACK)]
+        minus_s = [tile([P, 1], F32, "minus_s%d" % t) for t in range(PACK)]
+        result = [tile([P, SLOTS], F32, "result%d" % t) for t in range(PACK)]
+        out0_rows = out_0.rearrange("(q t) i -> q t i", t=PACK)
+        for t in range(PACK):
+            nc.tensor.matmul_mx(out=dp[t][:], lhsT=dvd[t][0].bitcast(E5M2), lhsT_scale=dvd[t][1],
                                 rhs=c_codes[:].bitcast(E4M3), rhs_scale=c_scales[:], start=True, stop=True)
 
-        def row_sums(m):
-            nc.vector.scalar_tensor_tensor(weighted[m][:], dp[m][:], -1.0, pm_sb[:, m, :], MULT, MULT, accum_out=minus_s[m][:])
+        def row_sums(t):
+            nc.vector.scalar_tensor_tensor(weighted[t][:], dp[t][:], -1.0, pm_sb[:, t, :], MULT, MULT, accum_out=minus_s[t][:])
 
-        def finish(m):
-            split = GPSIMD_COLUMNS[m]
+        def finish(t):
+            split = GPSIMD_COLUMNS[t]
             if split:
-                centred = sb.tile([P, split], F32, name="centred%d" % m)
-                nc.scalar.activation(centred[:], dp[m][:, :split], IDENTITY, bias=minus_s[m][:])
-                nc.gpsimd.tensor_tensor(result[m][:, :split], centred[:], pm_sb[:, m, :split], MULT)
+                centred = tile([P, split], F32, "centred%d" % t)
+                nc.scalar.activation(centred[:], dp[t][:, :split], IDENTITY, bias=minus_s[t][:])
+                nc.gpsimd.tensor_tensor(result[t][:, :split], centred[:], pm_sb[:, t, :split], MULT)
             if split < SLOTS:
-                nc.vector.scalar_tensor_tensor(result[m][:, split:], dp[m][:, split:], minus_s[m][:], pm_sb[:, m, split:], ADD, MULT)
+                nc.vector.scalar_tensor_tensor(result[t][:, split:], dp[t][:, split:], minus_s[t][:], pm_sb[:, t, split:], ADD, MULT)
             queue = nc.sync if split else nc.scalar
-            queue.dma_start(out_0[m * P : (m + 1) * P, :], result[m][:])
+            queue.dma_start(out0_rows[:, t, :], result[t][:])
 
-        for m in range(PACK):
-            row_sums(m)
-        for m in (0, 2, 3, 1):
-            finish(m)
+        for t in range(PACK):
+            row_sums(t)
+        for t in (0, 2, 3, 1):
+            finish(t)

@@ -70,8 +70,8 @@ def tile_attend_gsoftc_kernel(tc, cT, dvT, pm, pw, offs, out_0, out_1):
 
         def turn(u):
             part = rounded[:, 2 * u * R : 2 * (u + 1) * R]
-            nc.vector.tensor_copy(part.rearrange("p (j w q e) -> p j w q e", j=2, w=2, e=2),
-                                  dv_raw[u][:].rearrange("p (j q w e) -> p j w q e", j=2, w=2, e=2))
+            nc.scalar.copy(part.rearrange("p (j w q e) -> p j w q e", j=2, w=2, e=2),
+                           dv_raw[u][:].rearrange("p (j q w e) -> p j w q e", j=2, w=2, e=2))
             words = part.bitcast(F32)
             bank = psum.tile([P, 2, 2, P], F32, name="turned%d" % u, tag="bank%d" % u)
             for j in range(2):

@@ -58,7 +58,7 @@ def tile_attend_gsoftc_kernel(tc, cT, dvT, pm, pw, offs, out_0, out_1):
 
         ident = tile([P, P], F32, "ident")
         make_identity(nc, ident[:])
-        windows = [tile([P, T], F32, "window%d" % w) for w in range(3)]
+        windows = [tile([P, T], F32, "window%d" % w) for w in range(2)]
         for window in windows:
             nc.vector.memset(window[:].bitcast(I32), 0)
         pw_codes = tile([P, HALF + SLOTS], U32, "pw_codes")
@@ -135,6 +135,8 @@ def tile_attend_gsoftc_kernel(tc, cT, dvT, pm, pw, offs, out_0, out_1):
         dvd_woven0 = tile([P, 2 * R], BF16, "dvd_woven0", "dvr_woven0")
         weave_dvd(0, dvd_woven0[:])
         dvd = quantize_dv("dvd0", dvd_woven0[:])
+        windows.append(tile([P, T], F32, "window2", "dvr_woven0"))
+        nc.gpsimd.memset(windows[2][:].bitcast(I32), 0)
 
         dc0a = copy_out(early[:, HALF:], "dc0a")
         scatter(windows[0], dc0a[:], 0, HALF)

@@ -23,7 +23,7 @@ P = 128
 PACK = 4
 HALF = SLOTS // 2
 HALF_T = T // 2
-GPSIMD_COLUMNS = (512, 320, 0, 0)
+GPSIMD_COLUMNS = (512, 0, 192, 0)
 
 
 def weave_views(dst, src):
@@ -199,7 +199,10 @@ def tile_attend_gsoftc_kernel(tc, cT, dvT, pm, pw, offs, out_0, out_1):
             queue = nc.sync if split else nc.scalar
             queue.dma_start(out0_rows[:, t, :], result[t][:])
 
-        for t in range(PACK):
+        for t in range(PACK - 1):
             row_sums(t)
-        for t in (0, 2, 3, 1):
-            finish(t)
+        finish(0)
+        finish(1)
+        row_sums(PACK - 1)
+        finish(2)
+        finish(3)

@@ -34,6 +34,7 @@ def tile_attend_gsoftc_kernel(tc, cT, dvT, pm, pw, offs, out_0, out_1):
     nc = tc.nc
     with ExitStack() as ctx:
         sb = ctx.enter_context(tc.tile_pool(name="sb", bufs=1))
+        laid = ctx.enter_context(tc.tile_pool(name="laid", bufs=1))
         psum = ctx.enter_context(tc.psum_pool(name="psum", bufs=1))
 
         def tile(shape, dtype, name, tag=None):
@@ -42,15 +43,16 @@ def tile_attend_gsoftc_kernel(tc, cT, dvT, pm, pw, offs, out_0, out_1):
         offsets = sb.tile([P, SLOTS // 16], U16, name="offsets")
         dv_raw = [tile([P, 2 * R], F32, "dv_raw%d" % u) for u in range(2)]
         pw_raw = [tile([P, PACK, HALF], F32, "pw_raw%d" % h) for h in range(2)]
-        c_raw = [[tile([P, 2, HALF_T], F32, "c_raw%d%d" % (u, h)) for h in range(2)] for u in range(2)]
+        c_raw = [[tile([P, 2, HALF_T], F32, "c_raw00"), laid.tile([P, 2, HALF_T], F32, name="c_raw01", offset=2048, align_bytes=64)],
+                 [tile([P, 2, HALF_T], F32, "c_raw1%d" % h) for h in range(2)]]
 
         dv_rows = dvT.rearrange("(p j) r -> p (j r)", j=PACK)
         pw_rows = pw.rearrange("(p t) i -> p t i", t=PACK)
         c_rows = cT.rearrange("(p j) t -> p j t", j=PACK)
-        for u in range(2):
-            nc.sync.dma_start(dv_raw[u][:], dv_rows[:, 2 * u * R : 2 * (u + 1) * R])
-        for h in range(2):
-            nc.sync.dma_start(pw_raw[h][:], pw_rows[:, :, h * HALF : (h + 1) * HALF])
+        nc.sync.dma_start(dv_raw[0][:], dv_rows[:, : 2 * R])
+        nc.sync.dma_start(pw_raw[0][:], pw_rows[:, :, :HALF])
+        nc.sync.dma_start(dv_raw[1][:], dv_rows[:, 2 * R :])
+        nc.sync.dma_start(pw_raw[1][:], pw_rows[:, :, HALF:])
         nc.sync.dma_start(offsets[:], offs)
         for u in range(2):
             for h in range(2):
@@ -68,22 +70,20 @@ def tile_attend_gsoftc_kernel(tc, cT, dvT, pm, pw, offs, out_0, out_1):
 
         rounded = tile([P, PACK * R], BF16, "dv_rounded")
 
-        def turn(u):
-            part = rounded[:, 2 * u * R : 2 * (u + 1) * R]
-            nc.scalar.copy(part.rearrange("p (j w q e) -> p j w q e", j=2, w=2, e=2),
-                           dv_raw[u][:].rearrange("p (j q w e) -> p j w q e", j=2, w=2, e=2))
+        def turn(first, bank):
+            planes = bank.shape[1]
+            part = rounded[:, first * R : (first + planes) * R]
+            raw = dv_raw[first // 2][:, first % 2 * R : (first % 2 + planes) * R]
+            nc.scalar.copy(part.rearrange("p (j w q e) -> p j w q e", j=planes, w=2, e=2),
+                           raw.rearrange("p (j q w e) -> p j w q e", j=planes, w=2, e=2))
             words = part.bitcast(F32)
-            bank = psum.tile([P, 2, 2, P], F32, name="turned%d" % u, tag="bank%d" % u)
-            for j in range(2):
+            for j in range(planes):
                 for w in range(2):
-                    first = (2 * j + w) * P
-                    nc.tensor.transpose(bank[:, j, w, :], words[:, first : first + P], ident[:])
-            return bank
+                    start = (2 * j + w) * P
+                    nc.tensor.transpose(bank[:, j, w, :], words[:, start : start + P], ident[:])
 
-        def weave_turned(u, bank):
-            woven = tile([P, 2 * R], BF16, "dvr_woven%d" % u)
-            nc.scalar.copy(woven[:].bitcast(F32).rearrange("q (j p w) -> q j p w", j=2, w=2), bank[:].rearrange("q j w p -> q j p w"))
-            return woven
+        def weave_turned(woven, bank):
+            nc.scalar.copy(woven.bitcast(F32).rearrange("q (j p w) -> q j p w", j=bank.shape[1], w=2), bank.rearrange("q j w p -> q j p w"))
 
         def quantize_dv(name, woven, codes_tag=None):
             width = woven.shape[1] // PACK
@@ -114,67 +114,80 @@ def tile_attend_gsoftc_kernel(tc, cT, dvT, pm, pw, offs, out_0, out_1):
         def scatter(window, dc, first, count):
             nc.vector.tensor_copy(window[:].indirect(offsets[:, first // 16 : (first + count) // 16]), dc)
 
-        def copy_out(source, name):
-            dc = tile([P, source.shape[1]], F32, name)
+        def copy_out(source, name, tag=None):
+            dc = tile([P, source.shape[1]], F32, name, tag)
             nc.scalar.copy(dc[:], source)
             return dc
 
         out1_rows = out_1.rearrange("(p j) t -> p j t", j=PACK)
 
-        banks = [turn(u) for u in range(2)]
-        woven = [weave_turned(u, banks[u]) for u in range(2)]
+        woven1 = tile([P, R], BF16, "dvr_woven1")
+        for j, woven in enumerate((rounded[:, 2 * R : 3 * R], woven1[:])):
+            bank = psum.tile([P, 1, 2, P], F32, name="turned%d" % j, tag="bank%d" % j)
+            turn(j, bank[:])
+            weave_turned(woven, bank[:])
         pw_woven0 = tile([P, PACK * HALF], BF16, "pw_woven0")
         weave_pw(0, pw_woven0[:])
-        dvr = quantize_dv("dvr0", woven[0][:])
+        dvr = quantize_dv("dvr0", rounded[:, 2 * R : 3 * R])
         quantize_pw(0, pw_woven0[:])
         early = product_dc(dvr[0], 0, "bank2")
-        pw_woven1 = tile([P, PACK * HALF], BF16, "pw_woven1", "dvr_woven0")
+        dvr.extend(quantize_dv("dvr1", woven1[:]))
+        bank23 = psum.tile([P, 2, 2, P], F32, name="turned23", tag="bank7")
+        turn(2, bank23[:])
+        pw_woven1 = tile([P, PACK * HALF], BF16, "pw_woven1", "dvr_woven1")
         weave_pw(1, pw_woven1[:])
-        dvr.extend(quantize_dv("dvr1", woven[1][:]))
         quantize_pw(1, pw_woven1[:])
-        dvd_woven0 = tile([P, 2 * R], BF16, "dvd_woven0", "dvr_woven0")
-        weave_dvd(0, dvd_woven0[:])
-        dvd = quantize_dv("dvd0", dvd_woven0[:])
-        windows.append(tile([P, T], F32, "window2", "dvr_woven0"))
-        nc.gpsimd.memset(windows[2][:].bitcast(I32), 0)
 
         dc0a = copy_out(early[:, HALF:], "dc0a")
         scatter(windows[0], dc0a[:], 0, HALF)
-        dc0b = copy_out(product_dc(dvr[0], HALF, "bank3")[:, HALF:], "dc0b")
+        second = product_dc(dvr[1], HALF, "bank4")
+        second_half = product_dc(dvr[0], HALF, "bank3")
+        woven23 = tile([P, 2 * R], BF16, "dvr_woven23")
+        weave_turned(woven23[:], bank23[:])
+        dvr.extend(quantize_dv("dvr23", woven23[:]))
+        windows.append(tile([P, T], F32, "window2", "dvr_woven23"))
+        nc.gpsimd.memset(windows[2][:].bitcast(I32), 0)
+        dc1 = copy_out(second[:], "dc1")
+        scatter(windows[1], dc1[:], 0, SLOTS)
+        nc.sync.dma_start(out1_rows[:, 1, :], windows[1][:])
+        pm_sb = tile([P, PACK, SLOTS], F32, "pm_sb", "dc1")
+        nc.sync.dma_start(pm_sb[:], pm.rearrange("(q t) i -> q t i", t=PACK))
+        dc0b = copy_out(second_half[:, HALF:], "dc0b")
         scatter(windows[0], dc0b[:], HALF, HALF)
         nc.sync.dma_start(out1_rows[:, 0, :], windows[0][:])
-        pm_sb = tile([P, PACK, SLOTS], F32, "pm_sb", "dc0b")
-        nc.sync.dma_start(pm_sb[:], pm.rearrange("(q t) i -> q t i", t=PACK))
-        for j in (1, 2):
-            dc = copy_out(product_dc(dvr[j], HALF, "bank%d" % (3 + j))[:], "dc%d" % j)
-            scatter(windows[j], dc[:], 0, SLOTS)
-            nc.sync.dma_start(out1_rows[:, j, :], windows[j][:])
+        third = product_dc(dvr[2], HALF, "bank5")
         last = product_dc(dvr[3], HALF, "bank6")
-        dc3a = copy_out(last[:, :HALF], "dc3a")
 
         picked = tile([P, 2, SLOTS], U32, "picked")
 
-        def gather(u, tag):
-            pairs = tile([P, T], U32, "c_pairs%d" % u, tag)
+        def gather(u, pairs):
             halves = pairs[:].bitcast(BF16).rearrange("p (t e) -> p t e", e=2)
             for h in range(2):
                 nc.scalar.activation(*weave_views(halves[:, h * HALF_T : (h + 1) * HALF_T, :], c_raw[u][h][:]), COPY)
             nc.vector.tensor_copy(picked[:, u, :], pairs[:].indirect(offsets[:]))
 
-        gather(0, "dvr1_codes")
-        scatter(windows[0], dc3a[:], 0, HALF)
-        gather(1, "c_raw01")
+        gather(0, tile([P, T], U32, "c_pairs0", "dvr0_codes"))
+        dc2 = laid.tile([P, SLOTS], F32, name="dc2", offset=1024, align_bytes=64)
+        nc.scalar.copy(dc2[:], third[:])
+        scatter(windows[2], dc2[:], 0, SLOTS)
+        nc.sync.dma_start(out1_rows[:, 2, :], windows[2][:])
+        gather(1, laid.tile([P, T], U32, name="c_pairs1", offset=3072, align_bytes=64))
         late = tile([P, HALF + R], F32, "late", "c_raw11")
-        nc.scalar.copy(late[:, :HALF], last[:, HALF:])
-        scatter(windows[0], late[:, :HALF], HALF, HALF)
-        nc.sync.dma_start(out1_rows[:, 3, :], windows[0][:])
-        weave_dvd(1, late[:, HALF:].bitcast(BF16))
+        nc.scalar.copy(late[:, :HALF], last[:, :HALF])
+        scatter(windows[1], late[:, :HALF], 0, HALF)
+        weave_dvd(0, late[:, HALF:].bitcast(BF16))
+        dvd = quantize_dv("dvd0", late[:, HALF:].bitcast(BF16))
         c_woven = tile([P, SLOTS * PACK], BF16, "c_woven")
         nc.scalar.copy(*weave_views(c_woven[:].bitcast(U32).rearrange("p (i u) -> p i u", u=2), picked[:]))
         c_codes = tile([P, SLOTS], U32, "c_codes")
         c_scales = tile([P, SLOTS], U8, "c_scales")
         nc.vector.quantize_mx(out=c_codes[:].bitcast(E4M3), scales=c_scales[:], in_=c_woven[:])
-        dvd.extend(quantize_dv("dvd1", late[:, HALF:].bitcast(BF16), "c_woven"))
+        latest = tile([P, HALF + R], F32, "latest", "picked")
+        nc.scalar.copy(latest[:, :HALF], last[:, HALF:])
+        scatter(windows[1], latest[:, :HALF], HALF, HALF)
+        nc.sync.dma_start(out1_rows[:, 3, :], windows[1][:])
+        weave_dvd(1, latest[:, HALF:].bitcast(BF16))
+        dvd.extend(quantize_dv("dvd1", latest[:, HALF:].bitcast(BF16)))
 
         dp = [psum.tile([P, SLOTS], F32, name="dp%d" % t, tag="bank%d" % t) for t in range(PACK)]
         weighted = [tile([P, SLOTS], F32, "weighted%d" % t) for t in range(PACK)]

@@ -34,7 +34,6 @@ def tile_attend_gsoftc_kernel(tc, cT, dvT, pm, pw, offs, out_0, out_1):
     nc = tc.nc
     with ExitStack() as ctx:
         sb = ctx.enter_context(tc.tile_pool(name="sb", bufs=1))
-        laid = ctx.enter_context(tc.tile_pool(name="laid", bufs=1))
         psum = ctx.enter_context(tc.psum_pool(name="psum", bufs=1))
 
         def tile(shape, dtype, name, tag=None):
@@ -43,16 +42,14 @@ def tile_attend_gsoftc_kernel(tc, cT, dvT, pm, pw, offs, out_0, out_1):
         offsets = sb.tile([P, SLOTS // 16], U16, name="offsets")
         dv_raw = [tile([P, 2 * R], F32, "dv_raw%d" % u) for u in range(2)]
         pw_raw = [tile([P, PACK, HALF], F32, "pw_raw%d" % h) for h in range(2)]
-        c_raw = [[tile([P, 2, HALF_T], F32, "c_raw00"), laid.tile([P, 2, HALF_T], F32, name="c_raw01", offset=2048, align_bytes=64)],
-                 [tile([P, 2, HALF_T], F32, "c_raw1%d" % h) for h in range(2)]]
+        c_raw = [[tile([P, 2, HALF_T], F32, "c_raw%d%d" % (u, h)) for h in range(2)] for u in range(2)]
 
         dv_rows = dvT.rearrange("(p j) r -> p (j r)", j=PACK)
         pw_rows = pw.rearrange("(p t) i -> p t i", t=PACK)
         c_rows = cT.rearrange("(p j) t -> p j t", j=PACK)
-        nc.sync.dma_start(dv_raw[0][:], dv_rows[:, : 2 * R])
-        nc.sync.dma_start(pw_raw[0][:], pw_rows[:, :, :HALF])
-        nc.sync.dma_start(dv_raw[1][:], dv_rows[:, 2 * R :])
-        nc.sync.dma_start(pw_raw[1][:], pw_rows[:, :, HALF:])
+        for half in range(2):
+            nc.sync.dma_start(dv_raw[half][:], dv_rows[:, 2 * half * R : 2 * (half + 1) * R])
+            nc.sync.dma_start(pw_raw[half][:], pw_rows[:, :, half * HALF : (half + 1) * HALF])
         nc.sync.dma_start(offsets[:], offs)
         for u in range(2):
             for h in range(2):
@@ -85,9 +82,9 @@ def tile_attend_gsoftc_kernel(tc, cT, dvT, pm, pw, offs, out_0, out_1):
         def weave_turned(woven, bank):
             nc.scalar.copy(woven.bitcast(F32).rearrange("q (j p w) -> q j p w", j=bank.shape[1], w=2), bank.rearrange("q j w p -> q j p w"))
 
-        def quantize_dv(name, woven, codes_tag=None):
+        def quantize_dv(name, woven):
             width = woven.shape[1] // PACK
-            codes = tile([P, width], U32, name + "_codes", codes_tag)
+            codes = tile([P, width], U32, name + "_codes")
             scales = tile([P, width], U8, name + "_scales")
             nc.vector.quantize_mx(out=codes[:].bitcast(E5M2), scales=scales[:], in_=woven)
             return [(codes[:, c : c + P], scales[:, c : c + P]) for c in range(0, width, P)]
@@ -114,80 +111,91 @@ def tile_attend_gsoftc_kernel(tc, cT, dvT, pm, pw, offs, out_0, out_1):
         def scatter(window, dc, first, count):
             nc.vector.tensor_copy(window[:].indirect(offsets[:, first // 16 : (first + count) // 16]), dc)
 
-        def copy_out(source, name, tag=None):
-            dc = tile([P, source.shape[1]], F32, name, tag)
+        def copy_out(source, name):
+            dc = tile([P, source.shape[1]], F32, name)
             nc.scalar.copy(dc[:], source)
             return dc
 
         out1_rows = out_1.rearrange("(p j) t -> p j t", j=PACK)
 
+        woven0 = rounded[:, 2 * R : 3 * R]
         woven1 = tile([P, R], BF16, "dvr_woven1")
-        for j, woven in enumerate((rounded[:, 2 * R : 3 * R], woven1[:])):
+        for j, woven in enumerate((woven0, woven1[:])):
             bank = psum.tile([P, 1, 2, P], F32, name="turned%d" % j, tag="bank%d" % j)
             turn(j, bank[:])
             weave_turned(woven, bank[:])
         pw_woven0 = tile([P, PACK * HALF], BF16, "pw_woven0")
         weave_pw(0, pw_woven0[:])
-        dvr = quantize_dv("dvr0", rounded[:, 2 * R : 3 * R])
+        dvr = quantize_dv("dvr0", woven0)
         quantize_pw(0, pw_woven0[:])
-        early = product_dc(dvr[0], 0, "bank2")
+        early0 = product_dc(dvr[0], 0, "bank2")
         dvr.extend(quantize_dv("dvr1", woven1[:]))
+        early1 = product_dc(dvr[1], 0, "bank6")
         bank23 = psum.tile([P, 2, 2, P], F32, name="turned23", tag="bank7")
         turn(2, bank23[:])
         pw_woven1 = tile([P, PACK * HALF], BF16, "pw_woven1", "dvr_woven1")
         weave_pw(1, pw_woven1[:])
         quantize_pw(1, pw_woven1[:])
 
-        dc0a = copy_out(early[:, HALF:], "dc0a")
+        dc0a = copy_out(early0[:, HALF:], "dc0a")
         scatter(windows[0], dc0a[:], 0, HALF)
-        second = product_dc(dvr[1], HALF, "bank4")
-        second_half = product_dc(dvr[0], HALF, "bank3")
+        dc1a = copy_out(early1[:, HALF:], "dc1a")
+        full1 = product_dc(dvr[1], HALF, "bank4")
+        full0 = product_dc(dvr[0], HALF, "bank3")
         woven23 = tile([P, 2 * R], BF16, "dvr_woven23")
         weave_turned(woven23[:], bank23[:])
         dvr.extend(quantize_dv("dvr23", woven23[:]))
         windows.append(tile([P, T], F32, "window2", "dvr_woven23"))
         nc.gpsimd.memset(windows[2][:].bitcast(I32), 0)
-        dc1 = copy_out(second[:], "dc1")
-        scatter(windows[1], dc1[:], 0, SLOTS)
-        nc.sync.dma_start(out1_rows[:, 1, :], windows[1][:])
-        pm_sb = tile([P, PACK, SLOTS], F32, "pm_sb", "dc1")
-        nc.sync.dma_start(pm_sb[:], pm.rearrange("(q t) i -> q t i", t=PACK))
-        dc0b = copy_out(second_half[:, HALF:], "dc0b")
-        scatter(windows[0], dc0b[:], HALF, HALF)
-        nc.sync.dma_start(out1_rows[:, 0, :], windows[0][:])
-        third = product_dc(dvr[2], HALF, "bank5")
-        last = product_dc(dvr[3], HALF, "bank6")
+        scatter(windows[1], dc1a[:], 0, HALF)
 
         picked = tile([P, 2, SLOTS], U32, "picked")
 
-        def gather(u, pairs):
+        def cast_chunk(u, h, pairs):
             halves = pairs[:].bitcast(BF16).rearrange("p (t e) -> p t e", e=2)
-            for h in range(2):
-                nc.scalar.activation(*weave_views(halves[:, h * HALF_T : (h + 1) * HALF_T, :], c_raw[u][h][:]), COPY)
+            nc.scalar.activation(*weave_views(halves[:, h * HALF_T : (h + 1) * HALF_T, :], c_raw[u][h][:]), COPY)
+
+        def gather(u, pairs):
             nc.vector.tensor_copy(picked[:, u, :], pairs[:].indirect(offsets[:]))
 
-        gather(0, tile([P, T], U32, "c_pairs0", "dvr0_codes"))
-        dc2 = laid.tile([P, SLOTS], F32, name="dc2", offset=1024, align_bytes=64)
-        nc.scalar.copy(dc2[:], third[:])
+        pairs0 = tile([P, T], U32, "c_pairs0", "dvr1_codes")
+        cast_chunk(0, 0, pairs0)
+        dc1b = copy_out(full1[:, HALF:], "dc1b")
+        scatter(windows[1], dc1b[:], HALF, HALF)
+        nc.sync.dma_start(out1_rows[:, 1, :], windows[1][:])
+        pm_sb = tile([P, PACK, SLOTS], F32, "pm_sb", "dc1b")
+        nc.sync.dma_start(pm_sb[:], pm.rearrange("(q t) i -> q t i", t=PACK))
+        dc0b = copy_out(full0[:, HALF:], "dc0b")
+        scatter(windows[0], dc0b[:], HALF, HALF)
+        nc.sync.dma_start(out1_rows[:, 0, :], windows[0][:])
+        full2 = product_dc(dvr[2], HALF, "bank5")
+        full3 = product_dc(dvr[3], HALF, "bank6")
+        cast_chunk(0, 1, pairs0)
+        gather(0, pairs0)
+        dc2 = copy_out(full2[:], "dc2")
         scatter(windows[2], dc2[:], 0, SLOTS)
         nc.sync.dma_start(out1_rows[:, 2, :], windows[2][:])
-        gather(1, laid.tile([P, T], U32, name="c_pairs1", offset=3072, align_bytes=64))
-        late = tile([P, HALF + R], F32, "late", "c_raw11")
-        nc.scalar.copy(late[:, :HALF], last[:, :HALF])
-        scatter(windows[1], late[:, :HALF], 0, HALF)
-        weave_dvd(0, late[:, HALF:].bitcast(BF16))
-        dvd = quantize_dv("dvd0", late[:, HALF:].bitcast(BF16))
+        pairs1 = tile([P, T], U32, "c_pairs1")
+        for h in range(2):
+            cast_chunk(1, h, pairs1)
+        gather(1, pairs1)
+
+        after_casts = tile([P, HALF + R], F32, "after_casts", "c_raw11")
+        nc.scalar.copy(after_casts[:, :HALF], full3[:, :HALF])
+        scatter(windows[1], after_casts[:, :HALF], 0, HALF)
+        weave_dvd(0, after_casts[:, HALF:].bitcast(BF16))
+        dvd = quantize_dv("dvd0", after_casts[:, HALF:].bitcast(BF16))
         c_woven = tile([P, SLOTS * PACK], BF16, "c_woven")
         nc.scalar.copy(*weave_views(c_woven[:].bitcast(U32).rearrange("p (i u) -> p i u", u=2), picked[:]))
         c_codes = tile([P, SLOTS], U32, "c_codes")
         c_scales = tile([P, SLOTS], U8, "c_scales")
         nc.vector.quantize_mx(out=c_codes[:].bitcast(E4M3), scales=c_scales[:], in_=c_woven[:])
-        latest = tile([P, HALF + R], F32, "latest", "picked")
-        nc.scalar.copy(latest[:, :HALF], last[:, HALF:])
-        scatter(windows[1], latest[:, :HALF], HALF, HALF)
+        after_weave = tile([P, HALF + R], F32, "after_weave", "picked")
+        nc.scalar.copy(after_weave[:, :HALF], full3[:, HALF:])
+        scatter(windows[1], after_weave[:, :HALF], HALF, HALF)
         nc.sync.dma_start(out1_rows[:, 3, :], windows[1][:])
-        weave_dvd(1, latest[:, HALF:].bitcast(BF16))
-        dvd.extend(quantize_dv("dvd1", latest[:, HALF:].bitcast(BF16)))
+        weave_dvd(1, after_weave[:, HALF:].bitcast(BF16))
+        dvd.extend(quantize_dv("dvd1", after_weave[:, HALF:].bitcast(BF16)))
 
         dp = [psum.tile([P, SLOTS], F32, name="dp%d" % t, tag="bank%d" % t) for t in range(PACK)]
         weighted = [tile([P, SLOTS], F32, "weighted%d" % t) for t in range(PACK)]

@@ -17,13 +17,10 @@ E5M2 = mybir.dt.float8_e5m2_x4
 COPY = mybir.ActivationFunctionType.Copy
 MULT = mybir.AluOpType.mult
 ADD = mybir.AluOpType.add
-IDENTITY = mybir.ActivationFunctionType.Identity
 
 P = 128
 PACK = 4
 HALF = SLOTS // 2
-HALF_T = T // 2
-GPSIMD_COLUMNS = (512, 0, 192, 0)
 
 
 def weave_views(dst, src):
@@ -40,35 +37,50 @@ def tile_attend_gsoftc_kernel(tc, cT, dvT, pm, pw, offs, out_0, out_1):
             return sb.tile(shape, dtype, name=name, tag=tag or name, align_bytes=64)
 
         offsets = sb.tile([P, SLOTS // 16], U16, name="offsets")
+        pw_raw = tile([P, PACK, SLOTS], F32, "pw_raw")
         dv_raw = [tile([P, 2 * R], F32, "dv_raw%d" % u) for u in range(2)]
-        pw_raw = [tile([P, PACK, HALF], F32, "pw_raw%d" % h) for h in range(2)]
-        c_raw = [[tile([P, 2, HALF_T], F32, "c_raw%d%d" % (u, h)) for h in range(2)] for u in range(2)]
+        c_raw = [tile([P, T], F32, "c_raw%d" % j) for j in range(PACK)]
+        pm_sb = tile([P, PACK, SLOTS], F32, "pm_sb")
 
         dv_rows = dvT.rearrange("(p j) r -> p (j r)", j=PACK)
-        pw_rows = pw.rearrange("(p t) i -> p t i", t=PACK)
         c_rows = cT.rearrange("(p j) t -> p j t", j=PACK)
-        for half in range(2):
-            nc.sync.dma_start(dv_raw[half][:], dv_rows[:, 2 * half * R : 2 * (half + 1) * R])
-            nc.sync.dma_start(pw_raw[half][:], pw_rows[:, :, half * HALF : (half + 1) * HALF])
-        nc.sync.dma_start(offsets[:], offs)
+        nc.sync.dma_start(pw_raw[:], pw.rearrange("(p t) i -> p t i", t=PACK))
         for u in range(2):
-            for h in range(2):
-                nc.sync.dma_start(c_raw[u][h][:], c_rows[:, 2 * u : 2 * u + 2, h * HALF_T : (h + 1) * HALF_T])
+            nc.sync.dma_start(dv_raw[u][:], dv_rows[:, 2 * u * R : 2 * (u + 1) * R])
+        nc.sync.dma_start(offsets[:], offs)
+        for j in range(PACK):
+            nc.sync.dma_start(c_raw[j][:], c_rows[:, j, :])
+        nc.sync.dma_start(pm_sb[:], pm.rearrange("(q t) i -> q t i", t=PACK))
 
         ident = tile([P, P], F32, "ident")
         make_identity(nc, ident[:])
         windows = [tile([P, T], F32, "window%d" % w) for w in range(2)]
         for window in windows:
             nc.vector.memset(window[:].bitcast(I32), 0)
-        pw_codes = tile([P, HALF + SLOTS], U32, "pw_codes")
-        pw_scales = tile([P, HALF + SLOTS], U8, "pw_scales")
-        nc.vector.memset(pw_codes[:, :HALF], 0)
-        nc.vector.memset(pw_scales[:, :HALF].bitcast(I32), 0)
+
+        def quantize(name, woven, fmt):
+            width = woven.shape[1] // PACK
+            codes = tile([P, width], U32, name + "_codes")
+            scales = tile([P, width], U8, name + "_scales")
+            nc.vector.quantize_mx(out=codes[:].bitcast(fmt), scales=scales[:], in_=woven)
+            return codes, scales
+
+        def quantize_dv(name, woven):
+            codes, scales = quantize(name, woven, E5M2)
+            return [(codes[:, c : c + P], scales[:, c : c + P]) for c in range(0, codes.shape[1], P)]
+
+        def product(bank, stationary, moving):
+            nc.tensor.matmul_mx(out=bank[:], lhsT=stationary[0].bitcast(E5M2), lhsT_scale=stationary[1],
+                                rhs=moving[0][:].bitcast(E4M3), rhs_scale=moving[1][:], start=True, stop=True)
+
+        pw_woven = tile([P, PACK * SLOTS], BF16, "pw_woven")
+        nc.vector.tensor_copy(*weave_views(pw_woven[:].rearrange("p (c t) -> p c t", t=PACK), pw_raw[:]))
+        pw_mx = quantize("pw", pw_woven[:], E4M3)
 
         rounded = tile([P, PACK * R], BF16, "dv_rounded")
 
-        def turn(first, bank):
-            planes = bank.shape[1]
+        def turn(first, planes, name):
+            bank = psum.tile([P, planes, 2, P], F32, name=name + "_bank", tag="bank%d" % first)
             part = rounded[:, first * R : (first + planes) * R]
             raw = dv_raw[first // 2][:, first % 2 * R : (first % 2 + planes) * R]
             nc.scalar.copy(part.rearrange("p (j w q e) -> p j w q e", j=planes, w=2, e=2),
@@ -78,152 +90,65 @@ def tile_attend_gsoftc_kernel(tc, cT, dvT, pm, pw, offs, out_0, out_1):
                 for w in range(2):
                     start = (2 * j + w) * P
                     nc.tensor.transpose(bank[:, j, w, :], words[:, start : start + P], ident[:])
+            woven = tile([P, planes * R], BF16, name)
+            nc.scalar.copy(woven[:].bitcast(F32).rearrange("q (j p w) -> q j p w", j=planes, w=2), bank[:].rearrange("q j w p -> q j p w"))
+            return quantize_dv(name, woven[:])
 
-        def weave_turned(woven, bank):
-            nc.scalar.copy(woven.bitcast(F32).rearrange("q (j p w) -> q j p w", j=bank.shape[1], w=2), bank.rearrange("q j w p -> q j p w"))
+        dvr = turn(0, 1, "dvr0") + turn(1, 1, "dvr1") + turn(2, 2, "dvr23")
+        dc_banks = [psum.tile([P, SLOTS], F32, name="dc_bank%d" % j, tag="bank%d" % (3 + j)) for j in range(PACK)]
+        for j in range(PACK):
+            product(dc_banks[j], dvr[j], pw_mx)
 
-        def quantize_dv(name, woven):
-            width = woven.shape[1] // PACK
-            codes = tile([P, width], U32, name + "_codes")
-            scales = tile([P, width], U8, name + "_scales")
-            nc.vector.quantize_mx(out=codes[:].bitcast(E5M2), scales=scales[:], in_=woven)
-            return [(codes[:, c : c + P], scales[:, c : c + P]) for c in range(0, width, P)]
-
-        def weave_dvd(h, woven):
-            nc.scalar.copy(woven.rearrange("p (e q j) -> p q j e", e=2, j=PACK),
-                           rounded[:].rearrange("p (j w q e) -> p w q j e", j=PACK, w=2, e=2)[:, h, :, :, :])
-
-        def product_dc(operand, first, bank_tag):
-            codes, scales = operand
-            bank = psum.tile([P, SLOTS], F32, name="dc_bank", tag=bank_tag)
-            nc.tensor.matmul_mx(out=bank[:], lhsT=codes.bitcast(E5M2), lhsT_scale=scales,
-                                rhs=pw_codes[:, first : first + SLOTS].bitcast(E4M3), rhs_scale=pw_scales[:, first : first + SLOTS],
-                                start=True, stop=True)
-            return bank
-
-        def quantize_pw(h, woven):
-            cols = slice((h + 1) * HALF, (h + 2) * HALF)
-            nc.vector.quantize_mx(out=pw_codes[:, cols].bitcast(E4M3), scales=pw_scales[:, cols], in_=woven)
-
-        def weave_pw(h, woven):
-            nc.vector.tensor_copy(*weave_views(woven.rearrange("p (c t) -> p c t", t=PACK), pw_raw[h][:]))
-
-        def scatter(window, dc, first, count):
-            nc.vector.tensor_copy(window[:].indirect(offsets[:, first // 16 : (first + count) // 16]), dc)
-
-        def copy_out(source, name):
-            dc = tile([P, source.shape[1]], F32, name)
-            nc.scalar.copy(dc[:], source)
-            return dc
+        dvd_woven = [tile([P, 2 * R], BF16, "dvd_woven%d" % h) for h in range(2)]
+        for h in range(2):
+            nc.vector.tensor_copy(dvd_woven[h][:].rearrange("p (e q j) -> p q j e", e=2, j=PACK),
+                                  rounded[:].rearrange("p (j w q e) -> p w q j e", j=PACK, w=2, e=2)[:, h, :, :, :])
+        dvd = quantize_dv("dvd0", dvd_woven[0][:]) + quantize_dv("dvd1", dvd_woven[1][:])
+        for h in range(2):
+            windows.append(tile([P, T], F32, "window%d" % (2 + h), "dvd_woven%d" % h))
+            nc.gpsimd.memset(windows[2 + h][:].bitcast(I32), 0)
 
         out1_rows = out_1.rearrange("(p j) t -> p j t", j=PACK)
 
-        woven0 = rounded[:, 2 * R : 3 * R]
-        woven1 = tile([P, R], BF16, "dvr_woven1")
-        for j, woven in enumerate((woven0, woven1[:])):
-            bank = psum.tile([P, 1, 2, P], F32, name="turned%d" % j, tag="bank%d" % j)
-            turn(j, bank[:])
-            weave_turned(woven, bank[:])
-        pw_woven0 = tile([P, PACK * HALF], BF16, "pw_woven0")
-        weave_pw(0, pw_woven0[:])
-        dvr = quantize_dv("dvr0", woven0)
-        quantize_pw(0, pw_woven0[:])
-        early0 = product_dc(dvr[0], 0, "bank2")
-        dvr.extend(quantize_dv("dvr1", woven1[:]))
-        early1 = product_dc(dvr[1], 0, "bank6")
-        bank23 = psum.tile([P, 2, 2, P], F32, name="turned23", tag="bank7")
-        turn(2, bank23[:])
-        pw_woven1 = tile([P, PACK * HALF], BF16, "pw_woven1", "dvr_woven1")
-        weave_pw(1, pw_woven1[:])
-        quantize_pw(1, pw_woven1[:])
+        for j in range(2):
+            dc = tile([P, SLOTS], F32, "dc%d" % j)
+            nc.scalar.copy(dc[:], dc_banks[j][:])
+            nc.vector.tensor_copy(windows[j][:].indirect(offsets[:]), dc[:])
+            nc.sync.dma_start(out1_rows[:, j, :], windows[j][:])
 
-        dc0a = copy_out(early0[:, HALF:], "dc0a")
-        scatter(windows[0], dc0a[:], 0, HALF)
-        dc1a = copy_out(early1[:, HALF:], "dc1a")
-        full1 = product_dc(dvr[1], HALF, "bank4")
-        full0 = product_dc(dvr[0], HALF, "bank3")
-        woven23 = tile([P, 2 * R], BF16, "dvr_woven23")
-        weave_turned(woven23[:], bank23[:])
-        dvr.extend(quantize_dv("dvr23", woven23[:]))
-        windows.append(tile([P, T], F32, "window2", "dvr_woven23"))
-        nc.gpsimd.memset(windows[2][:].bitcast(I32), 0)
-        scatter(windows[1], dc1a[:], 0, HALF)
+        picked = tile([P, PACK, SLOTS], BF16, "picked")
 
-        picked = tile([P, 2, SLOTS], U32, "picked")
+        def gather(j):
+            nc.scalar.activation(picked[:, j, :], c_raw[j][:].indirect(offsets[:]), COPY)
 
-        def cast_chunk(u, h, pairs):
-            halves = pairs[:].bitcast(BF16).rearrange("p (t e) -> p t e", e=2)
-            nc.scalar.activation(*weave_views(halves[:, h * HALF_T : (h + 1) * HALF_T, :], c_raw[u][h][:]), COPY)
+        def scatter_half(j, h, staged):
+            nc.scalar.copy(staged, dc_banks[j][:, h * HALF : (h + 1) * HALF])
+            nc.scalar.activation(windows[j][:].indirect(offsets[:, h * HALF // 16 : (h + 1) * HALF // 16]), staged, COPY)
 
-        def gather(u, pairs):
-            nc.vector.tensor_copy(picked[:, u, :], pairs[:].indirect(offsets[:]))
-
-        pairs0 = tile([P, T], U32, "c_pairs0", "dvr1_codes")
-        cast_chunk(0, 0, pairs0)
-        dc1b = copy_out(full1[:, HALF:], "dc1b")
-        scatter(windows[1], dc1b[:], HALF, HALF)
-        nc.sync.dma_start(out1_rows[:, 1, :], windows[1][:])
-        pm_sb = tile([P, PACK, SLOTS], F32, "pm_sb", "dc1b")
-        nc.sync.dma_start(pm_sb[:], pm.rearrange("(q t) i -> q t i", t=PACK))
-        dc0b = copy_out(full0[:, HALF:], "dc0b")
-        scatter(windows[0], dc0b[:], HALF, HALF)
-        nc.sync.dma_start(out1_rows[:, 0, :], windows[0][:])
-        full2 = product_dc(dvr[2], HALF, "bank5")
-        full3 = product_dc(dvr[3], HALF, "bank6")
-        cast_chunk(0, 1, pairs0)
-        gather(0, pairs0)
-        dc2 = copy_out(full2[:], "dc2")
-        scatter(windows[2], dc2[:], 0, SLOTS)
+        gather(0)
+        gather(1)
+        after1 = tile([P, HALF], F32, "after1", "c_raw1")
+        scatter_half(2, 0, after1[:])
+        gather(2)
+        gather(3)
+        after3 = tile([P, 3 * HALF], F32, "after3", "c_raw3")
+        scatter_half(2, 1, after3[:, :HALF])
         nc.sync.dma_start(out1_rows[:, 2, :], windows[2][:])
-        pairs1 = tile([P, T], U32, "c_pairs1")
         for h in range(2):
-            cast_chunk(1, h, pairs1)
-        gather(1, pairs1)
+            scatter_half(3, h, after3[:, (1 + h) * HALF : (2 + h) * HALF])
+        nc.sync.dma_start(out1_rows[:, 3, :], windows[3][:])
 
-        after_casts = tile([P, HALF + R], F32, "after_casts", "c_raw11")
-        nc.scalar.copy(after_casts[:, :HALF], full3[:, :HALF])
-        scatter(windows[1], after_casts[:, :HALF], 0, HALF)
-        weave_dvd(0, after_casts[:, HALF:].bitcast(BF16))
-        dvd = quantize_dv("dvd0", after_casts[:, HALF:].bitcast(BF16))
         c_woven = tile([P, SLOTS * PACK], BF16, "c_woven")
-        nc.scalar.copy(*weave_views(c_woven[:].bitcast(U32).rearrange("p (i u) -> p i u", u=2), picked[:]))
-        c_codes = tile([P, SLOTS], U32, "c_codes")
-        c_scales = tile([P, SLOTS], U8, "c_scales")
-        nc.vector.quantize_mx(out=c_codes[:].bitcast(E4M3), scales=c_scales[:], in_=c_woven[:])
-        after_weave = tile([P, HALF + R], F32, "after_weave", "picked")
-        nc.scalar.copy(after_weave[:, :HALF], full3[:, HALF:])
-        scatter(windows[1], after_weave[:, :HALF], HALF, HALF)
-        nc.sync.dma_start(out1_rows[:, 3, :], windows[1][:])
-        weave_dvd(1, after_weave[:, HALF:].bitcast(BF16))
-        dvd.extend(quantize_dv("dvd1", after_weave[:, HALF:].bitcast(BF16)))
+        nc.vector.tensor_copy(*weave_views(c_woven[:].rearrange("p (c t) -> p c t", t=PACK), picked[:]))
+        c_mx = quantize("c", c_woven[:], E4M3)
 
-        dp = [psum.tile([P, SLOTS], F32, name="dp%d" % t, tag="bank%d" % t) for t in range(PACK)]
-        weighted = [tile([P, SLOTS], F32, "weighted%d" % t) for t in range(PACK)]
-        minus_s = [tile([P, 1], F32, "minus_s%d" % t) for t in range(PACK)]
-        result = [tile([P, SLOTS], F32, "result%d" % t) for t in range(PACK)]
         out0_rows = out_0.rearrange("(q t) i -> q t i", t=PACK)
         for t in range(PACK):
-            nc.tensor.matmul_mx(out=dp[t][:], lhsT=dvd[t][0].bitcast(E5M2), lhsT_scale=dvd[t][1],
-                                rhs=c_codes[:].bitcast(E4M3), rhs_scale=c_scales[:], start=True, stop=True)
-
-        def row_sums(t):
-            nc.vector.scalar_tensor_tensor(weighted[t][:], dp[t][:], -1.0, pm_sb[:, t, :], MULT, MULT, accum_out=minus_s[t][:])
-
-        def finish(t):
-            split = GPSIMD_COLUMNS[t]
-            if split:
-                centred = tile([P, split], F32, "centred%d" % t)
-                nc.scalar.activation(centred[:], dp[t][:, :split], IDENTITY, bias=minus_s[t][:])
-                nc.gpsimd.tensor_tensor(result[t][:, :split], centred[:], pm_sb[:, t, :split], MULT)
-            if split < SLOTS:
-                nc.vector.scalar_tensor_tensor(result[t][:, split:], dp[t][:, split:], minus_s[t][:], pm_sb[:, t, split:], ADD, MULT)
-            queue = nc.sync if split else nc.scalar
-            queue.dma_start(out0_rows[:, t, :], result[t][:])
-
-        for t in range(PACK - 1):
-            row_sums(t)
-        finish(0)
-        finish(1)
-        row_sums(PACK - 1)
-        finish(2)
-        finish(3)
+            dp = psum.tile([P, SLOTS], F32, name="dp%d" % t, tag="bank%d" % (t if t < 3 else 7))
+            product(dp, dvd[t], c_mx)
+            weighted = tile([P, SLOTS], F32, "weighted%d" % t)
+            minus_s = tile([P, 1], F32, "minus_s%d" % t)
+            result = tile([P, SLOTS], F32, "result%d" % t)
+            nc.vector.scalar_tensor_tensor(weighted[:], dp[:], -1.0, pm_sb[:, t, :], MULT, MULT, accum_out=minus_s[:])
+            nc.vector.scalar_tensor_tensor(result[:], dp[:], minus_s[:], pm_sb[:, t, :], ADD, MULT)
+            nc.sync.dma_start(out0_rows[:, t, :], result[:])

@@ -38,16 +38,16 @@ def tile_attend_gsoftc_kernel(tc, cT, dvT, pm, pw, offs, out_0, out_1):
 
         offsets = sb.tile([P, SLOTS // 16], U16, name="offsets")
         pw_raw = tile([P, PACK, SLOTS], F32, "pw_raw")
-        dv_raw = [tile([P, 2 * R], F32, "dv_raw%d" % u) for u in range(2)]
+        dv_raw = [tile([P, R], F32, "dv_raw0"), tile([P, 3 * R], F32, "dv_raw123")]
         c_raw = [tile([P, T], F32, "c_raw%d" % j) for j in range(PACK)]
         pm_sb = tile([P, PACK, SLOTS], F32, "pm_sb")
 
         dv_rows = dvT.rearrange("(p j) r -> p (j r)", j=PACK)
         c_rows = cT.rearrange("(p j) t -> p j t", j=PACK)
+        nc.sync.dma_start(dv_raw[0][:], dv_rows[:, :R])
         nc.sync.dma_start(pw_raw[:], pw.rearrange("(p t) i -> p t i", t=PACK))
-        for u in range(2):
-            nc.sync.dma_start(dv_raw[u][:], dv_rows[:, 2 * u * R : 2 * (u + 1) * R])
         nc.sync.dma_start(offsets[:], offs)
+        nc.sync.dma_start(dv_raw[1][:], dv_rows[:, R:])
         for j in range(PACK):
             nc.sync.dma_start(c_raw[j][:], c_rows[:, j, :])
         nc.sync.dma_start(pm_sb[:], pm.rearrange("(q t) i -> q t i", t=PACK))
@@ -70,85 +70,95 @@ def tile_attend_gsoftc_kernel(tc, cT, dvT, pm, pw, offs, out_0, out_1):
             return [(codes[:, c : c + P], scales[:, c : c + P]) for c in range(0, codes.shape[1], P)]
 
         def product(bank, stationary, moving):
-            nc.tensor.matmul_mx(out=bank[:], lhsT=stationary[0].bitcast(E5M2), lhsT_scale=stationary[1],
+            nc.tensor.matmul_mx(out=bank, lhsT=stationary[0].bitcast(E5M2), lhsT_scale=stationary[1],
                                 rhs=moving[0][:].bitcast(E4M3), rhs_scale=moving[1][:], start=True, stop=True)
 
-        pw_woven = tile([P, PACK * SLOTS], BF16, "pw_woven")
-        nc.vector.tensor_copy(*weave_views(pw_woven[:].rearrange("p (c t) -> p c t", t=PACK), pw_raw[:]))
-        pw_mx = quantize("pw", pw_woven[:], E4M3)
+        staging = tile([P, (PACK + 2) * R], BF16, "staging")
+        rounded = staging[:, : PACK * R]
+        turned0 = staging[:, 7 * R // 2 : 9 * R // 2]
+        pw_woven = [staging[:, 2 * R : 4 * R], staging[:, 4 * R :]]
 
-        rounded = tile([P, PACK * R], BF16, "dv_rounded")
+        def round_dv(first, planes, raw, copy):
+            copy(rounded[:, first * R : (first + planes) * R].rearrange("p (j w q e) -> p j w q e", j=planes, w=2, e=2),
+                 raw.rearrange("p (j q w e) -> p j w q e", j=planes, w=2, e=2))
 
-        def turn(first, planes, name):
-            bank = psum.tile([P, planes, 2, P], F32, name=name + "_bank", tag="bank%d" % first)
-            part = rounded[:, first * R : (first + planes) * R]
-            raw = dv_raw[first // 2][:, first % 2 * R : (first % 2 + planes) * R]
-            nc.scalar.copy(part.rearrange("p (j w q e) -> p j w q e", j=planes, w=2, e=2),
-                           raw.rearrange("p (j q w e) -> p j w q e", j=planes, w=2, e=2))
-            words = part.bitcast(F32)
+        def turn(first, planes, copy, woven):
+            bank = psum.tile([P, planes, 2, P], F32, name="turned%d" % first, tag="bank%d" % first)
+            words = rounded[:, first * R : (first + planes) * R].bitcast(F32)
             for j in range(planes):
                 for w in range(2):
                     start = (2 * j + w) * P
                     nc.tensor.transpose(bank[:, j, w, :], words[:, start : start + P], ident[:])
-            woven = tile([P, planes * R], BF16, name)
-            nc.scalar.copy(woven[:].bitcast(F32).rearrange("q (j p w) -> q j p w", j=planes, w=2), bank[:].rearrange("q j w p -> q j p w"))
-            return quantize_dv(name, woven[:])
+            copy(woven.bitcast(F32).rearrange("q (j p w) -> q j p w", j=planes, w=2), bank[:].rearrange("q j w p -> q j p w"))
+            return quantize_dv("dvr%d" % first, woven)
 
-        dvr = turn(0, 1, "dvr0") + turn(1, 1, "dvr1") + turn(2, 2, "dvr23")
-        dc_banks = [psum.tile([P, SLOTS], F32, name="dc_bank%d" % j, tag="bank%d" % (3 + j)) for j in range(PACK)]
-        for j in range(PACK):
-            product(dc_banks[j], dvr[j], pw_mx)
+        def quantize_dvd(h, tag):
+            woven = tile([P, 2 * R], BF16, "dvd_woven%d" % h, tag)
+            nc.vector.tensor_copy(woven[:].rearrange("p (e q j) -> p q j e", e=2, j=PACK),
+                                  rounded.rearrange("p (j w q e) -> p w q j e", j=PACK, w=2, e=2)[:, h, :, :, :])
+            return quantize_dv("dvd%d" % h, woven[:])
 
-        dvd_woven = [tile([P, 2 * R], BF16, "dvd_woven%d" % h) for h in range(2)]
-        for h in range(2):
-            nc.vector.tensor_copy(dvd_woven[h][:].rearrange("p (e q j) -> p q j e", e=2, j=PACK),
-                                  rounded[:].rearrange("p (j w q e) -> p w q j e", j=PACK, w=2, e=2)[:, h, :, :, :])
-        dvd = quantize_dv("dvd0", dvd_woven[0][:]) + quantize_dv("dvd1", dvd_woven[1][:])
-        for h in range(2):
-            windows.append(tile([P, T], F32, "window%d" % (2 + h), "dvd_woven%d" % h))
-            nc.gpsimd.memset(windows[2 + h][:].bitcast(I32), 0)
+        def quantize_pw(h, copy):
+            copy(*weave_views(pw_woven[h].rearrange("p (c t) -> p c t", t=PACK), pw_raw[:, :, h * HALF : (h + 1) * HALF]))
+            return quantize("pw%d" % h, pw_woven[h], E4M3)
 
         out1_rows = out_1.rearrange("(p j) t -> p j t", j=PACK)
 
-        for j in range(2):
-            dc = tile([P, SLOTS], F32, "dc%d" % j)
-            nc.scalar.copy(dc[:], dc_banks[j][:])
-            nc.vector.tensor_copy(windows[j][:].indirect(offsets[:]), dc[:])
-            nc.sync.dma_start(out1_rows[:, j, :], windows[j][:])
+        def products_dc(planes, h, copy, bank_nr):
+            bank = psum.tile([P, len(planes), HALF], F32, name="dc_bank%d" % bank_nr, tag="bank%d" % bank_nr)
+            for e, j in enumerate(planes):
+                product(bank[:, e, :], dvr[j], pw_mx[h])
+            dc = tile([P, len(planes), HALF], F32, "dc%d" % bank_nr)
+            copy(dc[:], bank[:])
+            return {j: dc[:, e, :] for e, j in enumerate(planes)}
 
-        picked = tile([P, PACK, SLOTS], BF16, "picked")
+        def products_plane(j, bank_nr):
+            bank = psum.tile([P, 2, HALF], F32, name="dc_bank%d" % bank_nr, tag="bank%d" % bank_nr)
+            for h in range(2):
+                product(bank[:, h, :], dvr[j], pw_mx[h])
+            dc = tile([P, 2, HALF], F32, "dc%d" % bank_nr)
+            nc.vector.tensor_copy(dc[:], bank[:])
+            return [{j: dc[:, h, :]} for h in range(2)]
 
-        def gather(j):
-            nc.scalar.activation(picked[:, j, :], c_raw[j][:].indirect(offsets[:]), COPY)
+        def scatter_half(j, h, dc):
+            nc.scalar.activation(windows[j][:].indirect(offsets[:, h * HALF // 16 : (h + 1) * HALF // 16]), dc[j], COPY)
+            if h == 1:
+                nc.sync.dma_start(out1_rows[:, j, :], windows[j][:])
 
-        def scatter_half(j, h, staged):
-            nc.scalar.copy(staged, dc_banks[j][:, h * HALF : (h + 1) * HALF])
-            nc.scalar.activation(windows[j][:].indirect(offsets[:, h * HALF // 16 : (h + 1) * HALF // 16]), staged, COPY)
-
-        gather(0)
-        gather(1)
-        after1 = tile([P, HALF], F32, "after1", "c_raw1")
-        scatter_half(2, 0, after1[:])
-        gather(2)
-        gather(3)
-        after3 = tile([P, 3 * HALF], F32, "after3", "c_raw3")
-        scatter_half(2, 1, after3[:, :HALF])
-        nc.sync.dma_start(out1_rows[:, 2, :], windows[2][:])
+        round_dv(0, 1, dv_raw[0][:], nc.scalar.copy)
+        dvr = turn(0, 1, nc.scalar.copy, turned0)
+        pw_mx = [quantize_pw(0, nc.vector.tensor_copy), quantize_pw(1, nc.scalar.copy)]
         for h in range(2):
-            scatter_half(3, h, after3[:, (1 + h) * HALF : (2 + h) * HALF])
-        nc.sync.dma_start(out1_rows[:, 3, :], windows[3][:])
+            scatter_half(0, h, products_dc([0], h, nc.scalar.copy, 3 + h))
+        round_dv(1, 3, dv_raw[1][:], nc.vector.tensor_copy)
+        dvr.extend(turn(1, 1, nc.vector.tensor_copy, tile([P, R], BF16, "dvr_woven1")[:]))
+        dvr.extend(turn(2, 2, nc.vector.tensor_copy, tile([P, 2 * R], BF16, "dvr_woven2")[:]))
+        dc1 = products_plane(1, 5)
+        for h in range(2):
+            scatter_half(1, h, dc1[h])
+        dvd = quantize_dvd(0, None)
+        dc23 = {j: products_plane(j, 4 + j) for j in (2, 3)}
 
-        c_woven = tile([P, SLOTS * PACK], BF16, "c_woven")
-        nc.vector.tensor_copy(*weave_views(c_woven[:].rearrange("p (c t) -> p c t", t=PACK), picked[:]))
+        c_woven = tile([P, SLOTS * PACK], BF16, "c_woven", "dvr_woven2")
+        for j in range(PACK):
+            nc.vector.tensor_copy(c_woven[:].rearrange("p (c t) -> p c t", t=PACK)[:, :, j], c_raw[j][:].indirect(offsets[:]))
         c_mx = quantize("c", c_woven[:], E4M3)
+        dvd.extend(quantize_dvd(1, "c_raw2"))
+
+        for name, tag in (("window2", "c_raw0"), ("window3", "c_raw1")):
+            windows.append(tile([P, T], F32, name, tag))
+            nc.gpsimd.memset(windows[-1][:].bitcast(I32), 0)
+        for j in (2, 3):
+            for h in range(2):
+                scatter_half(j, h, dc23[j][h])
 
         out0_rows = out_0.rearrange("(q t) i -> q t i", t=PACK)
+        result = tile([P, PACK, SLOTS], F32, "result")
         for t in range(PACK):
-            dp = psum.tile([P, SLOTS], F32, name="dp%d" % t, tag="bank%d" % (t if t < 3 else 7))
-            product(dp, dvd[t], c_mx)
+            dp = psum.tile([P, SLOTS], F32, name="dp%d" % t, tag="bank%d" % t)
+            product(dp[:], dvd[t], c_mx)
             weighted = tile([P, SLOTS], F32, "weighted%d" % t)
             minus_s = tile([P, 1], F32, "minus_s%d" % t)
-            result = tile([P, SLOTS], F32, "result%d" % t)
             nc.vector.scalar_tensor_tensor(weighted[:], dp[:], -1.0, pm_sb[:, t, :], MULT, MULT, accum_out=minus_s[:])
-            nc.vector.scalar_tensor_tensor(result[:], dp[:], minus_s[:], pm_sb[:, t, :], ADD, MULT)
-            nc.sync.dma_start(out0_rows[:, t, :], result[:])
+            nc.vector.scalar_tensor_tensor(result[:, t, :], dp[:], minus_s[:], pm_sb[:, t, :], ADD, MULT)
+            nc.sync.dma_start(out0_rows[:, t, :], result[:, t, :])

@@ -17,10 +17,12 @@ E5M2 = mybir.dt.float8_e5m2_x4
 COPY = mybir.ActivationFunctionType.Copy
 MULT = mybir.AluOpType.mult
 ADD = mybir.AluOpType.add
+IDENTITY = mybir.ActivationFunctionType.Identity
 
 P = 128
 PACK = 4
 HALF = SLOTS // 2
+GPSIMD_COLUMNS = (512, 0, 0, 0)
 
 
 def weave_views(dst, src):
@@ -38,16 +40,16 @@ def tile_attend_gsoftc_kernel(tc, cT, dvT, pm, pw, offs, out_0, out_1):
 
         offsets = sb.tile([P, SLOTS // 16], U16, name="offsets")
         pw_raw = tile([P, PACK, SLOTS], F32, "pw_raw")
-        dv_raw = [tile([P, R], F32, "dv_raw0"), tile([P, 3 * R], F32, "dv_raw123")]
+        dv_raw = [tile([P, 2 * R], F32, "dv_raw%d" % u) for u in range(2)]
         c_raw = [tile([P, T], F32, "c_raw%d" % j) for j in range(PACK)]
         pm_sb = tile([P, PACK, SLOTS], F32, "pm_sb")
 
         dv_rows = dvT.rearrange("(p j) r -> p (j r)", j=PACK)
         c_rows = cT.rearrange("(p j) t -> p j t", j=PACK)
-        nc.sync.dma_start(dv_raw[0][:], dv_rows[:, :R])
+        nc.sync.dma_start(dv_raw[0][:], dv_rows[:, : 2 * R])
         nc.sync.dma_start(pw_raw[:], pw.rearrange("(p t) i -> p t i", t=PACK))
         nc.sync.dma_start(offsets[:], offs)
-        nc.sync.dma_start(dv_raw[1][:], dv_rows[:, R:])
+        nc.sync.dma_start(dv_raw[1][:], dv_rows[:, 2 * R :])
         for j in range(PACK):
             nc.sync.dma_start(c_raw[j][:], c_rows[:, j, :])
         nc.sync.dma_start(pm_sb[:], pm.rearrange("(q t) i -> q t i", t=PACK))
@@ -75,7 +77,7 @@ def tile_attend_gsoftc_kernel(tc, cT, dvT, pm, pw, offs, out_0, out_1):
 
         staging = tile([P, (PACK + 2) * R], BF16, "staging")
         rounded = staging[:, : PACK * R]
-        turned0 = staging[:, 7 * R // 2 : 9 * R // 2]
+        turned1 = staging[:, 7 * R // 2 : 9 * R // 2]
         pw_woven = [staging[:, 2 * R : 4 * R], staging[:, 4 * R :]]
 
         def round_dv(first, planes, raw, copy):
@@ -92,11 +94,10 @@ def tile_attend_gsoftc_kernel(tc, cT, dvT, pm, pw, offs, out_0, out_1):
             copy(woven.bitcast(F32).rearrange("q (j p w) -> q j p w", j=planes, w=2), bank[:].rearrange("q j w p -> q j p w"))
             return quantize_dv("dvr%d" % first, woven)
 
-        def quantize_dvd(h, tag):
-            woven = tile([P, 2 * R], BF16, "dvd_woven%d" % h, tag)
-            nc.vector.tensor_copy(woven[:].rearrange("p (e q j) -> p q j e", e=2, j=PACK),
+        def quantize_dvd(h, woven):
+            nc.vector.tensor_copy(woven.rearrange("p (e q j) -> p q j e", e=2, j=PACK),
                                   rounded.rearrange("p (j w q e) -> p w q j e", j=PACK, w=2, e=2)[:, h, :, :, :])
-            return quantize_dv("dvd%d" % h, woven[:])
+            return quantize_dv("dvd%d" % h, woven)
 
         def quantize_pw(h, copy):
             copy(*weave_views(pw_woven[h].rearrange("p (c t) -> p c t", t=PACK), pw_raw[:, :, h * HALF : (h + 1) * HALF]))
@@ -104,61 +105,66 @@ def tile_attend_gsoftc_kernel(tc, cT, dvT, pm, pw, offs, out_0, out_1):
 
         out1_rows = out_1.rearrange("(p j) t -> p j t", j=PACK)
 
-        def products_dc(planes, h, copy, bank_nr):
-            bank = psum.tile([P, len(planes), HALF], F32, name="dc_bank%d" % bank_nr, tag="bank%d" % bank_nr)
+        def products_dc(planes, h, copy, bank_nr, tag=None):
+            bank = psum.tile([P, len(planes), HALF], F32, name="dc_bank%d%d" % (planes[0], h), tag="bank%d" % bank_nr)
             for e, j in enumerate(planes):
                 product(bank[:, e, :], dvr[j], pw_mx[h])
-            dc = tile([P, len(planes), HALF], F32, "dc%d" % bank_nr)
+            dc = tile([P, len(planes), HALF], F32, "dc%d%d" % (planes[0], h), tag)
             copy(dc[:], bank[:])
             return {j: dc[:, e, :] for e, j in enumerate(planes)}
 
-        def products_plane(j, bank_nr):
-            bank = psum.tile([P, 2, HALF], F32, name="dc_bank%d" % bank_nr, tag="bank%d" % bank_nr)
-            for h in range(2):
-                product(bank[:, h, :], dvr[j], pw_mx[h])
-            dc = tile([P, 2, HALF], F32, "dc%d" % bank_nr)
-            nc.vector.tensor_copy(dc[:], bank[:])
-            return [{j: dc[:, h, :]} for h in range(2)]
+        def scalar_move(out, in_):
+            nc.scalar.activation(out, in_, COPY)
 
-        def scatter_half(j, h, dc):
-            nc.scalar.activation(windows[j][:].indirect(offsets[:, h * HALF // 16 : (h + 1) * HALF // 16]), dc[j], COPY)
+        def scatter_half(j, h, dc, move=scalar_move):
+            move(windows[j][:].indirect(offsets[:, h * HALF // 16 : (h + 1) * HALF // 16]), dc[j])
             if h == 1:
                 nc.sync.dma_start(out1_rows[:, j, :], windows[j][:])
 
-        round_dv(0, 1, dv_raw[0][:], nc.scalar.copy)
-        dvr = turn(0, 1, nc.scalar.copy, turned0)
+        dvr = []
+        for j, woven in enumerate((tile([P, R], BF16, "turned0")[:], turned1)):
+            round_dv(j, 1, dv_raw[0][:, j * R : (j + 1) * R], nc.scalar.copy)
+            dvr.extend(turn(j, 1, nc.scalar.copy, woven))
         pw_mx = [quantize_pw(0, nc.vector.tensor_copy), quantize_pw(1, nc.scalar.copy)]
-        for h in range(2):
-            scatter_half(0, h, products_dc([0], h, nc.scalar.copy, 3 + h))
-        round_dv(1, 3, dv_raw[1][:], nc.vector.tensor_copy)
-        dvr.extend(turn(1, 1, nc.vector.tensor_copy, tile([P, R], BF16, "dvr_woven1")[:]))
-        dvr.extend(turn(2, 2, nc.vector.tensor_copy, tile([P, 2 * R], BF16, "dvr_woven2")[:]))
-        dc1 = products_plane(1, 5)
-        for h in range(2):
-            scatter_half(1, h, dc1[h])
-        dvd = quantize_dvd(0, None)
-        dc23 = {j: products_plane(j, 4 + j) for j in (2, 3)}
-
-        c_woven = tile([P, SLOTS * PACK], BF16, "c_woven", "dvr_woven2")
-        for j in range(PACK):
-            nc.vector.tensor_copy(c_woven[:].rearrange("p (c t) -> p c t", t=PACK)[:, :, j], c_raw[j][:].indirect(offsets[:]))
-        c_mx = quantize("c", c_woven[:], E4M3)
-        dvd.extend(quantize_dvd(1, "c_raw2"))
-
-        for name, tag in (("window2", "c_raw0"), ("window3", "c_raw1")):
+        for j in range(2):
+            scatter_half(j, 0, products_dc([j], 0, nc.scalar.copy, 3 + j))
+        scatter_half(0, 1, products_dc([0], 1, nc.vector.tensor_copy, 5))
+        round_dv(2, 1, dv_raw[1][:, :R], nc.scalar.copy)
+        round_dv(3, 1, dv_raw[1][:, R:], nc.vector.tensor_copy)
+        gathered = tile([P, (PACK + 1) * SLOTS], BF16, "gathered")
+        picked = gathered[:, SLOTS:].rearrange("p (j i) -> p j i", j=PACK)
+        dvr.extend(turn(2, 2, nc.vector.tensor_copy, gathered[:, 5 * SLOTS // 2 : 9 * SLOTS // 2]))
+        dvd = quantize_dvd(0, gathered[:, : 2 * SLOTS])
+        dc23 = [products_dc([2, 3], h, nc.scalar.copy, 6 + h) for h in range(2)]
+        for name, tag in (("window2", "dvr2_codes"), ("window3", "dvr2_scales")):
             windows.append(tile([P, T], F32, name, tag))
             nc.gpsimd.memset(windows[-1][:].bitcast(I32), 0)
+
+        for j in range(PACK):
+            nc.vector.tensor_copy(picked[:, j, :], c_raw[j][:].indirect(offsets[:]))
+            if j == 0:
+                scatter_half(1, 1, products_dc([1], 1, nc.vector.tensor_copy, 0, "c_raw0"), nc.vector.tensor_copy)
         for j in (2, 3):
             for h in range(2):
-                scatter_half(j, h, dc23[j][h])
+                scatter_half(j, h, dc23[h])
+        c_woven = tile([P, SLOTS * PACK], BF16, "c_woven")
+        nc.vector.tensor_copy(*weave_views(c_woven[:].rearrange("p (c t) -> p c t", t=PACK), picked))
+        c_mx = quantize("c", c_woven[:], E4M3)
+        dvd.extend(quantize_dvd(1, tile([P, 2 * R], BF16, "dvd_woven1", "c_raw2")[:]))
 
         out0_rows = out_0.rearrange("(q t) i -> q t i", t=PACK)
-        result = tile([P, PACK, SLOTS], F32, "result")
+        dp = [psum.tile([P, SLOTS], F32, name="dp%d" % t, tag="bank%d" % t) for t in range(PACK)]
+        weighted = [tile([P, SLOTS], F32, "weighted%d" % t) for t in range(PACK)]
+        minus_s = [tile([P, 1], F32, "minus_s%d" % t) for t in range(PACK)]
+        result = [tile([P, SLOTS], F32, "result%d" % t) for t in range(PACK)]
         for t in range(PACK):
-            dp = psum.tile([P, SLOTS], F32, name="dp%d" % t, tag="bank%d" % t)
-            product(dp[:], dvd[t], c_mx)
-            weighted = tile([P, SLOTS], F32, "weighted%d" % t)
-            minus_s = tile([P, 1], F32, "minus_s%d" % t)
-            nc.vector.scalar_tensor_tensor(weighted[:], dp[:], -1.0, pm_sb[:, t, :], MULT, MULT, accum_out=minus_s[:])
-            nc.vector.scalar_tensor_tensor(result[:, t, :], dp[:], minus_s[:], pm_sb[:, t, :], ADD, MULT)
-            nc.sync.dma_start(out0_rows[:, t, :], result[:, t, :])
+            product(dp[t][:], dvd[t], c_mx)
+            nc.vector.scalar_tensor_tensor(weighted[t][:], dp[t][:], -1.0, pm_sb[:, t, :], MULT, MULT, accum_out=minus_s[t][:])
+            split = GPSIMD_COLUMNS[t]
+            if split:
+                centred = tile([P, split], F32, "centred%d" % t)
+                nc.scalar.activation(centred[:], dp[t][:, :split], IDENTITY, bias=minus_s[t][:])
+                nc.gpsimd.tensor_tensor(result[t][:, :split], centred[:], pm_sb[:, t, :split], MULT)
+            if split < SLOTS:
+                nc.vector.scalar_tensor_tensor(result[t][:, split:], dp[t][:, split:], minus_s[t][:], pm_sb[:, t, split:], ADD, MULT)
+            nc.sync.dma_start(out0_rows[:, t, :], result[t][:])

@@ -22,11 +22,10 @@ IDENTITY = mybir.ActivationFunctionType.Identity
 P = 128
 PACK = 4
 HALF = SLOTS // 2
-GPSIMD_COLUMNS = (512, 0, 0, 0)
 
 
 def weave_views(dst, src):
-    return dst.rearrange("p (c i) t -> p c t i", i=4), src.rearrange("p t (c i) -> p c t i", i=4)
+    return dst.rearrange("p (c i t) -> p c t i", i=4, t=PACK), src.rearrange("p t (c i) -> p c t i", i=4)
 
 
 def tile_attend_gsoftc_kernel(tc, cT, dvT, pm, pw, offs, out_0, out_1):
@@ -38,16 +37,24 @@ def tile_attend_gsoftc_kernel(tc, cT, dvT, pm, pw, offs, out_0, out_1):
         def tile(shape, dtype, name, tag=None):
             return sb.tile(shape, dtype, name=name, tag=tag or name, align_bytes=64)
 
+        def bank(shape, name, nr):
+            return psum.tile(shape, F32, name=name, tag="bank%d" % nr)
+
+        def half(h):
+            return slice(h * HALF, (h + 1) * HALF)
+
         offsets = sb.tile([P, SLOTS // 16], U16, name="offsets")
-        pw_raw = tile([P, PACK, SLOTS], F32, "pw_raw")
+        pw_raw = [tile([P, PACK, HALF], F32, "pw_raw%d" % h) for h in range(2)]
         dv_raw = [tile([P, 2 * R], F32, "dv_raw%d" % u) for u in range(2)]
         c_raw = [tile([P, T], F32, "c_raw%d" % j) for j in range(PACK)]
         pm_sb = tile([P, PACK, SLOTS], F32, "pm_sb")
 
         dv_rows = dvT.rearrange("(p j) r -> p (j r)", j=PACK)
+        pw_rows = pw.rearrange("(p t) i -> p t i", t=PACK)
         c_rows = cT.rearrange("(p j) t -> p j t", j=PACK)
         nc.sync.dma_start(dv_raw[0][:], dv_rows[:, : 2 * R])
-        nc.sync.dma_start(pw_raw[:], pw.rearrange("(p t) i -> p t i", t=PACK))
+        for h in range(2):
+            nc.sync.dma_start(pw_raw[h][:], pw_rows[:, :, half(h)])
         nc.sync.dma_start(offsets[:], offs)
         nc.sync.dma_start(dv_raw[1][:], dv_rows[:, 2 * R :])
         for j in range(PACK):
@@ -56,115 +63,138 @@ def tile_attend_gsoftc_kernel(tc, cT, dvT, pm, pw, offs, out_0, out_1):
 
         ident = tile([P, P], F32, "ident")
         make_identity(nc, ident[:])
-        windows = [tile([P, T], F32, "window%d" % w) for w in range(2)]
+        windows = [tile([P, T], F32, "window%d" % w) for w in range(3)]
         for window in windows:
             nc.vector.memset(window[:].bitcast(I32), 0)
 
-        def quantize(name, woven, fmt):
-            width = woven.shape[1] // PACK
-            codes = tile([P, width], U32, name + "_codes")
-            scales = tile([P, width], U8, name + "_scales")
-            nc.vector.quantize_mx(out=codes[:].bitcast(fmt), scales=scales[:], in_=woven)
-            return codes, scales
+        def mx_tiles(name, width):
+            return tile([P, width], U32, name + "_codes"), tile([P, width], U8, name + "_scales")
 
-        def quantize_dv(name, woven):
-            codes, scales = quantize(name, woven, E5M2)
-            return [(codes[:, c : c + P], scales[:, c : c + P]) for c in range(0, codes.shape[1], P)]
+        def quantize(mx, cols, woven, fmt):
+            nc.vector.quantize_mx(out=mx[0][:, cols].bitcast(fmt), scales=mx[1][:, cols], in_=woven)
 
-        def product(bank, stationary, moving):
-            nc.tensor.matmul_mx(out=bank, lhsT=stationary[0].bitcast(E5M2), lhsT_scale=stationary[1],
-                                rhs=moving[0][:].bitcast(E4M3), rhs_scale=moving[1][:], start=True, stop=True)
+        def product(out, dv_mx, block, mx, cols):
+            rows = slice(block * P, (block + 1) * P)
+            nc.tensor.matmul_mx(out=out, lhsT=dv_mx[0][:, rows].bitcast(E5M2), lhsT_scale=dv_mx[1][:, rows],
+                                rhs=mx[0][:, cols].bitcast(E4M3), rhs_scale=mx[1][:, cols], start=True, stop=True)
 
-        staging = tile([P, (PACK + 2) * R], BF16, "staging")
-        rounded = staging[:, : PACK * R]
-        turned1 = staging[:, 7 * R // 2 : 9 * R // 2]
-        pw_woven = [staging[:, 2 * R : 4 * R], staging[:, 4 * R :]]
+        rounded = tile([P, PACK * R], BF16, "rounded")
+        pw_woven = [tile([P, PACK * HALF], BF16, "pw_woven0")[:], rounded[:, 2 * R :]]
 
         def round_dv(first, planes, raw, copy):
             copy(rounded[:, first * R : (first + planes) * R].rearrange("p (j w q e) -> p j w q e", j=planes, w=2, e=2),
                  raw.rearrange("p (j q w e) -> p j w q e", j=planes, w=2, e=2))
 
-        def turn(first, planes, copy, woven):
-            bank = psum.tile([P, planes, 2, P], F32, name="turned%d" % first, tag="bank%d" % first)
+        def transpose_words(first, planes, nr):
+            turned = bank([P, planes, 2, P], "turned_bank%d" % first, nr)
             words = rounded[:, first * R : (first + planes) * R].bitcast(F32)
             for j in range(planes):
                 for w in range(2):
                     start = (2 * j + w) * P
-                    nc.tensor.transpose(bank[:, j, w, :], words[:, start : start + P], ident[:])
-            copy(woven.bitcast(F32).rearrange("q (j p w) -> q j p w", j=planes, w=2), bank[:].rearrange("q j w p -> q j p w"))
-            return quantize_dv("dvr%d" % first, woven)
+                    nc.tensor.transpose(turned[:, j, w, :], words[:, start : start + P], ident[:])
+            return turned
 
-        def quantize_dvd(h, woven):
-            nc.vector.tensor_copy(woven.rearrange("p (e q j) -> p q j e", e=2, j=PACK),
-                                  rounded.rearrange("p (j w q e) -> p w q j e", j=PACK, w=2, e=2)[:, h, :, :, :])
-            return quantize_dv("dvd%d" % h, woven)
-
-        def quantize_pw(h, copy):
-            copy(*weave_views(pw_woven[h].rearrange("p (c t) -> p c t", t=PACK), pw_raw[:, :, h * HALF : (h + 1) * HALF]))
-            return quantize("pw%d" % h, pw_woven[h], E4M3)
+        def weave_turned(woven, turned, copy):
+            copy(woven.bitcast(F32).rearrange("q (j p w) -> q j p w", p=P, w=2), turned[:].rearrange("q j w p -> q j p w"))
+            return woven
 
         out1_rows = out_1.rearrange("(p j) t -> p j t", j=PACK)
-
-        def products_dc(planes, h, copy, bank_nr, tag=None):
-            bank = psum.tile([P, len(planes), HALF], F32, name="dc_bank%d%d" % (planes[0], h), tag="bank%d" % bank_nr)
-            for e, j in enumerate(planes):
-                product(bank[:, e, :], dvr[j], pw_mx[h])
-            dc = tile([P, len(planes), HALF], F32, "dc%d%d" % (planes[0], h), tag)
-            copy(dc[:], bank[:])
-            return {j: dc[:, e, :] for e, j in enumerate(planes)}
 
         def scalar_move(out, in_):
             nc.scalar.activation(out, in_, COPY)
 
-        def scatter_half(j, h, dc, move=scalar_move):
-            move(windows[j][:].indirect(offsets[:, h * HALF // 16 : (h + 1) * HALF // 16]), dc[j])
+        def scatter(j, h, dc, move=scalar_move):
+            move(windows[j][:].indirect(offsets[:, h * HALF // 16 : (h + 1) * HALF // 16]), dc)
             if h == 1:
                 nc.sync.dma_start(out1_rows[:, j, :], windows[j][:])
 
-        dvr = []
-        for j, woven in enumerate((tile([P, R], BF16, "turned0")[:], turned1)):
-            round_dv(j, 1, dv_raw[0][:, j * R : (j + 1) * R], nc.scalar.copy)
-            dvr.extend(turn(j, 1, nc.scalar.copy, woven))
-        pw_mx = [quantize_pw(0, nc.vector.tensor_copy), quantize_pw(1, nc.scalar.copy)]
-        for j in range(2):
-            scatter_half(j, 0, products_dc([j], 0, nc.scalar.copy, 3 + j))
-        scatter_half(0, 1, products_dc([0], 1, nc.vector.tensor_copy, 5))
-        round_dv(2, 1, dv_raw[1][:, :R], nc.scalar.copy)
-        round_dv(3, 1, dv_raw[1][:, R:], nc.vector.tensor_copy)
-        gathered = tile([P, (PACK + 1) * SLOTS], BF16, "gathered")
-        picked = gathered[:, SLOTS:].rearrange("p (j i) -> p j i", j=PACK)
-        dvr.extend(turn(2, 2, nc.vector.tensor_copy, gathered[:, 5 * SLOTS // 2 : 9 * SLOTS // 2]))
-        dvd = quantize_dvd(0, gathered[:, : 2 * SLOTS])
-        dc23 = [products_dc([2, 3], h, nc.scalar.copy, 6 + h) for h in range(2)]
-        for name, tag in (("window2", "dvr2_codes"), ("window3", "dvr2_scales")):
-            windows.append(tile([P, T], F32, name, tag))
-            nc.gpsimd.memset(windows[-1][:].bitcast(I32), 0)
+        def copied(name, src, copy):
+            dc = tile(list(src.shape), F32, name)
+            copy(dc[:], src)
+            return dc
 
-        for j in range(PACK):
-            nc.vector.tensor_copy(picked[:, j, :], c_raw[j][:].indirect(offsets[:]))
-            if j == 0:
-                scatter_half(1, 1, products_dc([1], 1, nc.vector.tensor_copy, 0, "c_raw0"), nc.vector.tensor_copy)
-        for j in (2, 3):
-            for h in range(2):
-                scatter_half(j, h, dc23[h])
-        c_woven = tile([P, SLOTS * PACK], BF16, "c_woven")
-        nc.vector.tensor_copy(*weave_views(c_woven[:].rearrange("p (c t) -> p c t", t=PACK), picked))
-        c_mx = quantize("c", c_woven[:], E4M3)
-        dvd.extend(quantize_dvd(1, tile([P, 2 * R], BF16, "dvd_woven1", "c_raw2")[:]))
+        for j in range(2):
+            round_dv(j, 1, dv_raw[0][:, j * R : (j + 1) * R], nc.scalar.copy)
+        turned = [weave_turned(rounded[:, (2 + j) * R : (3 + j) * R], transpose_words(j, 1, j), nc.scalar.copy) for j in range(2)]
+        dvr = [mx_tiles("dvr0", P), mx_tiles("dvr1", P), mx_tiles("dvr23", 2 * P)]
+        pw_mx = mx_tiles("pw", SLOTS)
+        nc.vector.tensor_copy(*weave_views(pw_woven[0], pw_raw[0][:]))
+        quantize(dvr[0], slice(0, P), turned[0], E5M2)
+        quantize(pw_mx, half(0), pw_woven[0], E4M3)
+        quantize(dvr[1], slice(0, P), turned[1], E5M2)
+        first = []
+        for j in range(2):
+            b = bank([P, HALF], "dc_bank%d0" % j, 3 + j)
+            product(b[:], dvr[j], 0, pw_mx, half(0))
+            first.append(copied("dc%d0" % j, b[:], nc.scalar.copy))
+        for j in range(2):
+            scatter(j, 0, first[j][:])
+        nc.vector.tensor_copy(*weave_views(pw_woven[1], pw_raw[1][:]))
+        quantize(pw_mx, half(1), pw_woven[1], E4M3)
+        b = bank([P, 2, HALF], "dc_bank01", 5)
+        for j in range(2):
+            product(b[:, j, :], dvr[j], 0, pw_mx, half(1))
+        second = copied("dc01", b[:], nc.scalar.copy)
+        for j in range(2):
+            scatter(j, 1, second[:, j, :])
+
+        dvd = mx_tiles("dvd", R)
+
+        def weave_dvd(w, woven):
+            nc.vector.tensor_copy(woven.rearrange("p (e q j) -> p q j e", e=2, j=PACK),
+                                  rounded[:].rearrange("p (j w q e) -> p w q j e", j=PACK, w=2, e=2)[:, w, :, :, :])
+            return woven
+
+        round_dv(2, 2, dv_raw[1][:], nc.vector.tensor_copy)
+        turned_bank = transpose_words(2, 2, 2)
+        dvd_woven = weave_dvd(0, tile([P, 2 * R], BF16, "dvd_woven")[:])
+        turned23 = weave_turned(tile([P, 2 * R], BF16, "turned2")[:], turned_bank, nc.vector.tensor_copy)
+        quantize(dvr[2], slice(0, 2 * P), turned23, E5M2)
+        quantize(dvd, slice(0, 2 * P), dvd_woven, E5M2)
+        banks = [bank([P, HALF], "dc_bank20", 6), bank([P, SLOTS], "dc_bank3", 7), bank([P, HALF], "dc_bank21", 0)]
+        product(banks[0][:], dvr[2], 0, pw_mx, half(0))
+        product(banks[1][:], dvr[2], 1, pw_mx, slice(0, SLOTS))
+        product(banks[2][:], dvr[2], 0, pw_mx, half(1))
+        windows.append(tile([P, T], F32, "window3", "dvd_woven"))
+        nc.gpsimd.memset(windows[3][:].bitcast(I32), 0)
+
+        gathered = tile([P, PACK * SLOTS], BF16, "gathered", "turned2")
+        picked = gathered[:].rearrange("p (j i) -> p j i", j=PACK)
+        dc20 = gathered[:, 11 * SLOTS // 4 : 15 * SLOTS // 4].bitcast(F32)
+        nc.vector.tensor_copy(picked[:, 0, :], c_raw[0][:].indirect(offsets[:]))
+        nc.vector.tensor_copy(dc20, banks[0][:])
+        nc.vector.tensor_copy(picked[:, 1, :], c_raw[1][:].indirect(offsets[:]))
+        scatter(2, 0, dc20, nc.vector.tensor_copy)
+        dc3 = copied("dc3", banks[1][:], nc.scalar.copy)
+        dc21 = copied("dc21", banks[2][:], nc.scalar.copy)
+        scatter(3, 0, dc3[:, half(0)])
+        scatter(2, 1, dc21[:])
+        scatter(3, 1, dc3[:, half(1)])
+        nc.vector.tensor_copy(picked[:, 2, :], c_raw[2][:].indirect(offsets[:]))
+        for h in range(2):
+            nc.vector.tensor_copy(picked[:, 3, half(h)], c_raw[3][:].indirect(offsets[:, h * HALF // 16 : (h + 1) * HALF // 16]))
+        c_woven = tile([P, 2, PACK * HALF], BF16, "c_woven")
+        c_mx = mx_tiles("c", SLOTS)
+        for h in range(2):
+            nc.vector.tensor_copy(*weave_views(c_woven[:, h, :], picked[:, :, half(h)]))
+        for h in range(2):
+            quantize(c_mx, half(h), c_woven[:, h, :], E4M3)
+        quantize(dvd, slice(2 * P, R), weave_dvd(1, c_woven[:, 0, :]), E5M2)
 
         out0_rows = out_0.rearrange("(q t) i -> q t i", t=PACK)
-        dp = [psum.tile([P, SLOTS], F32, name="dp%d" % t, tag="bank%d" % t) for t in range(PACK)]
+        dp = [bank([P, SLOTS], "dp%d" % t, 1 + t) for t in range(PACK)]
+        for t in range(PACK):
+            for h in range(2):
+                product(dp[t][:, half(h)], dvd, t, c_mx, half(h))
         weighted = [tile([P, SLOTS], F32, "weighted%d" % t) for t in range(PACK)]
         minus_s = [tile([P, 1], F32, "minus_s%d" % t) for t in range(PACK)]
         result = [tile([P, SLOTS], F32, "result%d" % t) for t in range(PACK)]
         for t in range(PACK):
-            product(dp[t][:], dvd[t], c_mx)
             nc.vector.scalar_tensor_tensor(weighted[t][:], dp[t][:], -1.0, pm_sb[:, t, :], MULT, MULT, accum_out=minus_s[t][:])
-            split = GPSIMD_COLUMNS[t]
-            if split:
-                centred = tile([P, split], F32, "centred%d" % t)
-                nc.scalar.activation(centred[:], dp[t][:, :split], IDENTITY, bias=minus_s[t][:])
-                nc.gpsimd.tensor_tensor(result[t][:, :split], centred[:], pm_sb[:, t, :split], MULT)
-            if split < SLOTS:
-                nc.vector.scalar_tensor_tensor(result[t][:, split:], dp[t][:, split:], minus_s[t][:], pm_sb[:, t, split:], ADD, MULT)
+            if t == 0:
+                centred = tile([P, SLOTS], F32, "centred")
+                nc.scalar.activation(centred[:], dp[t][:], IDENTITY, bias=minus_s[t][:])
+                nc.gpsimd.tensor_tensor(result[t][:], centred[:], pm_sb[:, t, :], MULT)
+            else:
+                nc.vector.scalar_tensor_tensor(result[t][:], dp[t][:], minus_s[t][:], pm_sb[:, t, :], ADD, MULT)
             nc.sync.dma_start(out0_rows[:, t, :], result[t][:])

@@ -79,7 +79,8 @@ def tile_attend_gsoftc_kernel(tc, cT, dvT, pm, pw, offs, out_0, out_1):
                                 rhs=mx[0][:, cols].bitcast(E4M3), rhs_scale=mx[1][:, cols], start=True, stop=True)
 
         rounded = tile([P, PACK * R], BF16, "rounded")
-        pw_woven = [tile([P, PACK * HALF], BF16, "pw_woven0")[:], rounded[:, 2 * R :]]
+        pw_woven = [tile([P, PACK * HALF], BF16, "pw_woven%d" % h)[:] for h in range(2)]
+        turned_places = (pw_woven[1][:, :R], rounded[:, 3 * R :])
 
         def round_dv(first, planes, raw, copy):
             copy(rounded[:, first * R : (first + planes) * R].rearrange("p (j w q e) -> p j w q e", j=planes, w=2, e=2),
@@ -115,21 +116,22 @@ def tile_attend_gsoftc_kernel(tc, cT, dvT, pm, pw, offs, out_0, out_1):
 
         for j in range(2):
             round_dv(j, 1, dv_raw[0][:, j * R : (j + 1) * R], nc.scalar.copy)
-        turned = [weave_turned(rounded[:, (2 + j) * R : (3 + j) * R], transpose_words(j, 1, j), nc.scalar.copy) for j in range(2)]
+        turned = [weave_turned(turned_places[j], transpose_words(j, 1, j), nc.scalar.copy) for j in range(2)]
         dvr = [mx_tiles("dvr0", P), mx_tiles("dvr1", P), mx_tiles("dvr23", 2 * P)]
         pw_mx = mx_tiles("pw", SLOTS)
         nc.vector.tensor_copy(*weave_views(pw_woven[0], pw_raw[0][:]))
         quantize(dvr[0], slice(0, P), turned[0], E5M2)
         quantize(pw_mx, half(0), pw_woven[0], E4M3)
-        quantize(dvr[1], slice(0, P), turned[1], E5M2)
-        first = []
-        for j in range(2):
+
+        def first_half(j):
             b = bank([P, HALF], "dc_bank%d0" % j, 3 + j)
             product(b[:], dvr[j], 0, pw_mx, half(0))
-            first.append(copied("dc%d0" % j, b[:], nc.scalar.copy))
-        for j in range(2):
-            scatter(j, 0, first[j][:])
+            scatter(j, 0, copied("dc%d0" % j, b[:], nc.scalar.copy)[:])
+
+        first_half(0)
         nc.vector.tensor_copy(*weave_views(pw_woven[1], pw_raw[1][:]))
+        quantize(dvr[1], slice(0, P), turned[1], E5M2)
+        first_half(1)
         quantize(pw_mx, half(1), pw_woven[1], E4M3)
         b = bank([P, 2, HALF], "dc_bank01", 5)
         for j in range(2):
@@ -149,16 +151,16 @@ def tile_attend_gsoftc_kernel(tc, cT, dvT, pm, pw, offs, out_0, out_1):
         turned_bank = transpose_words(2, 2, 2)
         dvd_woven = weave_dvd(0, tile([P, 2 * R], BF16, "dvd_woven")[:])
         turned23 = weave_turned(tile([P, 2 * R], BF16, "turned2")[:], turned_bank, nc.vector.tensor_copy)
-        quantize(dvr[2], slice(0, 2 * P), turned23, E5M2)
         quantize(dvd, slice(0, 2 * P), dvd_woven, E5M2)
+        quantize(dvr[2], slice(0, 2 * P), turned23, E5M2)
         banks = [bank([P, HALF], "dc_bank20", 6), bank([P, SLOTS], "dc_bank3", 7), bank([P, HALF], "dc_bank21", 0)]
         product(banks[0][:], dvr[2], 0, pw_mx, half(0))
         product(banks[1][:], dvr[2], 1, pw_mx, slice(0, SLOTS))
         product(banks[2][:], dvr[2], 0, pw_mx, half(1))
-        windows.append(tile([P, T], F32, "window3", "dvd_woven"))
+        windows.append(tile([P, T], F32, "window3", "turned2"))
         nc.gpsimd.memset(windows[3][:].bitcast(I32), 0)
 
-        gathered = tile([P, PACK * SLOTS], BF16, "gathered", "turned2")
+        gathered = tile([P, PACK * SLOTS], BF16, "gathered", "dvd_woven")
         picked = gathered[:].rearrange("p (j i) -> p j i", j=PACK)
         dc20 = gathered[:, 11 * SLOTS // 4 : 15 * SLOTS // 4].bitcast(F32)
         nc.vector.tensor_copy(picked[:, 0, :], c_raw[0][:].indirect(offsets[:]))

@@ -46,7 +46,7 @@ def tile_attend_gsoftc_kernel(tc, cT, dvT, pm, pw, offs, out_0, out_1):
         offsets = sb.tile([P, SLOTS // 16], U16, name="offsets")
         pw_raw = [tile([P, PACK, HALF], F32, "pw_raw%d" % h) for h in range(2)]
         dv_raw = [tile([P, 2 * R], F32, "dv_raw%d" % u) for u in range(2)]
-        c_raw = [tile([P, T], F32, "c_raw%d" % j) for j in range(PACK)]
+        c_raw = [tile([P, 2, T], F32, "c_raw%d" % u) for u in range(2)]
         pm_sb = tile([P, PACK, SLOTS], F32, "pm_sb")
 
         dv_rows = dvT.rearrange("(p j) r -> p (j r)", j=PACK)
@@ -57,8 +57,8 @@ def tile_attend_gsoftc_kernel(tc, cT, dvT, pm, pw, offs, out_0, out_1):
             nc.sync.dma_start(pw_raw[h][:], pw_rows[:, :, half(h)])
         nc.sync.dma_start(offsets[:], offs)
         nc.sync.dma_start(dv_raw[1][:], dv_rows[:, 2 * R :])
-        for j in range(PACK):
-            nc.sync.dma_start(c_raw[j][:], c_rows[:, j, :])
+        for u in range(2):
+            nc.sync.dma_start(c_raw[u][:], c_rows[:, 2 * u : 2 * u + 2, :])
         nc.sync.dma_start(pm_sb[:], pm.rearrange("(q t) i -> q t i", t=PACK))
 
         ident = tile([P, P], F32, "ident")
@@ -104,13 +104,13 @@ def tile_attend_gsoftc_kernel(tc, cT, dvT, pm, pw, offs, out_0, out_1):
         def scalar_move(out, in_):
             nc.scalar.activation(out, in_, COPY)
 
-        def scatter(j, h, dc, move=scalar_move):
-            move(windows[j][:].indirect(offsets[:, h * HALF // 16 : (h + 1) * HALF // 16]), dc)
+        def scatter(j, h, dc):
+            scalar_move(windows[j][:].indirect(offsets[:, h * HALF // 16 : (h + 1) * HALF // 16]), dc)
             if h == 1:
                 nc.sync.dma_start(out1_rows[:, j, :], windows[j][:])
 
-        def copied(name, src, copy):
-            dc = tile(list(src.shape), F32, name)
+        def copied(name, src, copy, tag=None):
+            dc = tile(list(src.shape), F32, name, tag)
             copy(dc[:], src)
             return dc
 
@@ -136,7 +136,7 @@ def tile_attend_gsoftc_kernel(tc, cT, dvT, pm, pw, offs, out_0, out_1):
         b = bank([P, 2, HALF], "dc_bank01", 5)
         for j in range(2):
             product(b[:, j, :], dvr[j], 0, pw_mx, half(1))
-        second = copied("dc01", b[:], nc.scalar.copy)
+        second = copied("dc01", b[:], nc.vector.tensor_copy)
         for j in range(2):
             scatter(j, 1, second[:, j, :])
 
@@ -153,50 +153,52 @@ def tile_attend_gsoftc_kernel(tc, cT, dvT, pm, pw, offs, out_0, out_1):
         turned23 = weave_turned(tile([P, 2 * R], BF16, "turned2")[:], turned_bank, nc.vector.tensor_copy)
         quantize(dvd, slice(0, 2 * P), dvd_woven, E5M2)
         quantize(dvr[2], slice(0, 2 * P), turned23, E5M2)
-        banks = [bank([P, HALF], "dc_bank20", 6), bank([P, SLOTS], "dc_bank3", 7), bank([P, HALF], "dc_bank21", 0)]
-        product(banks[0][:], dvr[2], 0, pw_mx, half(0))
-        product(banks[1][:], dvr[2], 1, pw_mx, slice(0, SLOTS))
-        product(banks[2][:], dvr[2], 0, pw_mx, half(1))
+        banks = [bank([P, SLOTS], "dc_bank%d" % (2 + j), 6 + j) for j in range(2)]
+        for j in range(2):
+            product(banks[j][:], dvr[2], j, pw_mx, slice(0, SLOTS))
+        dvd_woven = weave_dvd(1, tile([P, 2 * R], BF16, "dvd_woven1", "turned2")[:])
+
+        gathered = tile([P, PACK * SLOTS], F32, "gathered", "dvd_woven")
+        picked = gathered[:].rearrange("p (j i) -> p j i", j=PACK)
+        dc2 = gathered[:, 11 * SLOTS // 4 : 15 * SLOTS // 4]
+        nc.vector.tensor_copy(dc2, banks[0][:])
+        quantize(dvd, slice(2 * P, R), dvd_woven, E5M2)
         windows.append(tile([P, T], F32, "window3", "turned2"))
         nc.gpsimd.memset(windows[3][:].bitcast(I32), 0)
-
-        gathered = tile([P, PACK * SLOTS], BF16, "gathered", "dvd_woven")
-        picked = gathered[:].rearrange("p (j i) -> p j i", j=PACK)
-        dc20 = gathered[:, 11 * SLOTS // 4 : 15 * SLOTS // 4].bitcast(F32)
-        nc.vector.tensor_copy(picked[:, 0, :], c_raw[0][:].indirect(offsets[:]))
-        nc.vector.tensor_copy(dc20, banks[0][:])
-        nc.vector.tensor_copy(picked[:, 1, :], c_raw[1][:].indirect(offsets[:]))
-        scatter(2, 0, dc20, nc.vector.tensor_copy)
-        dc3 = copied("dc3", banks[1][:], nc.scalar.copy)
-        dc21 = copied("dc21", banks[2][:], nc.scalar.copy)
-        scatter(3, 0, dc3[:, half(0)])
-        scatter(2, 1, dc21[:])
-        scatter(3, 1, dc3[:, half(1)])
-        nc.vector.tensor_copy(picked[:, 2, :], c_raw[2][:].indirect(offsets[:]))
+        nc.vector.tensor_copy(windows[2][:].indirect(offsets[:]), dc2)
+        nc.sync.dma_start(out1_rows[:, 2, :], windows[2][:])
+        for j in range(2):
+            scalar_move(picked[:, j, :], c_raw[0][:, j, :].indirect(offsets[:]))
+        nc.vector.tensor_copy(picked[:, 2, :], c_raw[1][:, 0, :].indirect(offsets[:]))
+        dc3 = copied("dc3", banks[1][:], nc.scalar.copy, "c_raw0")
         for h in range(2):
-            nc.vector.tensor_copy(picked[:, 3, half(h)], c_raw[3][:].indirect(offsets[:, h * HALF // 16 : (h + 1) * HALF // 16]))
+            scatter(3, h, dc3[:, half(h)])
+        for h in range(2):
+            nc.vector.tensor_copy(picked[:, 3, half(h)], c_raw[1][:, 1, :].indirect(offsets[:, h * HALF // 16 : (h + 1) * HALF // 16]))
         c_woven = tile([P, 2, PACK * HALF], BF16, "c_woven")
         c_mx = mx_tiles("c", SLOTS)
         for h in range(2):
             nc.vector.tensor_copy(*weave_views(c_woven[:, h, :], picked[:, :, half(h)]))
         for h in range(2):
             quantize(c_mx, half(h), c_woven[:, h, :], E4M3)
-        quantize(dvd, slice(2 * P, R), weave_dvd(1, c_woven[:, 0, :]), E5M2)
 
         out0_rows = out_0.rearrange("(q t) i -> q t i", t=PACK)
         dp = [bank([P, SLOTS], "dp%d" % t, 1 + t) for t in range(PACK)]
-        for t in range(PACK):
-            for h in range(2):
-                product(dp[t][:, half(h)], dvd, t, c_mx, half(h))
+        for h in range(2):
+            product(dp[0][:, half(h)], dvd, 0, c_mx, half(h))
+        for t in range(1, PACK):
+            product(dp[t][:], dvd, t, c_mx, slice(0, SLOTS))
         weighted = [tile([P, SLOTS], F32, "weighted%d" % t) for t in range(PACK)]
         minus_s = [tile([P, 1], F32, "minus_s%d" % t) for t in range(PACK)]
-        result = [tile([P, SLOTS], F32, "result%d" % t) for t in range(PACK)]
+        pairs = [tile([P, 2, SLOTS], F32, "result%d" % u) for u in range(2)]
+        result = [pairs[t // 2][:, t % 2, :] for t in range(PACK)]
         for t in range(PACK):
             nc.vector.scalar_tensor_tensor(weighted[t][:], dp[t][:], -1.0, pm_sb[:, t, :], MULT, MULT, accum_out=minus_s[t][:])
             if t == 0:
                 centred = tile([P, SLOTS], F32, "centred")
                 nc.scalar.activation(centred[:], dp[t][:], IDENTITY, bias=minus_s[t][:])
-                nc.gpsimd.tensor_tensor(result[t][:], centred[:], pm_sb[:, t, :], MULT)
+                nc.gpsimd.tensor_tensor(result[t], centred[:], pm_sb[:, t, :], MULT)
             else:
-                nc.vector.scalar_tensor_tensor(result[t][:], dp[t][:], minus_s[t][:], pm_sb[:, t, :], ADD, MULT)
-            nc.sync.dma_start(out0_rows[:, t, :], result[t][:])
+                nc.vector.scalar_tensor_tensor(result[t], dp[t][:], minus_s[t][:], pm_sb[:, t, :], ADD, MULT)
+            if t % 2:
+                nc.sync.dma_start(out0_rows[:, t - 1 : t + 1, :], pairs[t // 2][:])

@@ -22,6 +22,7 @@ IDENTITY = mybir.ActivationFunctionType.Identity
 P = 128
 PACK = 4
 HALF = SLOTS // 2
+ALIGN = 256
 
 
 def weave_views(dst, src):
@@ -35,7 +36,7 @@ def tile_attend_gsoftc_kernel(tc, cT, dvT, pm, pw, offs, out_0, out_1):
         psum = ctx.enter_context(tc.psum_pool(name="psum", bufs=1))
 
         def tile(shape, dtype, name, tag=None):
-            return sb.tile(shape, dtype, name=name, tag=tag or name, align_bytes=64)
+            return sb.tile(shape, dtype, name=name, tag=tag or name, align_bytes=ALIGN)
 
         def bank(shape, name, nr):
             return psum.tile(shape, F32, name=name, tag="bank%d" % nr)

@@ -65,8 +65,12 @@ def tile_attend_gsoftc_kernel(tc, cT, dvT, pm, pw, offs, out_0, out_1):
         ident = tile([P, P], F32, "ident")
         make_identity(nc, ident[:])
         windows = [tile([P, T], F32, "window%d" % w) for w in range(3)]
-        for window in windows:
-            nc.vector.memset(window[:].bitcast(I32), 0)
+        for words in (windows[0][:].bitcast(I32), windows[2][:, : T // 2].bitcast(I32)):
+            cut = words.shape[1] // 2 - 1
+            nc.vector.memset(words[:, :cut], 0)
+            nc.vector.memset(words[:, cut:], 0)
+        for words in (windows[1][:].bitcast(I32), windows[2][:, T // 2 :].bitcast(I32)):
+            nc.gpsimd.memset(words, 0)
 
         def mx_tiles(name, width):
             return tile([P, width], U32, name + "_codes"), tile([P, width], U8, name + "_scales")
@@ -141,7 +145,7 @@ def tile_attend_gsoftc_kernel(tc, cT, dvT, pm, pw, offs, out_0, out_1):
         for j in range(2):
             scatter(j, 1, second[:, j, :])
 
-        dvd = mx_tiles("dvd", R)
+        dvd = [mx_tiles("dvd0", 2 * P)]
 
         def weave_dvd(w, woven):
             nc.vector.tensor_copy(woven.rearrange("p (e q j) -> p q j e", e=2, j=PACK),
@@ -152,7 +156,7 @@ def tile_attend_gsoftc_kernel(tc, cT, dvT, pm, pw, offs, out_0, out_1):
         turned_bank = transpose_words(2, 2, 2)
         dvd_woven = weave_dvd(0, tile([P, 2 * R], BF16, "dvd_woven")[:])
         turned23 = weave_turned(tile([P, 2 * R], BF16, "turned2")[:], turned_bank, nc.vector.tensor_copy)
-        quantize(dvd, slice(0, 2 * P), dvd_woven, E5M2)
+        quantize(dvd[0], slice(0, 2 * P), dvd_woven, E5M2)
         quantize(dvr[2], slice(0, 2 * P), turned23, E5M2)
         banks = [bank([P, SLOTS], "dc_bank%d" % (2 + j), 6 + j) for j in range(2)]
         for j in range(2):
@@ -163,43 +167,43 @@ def tile_attend_gsoftc_kernel(tc, cT, dvT, pm, pw, offs, out_0, out_1):
         picked = gathered[:].rearrange("p (j i) -> p j i", j=PACK)
         dc2 = gathered[:, 11 * SLOTS // 4 : 15 * SLOTS // 4]
         nc.vector.tensor_copy(dc2, banks[0][:])
-        quantize(dvd, slice(2 * P, R), dvd_woven, E5M2)
-        windows.append(tile([P, T], F32, "window3", "turned2"))
+        windows.append(tile([P, T], F32, "window3", "rounded"))
         nc.gpsimd.memset(windows[3][:].bitcast(I32), 0)
         nc.vector.tensor_copy(windows[2][:].indirect(offsets[:]), dc2)
         nc.sync.dma_start(out1_rows[:, 2, :], windows[2][:])
         for j in range(2):
             scalar_move(picked[:, j, :], c_raw[0][:, j, :].indirect(offsets[:]))
         nc.vector.tensor_copy(picked[:, 2, :], c_raw[1][:, 0, :].indirect(offsets[:]))
-        dc3 = copied("dc3", banks[1][:], nc.scalar.copy, "c_raw0")
+        for h, move in enumerate((scalar_move, nc.vector.tensor_copy)):
+            move(picked[:, 3, half(h)], c_raw[1][:, 1, :].indirect(offsets[:, h * HALF // 16 : (h + 1) * HALF // 16]))
+        dc3 = copied("dc3", banks[1][:], nc.scalar.copy, "c_raw1")
         for h in range(2):
             scatter(3, h, dc3[:, half(h)])
-        for h in range(2):
-            nc.vector.tensor_copy(picked[:, 3, half(h)], c_raw[1][:, 1, :].indirect(offsets[:, h * HALF // 16 : (h + 1) * HALF // 16]))
-        c_woven = tile([P, 2, PACK * HALF], BF16, "c_woven")
+        c_woven = [tile([P, PACK * HALF], BF16, "c_woven%d" % h)[:] for h in range(2)]
         c_mx = mx_tiles("c", SLOTS)
         for h in range(2):
-            nc.vector.tensor_copy(*weave_views(c_woven[:, h, :], picked[:, :, half(h)]))
+            nc.vector.tensor_copy(*weave_views(c_woven[h], picked[:, :, half(h)]))
         for h in range(2):
-            quantize(c_mx, half(h), c_woven[:, h, :], E4M3)
+            quantize(c_mx, half(h), c_woven[h], E4M3)
+        dvd.append((tile([P, 2 * P], U32, "dvd1_codes", "c_woven0"), tile([P, 2 * P], U8, "dvd1_scales")))
+        quantize(dvd[1], slice(0, 2 * P), dvd_woven, E5M2)
 
         out0_rows = out_0.rearrange("(q t) i -> q t i", t=PACK)
         dp = [bank([P, SLOTS], "dp%d" % t, 1 + t) for t in range(PACK)]
         for h in range(2):
-            product(dp[0][:, half(h)], dvd, 0, c_mx, half(h))
+            product(dp[0][:, half(h)], dvd[0], 0, c_mx, half(h))
         for t in range(1, PACK):
-            product(dp[t][:], dvd, t, c_mx, slice(0, SLOTS))
+            product(dp[t][:], dvd[t // 2], t % 2, c_mx, slice(0, SLOTS))
         weighted = [tile([P, SLOTS], F32, "weighted%d" % t) for t in range(PACK)]
         minus_s = [tile([P, 1], F32, "minus_s%d" % t) for t in range(PACK)]
         pairs = [tile([P, 2, SLOTS], F32, "result%d" % u) for u in range(2)]
         result = [pairs[t // 2][:, t % 2, :] for t in range(PACK)]
         for t in range(PACK):
             nc.vector.scalar_tensor_tensor(weighted[t][:], dp[t][:], -1.0, pm_sb[:, t, :], MULT, MULT, accum_out=minus_s[t][:])
-            if t == 0:
-                centred = tile([P, SLOTS], F32, "centred")
-                nc.scalar.activation(centred[:], dp[t][:], IDENTITY, bias=minus_s[t][:])
-                nc.gpsimd.tensor_tensor(result[t], centred[:], pm_sb[:, t, :], MULT)
-            else:
-                nc.vector.scalar_tensor_tensor(result[t], dp[t][:], minus_s[t][:], pm_sb[:, t, :], ADD, MULT)
-            if t % 2:
-                nc.sync.dma_start(out0_rows[:, t - 1 : t + 1, :], pairs[t // 2][:])
+        centred = tile([P, SLOTS], F32, "centred")
+        nc.scalar.activation(centred[:], dp[0][:], IDENTITY, bias=minus_s[0][:])
+        nc.gpsimd.tensor_tensor(result[0], centred[:], pm_sb[:, 0, :], MULT)
+        for t in (2, 3, 1):
+            nc.vector.scalar_tensor_tensor(result[t], dp[t][:], minus_s[t][:], pm_sb[:, t, :], ADD, MULT)
+        for u in (1, 0):
+            nc.sync.dma_start(out0_rows[:, 2 * u : 2 * u + 2, :], pairs[u][:])

@@ -65,12 +65,8 @@ def tile_attend_gsoftc_kernel(tc, cT, dvT, pm, pw, offs, out_0, out_1):
         ident = tile([P, P], F32, "ident")
         make_identity(nc, ident[:])
         windows = [tile([P, T], F32, "window%d" % w) for w in range(3)]
-        for words in (windows[0][:].bitcast(I32), windows[2][:, : T // 2].bitcast(I32)):
-            cut = words.shape[1] // 2 - 1
-            nc.vector.memset(words[:, :cut], 0)
-            nc.vector.memset(words[:, cut:], 0)
-        for words in (windows[1][:].bitcast(I32), windows[2][:, T // 2 :].bitcast(I32)):
-            nc.gpsimd.memset(words, 0)
+        for window in windows:
+            nc.vector.memset(window[:].bitcast(I32), 0)
 
         def mx_tiles(name, width):
             return tile([P, width], U32, name + "_codes"), tile([P, width], U8, name + "_scales")
@@ -128,22 +124,21 @@ def tile_attend_gsoftc_kernel(tc, cT, dvT, pm, pw, offs, out_0, out_1):
         quantize(dvr[0], slice(0, P), turned[0], E5M2)
         quantize(pw_mx, half(0), pw_woven[0], E4M3)
 
-        def first_half(j):
-            b = bank([P, HALF], "dc_bank%d0" % j, 3 + j)
-            product(b[:], dvr[j], 0, pw_mx, half(0))
-            scatter(j, 0, copied("dc%d0" % j, b[:], nc.scalar.copy)[:])
-
-        first_half(0)
+        b = bank([P, HALF], "dc_bank00", 3)
+        product(b[:], dvr[0], 0, pw_mx, half(0))
+        scatter(0, 0, copied("dc00", b[:], nc.scalar.copy)[:])
         nc.vector.tensor_copy(*weave_views(pw_woven[1], pw_raw[1][:]))
         quantize(dvr[1], slice(0, P), turned[1], E5M2)
-        first_half(1)
         quantize(pw_mx, half(1), pw_woven[1], E4M3)
-        b = bank([P, 2, HALF], "dc_bank01", 5)
-        for j in range(2):
-            product(b[:, j, :], dvr[j], 0, pw_mx, half(1))
-        second = copied("dc01", b[:], nc.vector.tensor_copy)
-        for j in range(2):
-            scatter(j, 1, second[:, j, :])
+        b = bank([P, SLOTS], "dc_bank1", 4)
+        product(b[:], dvr[1], 0, pw_mx, slice(0, SLOTS))
+        dc1 = copied("dc1", b[:], nc.vector.tensor_copy)
+        b = bank([P, HALF], "dc_bank01", 5)
+        product(b[:], dvr[0], 0, pw_mx, half(1))
+        dc01 = copied("dc01", b[:], nc.vector.tensor_copy)
+        scatter(1, 0, dc1[:, half(0)])
+        scatter(0, 1, dc01[:])
+        scatter(1, 1, dc1[:, half(1)])
 
         dvd = [mx_tiles("dvd0", 2 * P)]
 
@@ -174,11 +169,13 @@ def tile_attend_gsoftc_kernel(tc, cT, dvT, pm, pw, offs, out_0, out_1):
         for j in range(2):
             scalar_move(picked[:, j, :], c_raw[0][:, j, :].indirect(offsets[:]))
         nc.vector.tensor_copy(picked[:, 2, :], c_raw[1][:, 0, :].indirect(offsets[:]))
-        for h, move in enumerate((scalar_move, nc.vector.tensor_copy)):
-            move(picked[:, 3, half(h)], c_raw[1][:, 1, :].indirect(offsets[:, h * HALF // 16 : (h + 1) * HALF // 16]))
-        dc3 = copied("dc3", banks[1][:], nc.scalar.copy, "c_raw1")
+        dc3 = tile([P, SLOTS], F32, "dc3", "c_raw0")
+        for h in range(2):
+            nc.scalar.copy(dc3[:, half(h)], banks[1][:, half(h)])
         for h in range(2):
             scatter(3, h, dc3[:, half(h)])
+        for h in range(2):
+            nc.vector.tensor_copy(picked[:, 3, half(h)], c_raw[1][:, 1, :].indirect(offsets[:, h * HALF // 16 : (h + 1) * HALF // 16]))
         c_woven = [tile([P, PACK * HALF], BF16, "c_woven%d" % h)[:] for h in range(2)]
         c_mx = mx_tiles("c", SLOTS)
         for h in range(2):
@@ -200,10 +197,11 @@ def tile_attend_gsoftc_kernel(tc, cT, dvT, pm, pw, offs, out_0, out_1):
         result = [pairs[t // 2][:, t % 2, :] for t in range(PACK)]
         for t in range(PACK):
             nc.vector.scalar_tensor_tensor(weighted[t][:], dp[t][:], -1.0, pm_sb[:, t, :], MULT, MULT, accum_out=minus_s[t][:])
-        centred = tile([P, SLOTS], F32, "centred")
-        nc.scalar.activation(centred[:], dp[0][:], IDENTITY, bias=minus_s[0][:])
-        nc.gpsimd.tensor_tensor(result[0], centred[:], pm_sb[:, 0, :], MULT)
-        for t in (2, 3, 1):
-            nc.vector.scalar_tensor_tensor(result[t], dp[t][:], minus_s[t][:], pm_sb[:, t, :], ADD, MULT)
-        for u in (1, 0):
-            nc.sync.dma_start(out0_rows[:, 2 * u : 2 * u + 2, :], pairs[u][:])
+            if t == 0:
+                centred = tile([P, SLOTS], F32, "centred")
+                nc.scalar.activation(centred[:], dp[t][:], IDENTITY, bias=minus_s[t][:])
+                nc.gpsimd.tensor_tensor(result[t], centred[:], pm_sb[:, t, :], MULT)
+            else:
+                nc.vector.scalar_tensor_tensor(result[t], dp[t][:], minus_s[t][:], pm_sb[:, t, :], ADD, MULT)
+            if t % 2:
+                nc.sync.dma_start(out0_rows[:, t - 1 : t + 1, :], pairs[t // 2][:])

@@ -22,6 +22,7 @@ IDENTITY = mybir.ActivationFunctionType.Identity
 P = 128
 PACK = 4
 HALF = SLOTS // 2
+ASIDE = 384
 ALIGN = 256
 
 
@@ -65,8 +66,12 @@ def tile_attend_gsoftc_kernel(tc, cT, dvT, pm, pw, offs, out_0, out_1):
         ident = tile([P, P], F32, "ident")
         make_identity(nc, ident[:])
         windows = [tile([P, T], F32, "window%d" % w) for w in range(3)]
-        for window in windows:
-            nc.vector.memset(window[:].bitcast(I32), 0)
+        for words in (windows[0][:].bitcast(I32), windows[2][:, : T // 2].bitcast(I32)):
+            cut = words.shape[1] // 2 - 1
+            nc.vector.memset(words[:, :cut], 0)
+            nc.vector.memset(words[:, cut:], 0)
+        for words in (windows[1][:].bitcast(I32), windows[2][:, T // 2 :].bitcast(I32)):
+            nc.gpsimd.memset(words, 0)
 
         def mx_tiles(name, width):
             return tile([P, width], U32, name + "_codes"), tile([P, width], U8, name + "_scales")
@@ -129,16 +134,16 @@ def tile_attend_gsoftc_kernel(tc, cT, dvT, pm, pw, offs, out_0, out_1):
         scatter(0, 0, copied("dc00", b[:], nc.scalar.copy)[:])
         nc.vector.tensor_copy(*weave_views(pw_woven[1], pw_raw[1][:]))
         quantize(dvr[1], slice(0, P), turned[1], E5M2)
+        b = bank([P, HALF], "dc_bank10", 4)
+        product(b[:], dvr[1], 0, pw_mx, half(0))
+        scatter(1, 0, copied("dc10", b[:], nc.vector.tensor_copy)[:])
         quantize(pw_mx, half(1), pw_woven[1], E4M3)
-        b = bank([P, SLOTS], "dc_bank1", 4)
-        product(b[:], dvr[1], 0, pw_mx, slice(0, SLOTS))
-        dc1 = copied("dc1", b[:], nc.vector.tensor_copy)
-        b = bank([P, HALF], "dc_bank01", 5)
-        product(b[:], dvr[0], 0, pw_mx, half(1))
-        dc01 = copied("dc01", b[:], nc.vector.tensor_copy)
-        scatter(1, 0, dc1[:, half(0)])
-        scatter(0, 1, dc01[:])
-        scatter(1, 1, dc1[:, half(1)])
+        b = bank([P, 2, HALF], "dc_bank01", 5)
+        for j in range(2):
+            product(b[:, j, :], dvr[j], 0, pw_mx, half(1))
+        second = copied("dc01", b[:], nc.vector.tensor_copy)
+        for j in range(2):
+            scatter(j, 1, second[:, j, :])
 
         dvd = [mx_tiles("dvd0", 2 * P)]
 
@@ -195,13 +200,24 @@ def tile_attend_gsoftc_kernel(tc, cT, dvT, pm, pw, offs, out_0, out_1):
         minus_s = [tile([P, 1], F32, "minus_s%d" % t) for t in range(PACK)]
         pairs = [tile([P, 2, SLOTS], F32, "result%d" % u) for u in range(2)]
         result = [pairs[t // 2][:, t % 2, :] for t in range(PACK)]
+        centred = tile([P, 2, SLOTS], F32, "centred")
+
+        def finish_aside(t, cols):
+            nc.scalar.activation(centred[:, t // 2, cols], dp[t][:, cols], IDENTITY, bias=minus_s[t][:])
+            nc.gpsimd.tensor_tensor(result[t][:, cols], centred[:, t // 2, cols], pm_sb[:, t, cols], MULT)
+
+        def finish(t, cols):
+            nc.vector.scalar_tensor_tensor(result[t][:, cols], dp[t][:, cols], minus_s[t][:], pm_sb[:, t, cols], ADD, MULT)
+
         for t in range(PACK):
             nc.vector.scalar_tensor_tensor(weighted[t][:], dp[t][:], -1.0, pm_sb[:, t, :], MULT, MULT, accum_out=minus_s[t][:])
             if t == 0:
-                centred = tile([P, SLOTS], F32, "centred")
-                nc.scalar.activation(centred[:], dp[t][:], IDENTITY, bias=minus_s[t][:])
-                nc.gpsimd.tensor_tensor(result[t], centred[:], pm_sb[:, t, :], MULT)
+                for h in range(2):
+                    finish_aside(t, half(h))
+            elif t == 2:
+                finish_aside(t, slice(0, ASIDE))
+                finish(t, slice(ASIDE, SLOTS))
             else:
-                nc.vector.scalar_tensor_tensor(result[t], dp[t][:], minus_s[t][:], pm_sb[:, t, :], ADD, MULT)
+                finish(t, slice(0, SLOTS))
             if t % 2:
                 nc.sync.dma_start(out0_rows[:, t - 1 : t + 1, :], pairs[t // 2][:])

@@ -22,7 +22,6 @@ IDENTITY = mybir.ActivationFunctionType.Identity
 P = 128
 PACK = 4
 HALF = SLOTS // 2
-ASIDE = 384
 ALIGN = 256
 
 
@@ -48,7 +47,7 @@ def tile_attend_gsoftc_kernel(tc, cT, dvT, pm, pw, offs, out_0, out_1):
         offsets = sb.tile([P, SLOTS // 16], U16, name="offsets")
         pw_raw = [tile([P, PACK, HALF], F32, "pw_raw%d" % h) for h in range(2)]
         dv_raw = [tile([P, 2 * R], F32, "dv_raw%d" % u) for u in range(2)]
-        c_raw = [tile([P, 2, T], F32, "c_raw%d" % u) for u in range(2)]
+        c_raw = [tile([P, planes, T], F32, "c_raw%d" % u) for u, planes in enumerate((2, 1, 1))]
         pm_sb = tile([P, PACK, SLOTS], F32, "pm_sb")
 
         dv_rows = dvT.rearrange("(p j) r -> p (j r)", j=PACK)
@@ -59,8 +58,8 @@ def tile_attend_gsoftc_kernel(tc, cT, dvT, pm, pw, offs, out_0, out_1):
             nc.sync.dma_start(pw_raw[h][:], pw_rows[:, :, half(h)])
         nc.sync.dma_start(offsets[:], offs)
         nc.sync.dma_start(dv_raw[1][:], dv_rows[:, 2 * R :])
-        for u in range(2):
-            nc.sync.dma_start(c_raw[u][:], c_rows[:, 2 * u : 2 * u + 2, :])
+        for raw, planes in zip(c_raw, (slice(0, 2), slice(2, 3), slice(3, 4))):
+            nc.sync.dma_start(raw[:], c_rows[:, planes, :])
         nc.sync.dma_start(pm_sb[:], pm.rearrange("(q t) i -> q t i", t=PACK))
 
         ident = tile([P, P], F32, "ident")
@@ -173,14 +172,15 @@ def tile_attend_gsoftc_kernel(tc, cT, dvT, pm, pw, offs, out_0, out_1):
         nc.sync.dma_start(out1_rows[:, 2, :], windows[2][:])
         for j in range(2):
             scalar_move(picked[:, j, :], c_raw[0][:, j, :].indirect(offsets[:]))
-        nc.vector.tensor_copy(picked[:, 2, :], c_raw[1][:, 0, :].indirect(offsets[:]))
-        dc3 = tile([P, SLOTS], F32, "dc3", "c_raw0")
+        for h, move in enumerate((scalar_move, nc.vector.tensor_copy)):
+            move(picked[:, 2, half(h)], c_raw[1][:, 0, :].indirect(offsets[:, h * HALF // 16 : (h + 1) * HALF // 16]))
+        dc3 = tile([P, SLOTS], F32, "dc3", "c_raw1")
         for h in range(2):
             nc.scalar.copy(dc3[:, half(h)], banks[1][:, half(h)])
         for h in range(2):
             scatter(3, h, dc3[:, half(h)])
         for h in range(2):
-            nc.vector.tensor_copy(picked[:, 3, half(h)], c_raw[1][:, 1, :].indirect(offsets[:, h * HALF // 16 : (h + 1) * HALF // 16]))
+            nc.vector.tensor_copy(picked[:, 3, half(h)], c_raw[2][:, 0, :].indirect(offsets[:, h * HALF // 16 : (h + 1) * HALF // 16]))
         c_woven = [tile([P, PACK * HALF], BF16, "c_woven%d" % h)[:] for h in range(2)]
         c_mx = mx_tiles("c", SLOTS)
         for h in range(2):
@@ -200,11 +200,11 @@ def tile_attend_gsoftc_kernel(tc, cT, dvT, pm, pw, offs, out_0, out_1):
         minus_s = [tile([P, 1], F32, "minus_s%d" % t) for t in range(PACK)]
         pairs = [tile([P, 2, SLOTS], F32, "result%d" % u) for u in range(2)]
         result = [pairs[t // 2][:, t % 2, :] for t in range(PACK)]
-        centred = tile([P, 2, SLOTS], F32, "centred")
+        centred = tile([P, SLOTS], F32, "centred")
 
         def finish_aside(t, cols):
-            nc.scalar.activation(centred[:, t // 2, cols], dp[t][:, cols], IDENTITY, bias=minus_s[t][:])
-            nc.gpsimd.tensor_tensor(result[t][:, cols], centred[:, t // 2, cols], pm_sb[:, t, cols], MULT)
+            nc.scalar.activation(centred[:, cols], dp[t][:, cols], IDENTITY, bias=minus_s[t][:])
+            nc.gpsimd.tensor_tensor(result[t][:, cols], centred[:, cols], pm_sb[:, t, cols], MULT)
 
         def finish(t, cols):
             nc.vector.scalar_tensor_tensor(result[t][:, cols], dp[t][:, cols], minus_s[t][:], pm_sb[:, t, cols], ADD, MULT)
@@ -214,9 +214,6 @@ def tile_attend_gsoftc_kernel(tc, cT, dvT, pm, pw, offs, out_0, out_1):
             if t == 0:
                 for h in range(2):
                     finish_aside(t, half(h))
-            elif t == 2:
-                finish_aside(t, slice(0, ASIDE))
-                finish(t, slice(ASIDE, SLOTS))
             else:
                 finish(t, slice(0, SLOTS))
             if t % 2:

@@ -47,7 +47,7 @@ def tile_attend_gsoftc_kernel(tc, cT, dvT, pm, pw, offs, out_0, out_1):
         offsets = sb.tile([P, SLOTS // 16], U16, name="offsets")
         pw_raw = [tile([P, PACK, HALF], F32, "pw_raw%d" % h) for h in range(2)]
         dv_raw = [tile([P, 2 * R], F32, "dv_raw%d" % u) for u in range(2)]
-        c_raw = [tile([P, planes, T], F32, "c_raw%d" % u) for u, planes in enumerate((2, 1, 1))]
+        c_raw = [tile([P, 2, T], F32, "c_raw%d" % u) for u in range(2)]
         pm_sb = tile([P, PACK, SLOTS], F32, "pm_sb")
 
         dv_rows = dvT.rearrange("(p j) r -> p (j r)", j=PACK)
@@ -58,8 +58,8 @@ def tile_attend_gsoftc_kernel(tc, cT, dvT, pm, pw, offs, out_0, out_1):
             nc.sync.dma_start(pw_raw[h][:], pw_rows[:, :, half(h)])
         nc.sync.dma_start(offsets[:], offs)
         nc.sync.dma_start(dv_raw[1][:], dv_rows[:, 2 * R :])
-        for raw, planes in zip(c_raw, (slice(0, 2), slice(2, 3), slice(3, 4))):
-            nc.sync.dma_start(raw[:], c_rows[:, planes, :])
+        for u in range(2):
+            nc.sync.dma_start(c_raw[u][:], c_rows[:, 2 * u : 2 * u + 2, :])
         nc.sync.dma_start(pm_sb[:], pm.rearrange("(q t) i -> q t i", t=PACK))
 
         ident = tile([P, P], F32, "ident")
@@ -135,14 +135,16 @@ def tile_attend_gsoftc_kernel(tc, cT, dvT, pm, pw, offs, out_0, out_1):
         quantize(dvr[1], slice(0, P), turned[1], E5M2)
         b = bank([P, HALF], "dc_bank10", 4)
         product(b[:], dvr[1], 0, pw_mx, half(0))
-        scatter(1, 0, copied("dc10", b[:], nc.vector.tensor_copy)[:])
+        dc10 = copied("dc10", b[:], nc.scalar.copy)
         quantize(pw_mx, half(1), pw_woven[1], E4M3)
-        b = bank([P, 2, HALF], "dc_bank01", 5)
+        second = []
+        for j, copy in enumerate((nc.scalar.copy, nc.vector.tensor_copy)):
+            b = bank([P, HALF], "dc_bank%d1" % j, (5, 0)[j])
+            product(b[:], dvr[j], 0, pw_mx, half(1))
+            second.append(copied("dc%d1" % j, b[:], copy))
+        scatter(1, 0, dc10[:])
         for j in range(2):
-            product(b[:, j, :], dvr[j], 0, pw_mx, half(1))
-        second = copied("dc01", b[:], nc.vector.tensor_copy)
-        for j in range(2):
-            scatter(j, 1, second[:, j, :])
+            scatter(j, 1, second[j][:])
 
         dvd = [mx_tiles("dvd0", 2 * P)]
 
@@ -172,15 +174,14 @@ def tile_attend_gsoftc_kernel(tc, cT, dvT, pm, pw, offs, out_0, out_1):
         nc.sync.dma_start(out1_rows[:, 2, :], windows[2][:])
         for j in range(2):
             scalar_move(picked[:, j, :], c_raw[0][:, j, :].indirect(offsets[:]))
-        for h, move in enumerate((scalar_move, nc.vector.tensor_copy)):
-            move(picked[:, 2, half(h)], c_raw[1][:, 0, :].indirect(offsets[:, h * HALF // 16 : (h + 1) * HALF // 16]))
-        dc3 = tile([P, SLOTS], F32, "dc3", "c_raw1")
+        nc.vector.tensor_copy(picked[:, 2, :], c_raw[1][:, 0, :].indirect(offsets[:]))
+        dc3 = tile([P, SLOTS], F32, "dc3", "c_raw0")
         for h in range(2):
             nc.scalar.copy(dc3[:, half(h)], banks[1][:, half(h)])
         for h in range(2):
             scatter(3, h, dc3[:, half(h)])
         for h in range(2):
-            nc.vector.tensor_copy(picked[:, 3, half(h)], c_raw[2][:, 0, :].indirect(offsets[:, h * HALF // 16 : (h + 1) * HALF // 16]))
+            nc.vector.tensor_copy(picked[:, 3, half(h)], c_raw[1][:, 1, :].indirect(offsets[:, h * HALF // 16 : (h + 1) * HALF // 16]))
         c_woven = [tile([P, PACK * HALF], BF16, "c_woven%d" % h)[:] for h in range(2)]
         c_mx = mx_tiles("c", SLOTS)
         for h in range(2):

@@ -22,6 +22,7 @@ IDENTITY = mybir.ActivationFunctionType.Identity
 P = 128
 PACK = 4
 HALF = SLOTS // 2
+SHARE = 64
 ALIGN = 256
 
 
@@ -46,18 +47,17 @@ def tile_attend_gsoftc_kernel(tc, cT, dvT, pm, pw, offs, out_0, out_1):
 
         offsets = sb.tile([P, SLOTS // 16], U16, name="offsets")
         pw_raw = [tile([P, PACK, HALF], F32, "pw_raw%d" % h) for h in range(2)]
-        dv_raw = [tile([P, 2 * R], F32, "dv_raw%d" % u) for u in range(2)]
+        dv_raw = tile([P, PACK * R], F32, "dv_raw")
         c_raw = [tile([P, 2, T], F32, "c_raw%d" % u) for u in range(2)]
         pm_sb = tile([P, PACK, SLOTS], F32, "pm_sb")
 
         dv_rows = dvT.rearrange("(p j) r -> p (j r)", j=PACK)
         pw_rows = pw.rearrange("(p t) i -> p t i", t=PACK)
         c_rows = cT.rearrange("(p j) t -> p j t", j=PACK)
-        nc.sync.dma_start(dv_raw[0][:], dv_rows[:, : 2 * R])
+        nc.sync.dma_start(dv_raw[:], dv_rows)
         for h in range(2):
             nc.sync.dma_start(pw_raw[h][:], pw_rows[:, :, half(h)])
         nc.sync.dma_start(offsets[:], offs)
-        nc.sync.dma_start(dv_raw[1][:], dv_rows[:, 2 * R :])
         for u in range(2):
             nc.sync.dma_start(c_raw[u][:], c_rows[:, 2 * u : 2 * u + 2, :])
         nc.sync.dma_start(pm_sb[:], pm.rearrange("(q t) i -> q t i", t=PACK))
@@ -84,8 +84,8 @@ def tile_attend_gsoftc_kernel(tc, cT, dvT, pm, pw, offs, out_0, out_1):
                                 rhs=mx[0][:, cols].bitcast(E4M3), rhs_scale=mx[1][:, cols], start=True, stop=True)
 
         rounded = tile([P, PACK * R], BF16, "rounded")
-        pw_woven = [tile([P, PACK * HALF], BF16, "pw_woven%d" % h)[:] for h in range(2)]
-        turned_places = (pw_woven[1][:, :R], rounded[:, 3 * R :])
+        pw_woven = [dv_raw[:, :R].bitcast(BF16), tile([P, PACK * HALF], BF16, "pw_woven1")[:]]
+        turned_places = (pw_woven[1][:, :R], tile([P, R], BF16, "turned1")[:])
 
         def round_dv(first, planes, raw, copy):
             copy(rounded[:, first * R : (first + planes) * R].rearrange("p (j w q e) -> p j w q e", j=planes, w=2, e=2),
@@ -119,12 +119,16 @@ def tile_attend_gsoftc_kernel(tc, cT, dvT, pm, pw, offs, out_0, out_1):
             copy(dc[:], src)
             return dc
 
-        for j in range(2):
-            round_dv(j, 1, dv_raw[0][:, j * R : (j + 1) * R], nc.scalar.copy)
-        turned = [weave_turned(turned_places[j], transpose_words(j, 1, j), nc.scalar.copy) for j in range(2)]
+        round_dv(0, 1, dv_raw[:, :R], nc.vector.tensor_copy)
+        round_dv(1, 1, dv_raw[:, R : 2 * R], nc.scalar.copy)
+        round_dv(2, 2, dv_raw[:, 2 * R :], nc.vector.tensor_copy)
+        turned = [weave_turned(turned_places[0], transpose_words(0, 1, 0), nc.scalar.copy)]
+        nc.scalar.copy(*weave_views(pw_woven[0][:, : PACK * SHARE], pw_raw[0][:, :, :SHARE]))
+        turned.append(weave_turned(turned_places[1], transpose_words(1, 1, 1), nc.scalar.copy))
+        turned23 = weave_turned(tile([P, 2 * R], BF16, "turned2")[:], transpose_words(2, 2, 2), nc.scalar.copy)
         dvr = [mx_tiles("dvr0", P), mx_tiles("dvr1", P), mx_tiles("dvr23", 2 * P)]
         pw_mx = mx_tiles("pw", SLOTS)
-        nc.vector.tensor_copy(*weave_views(pw_woven[0], pw_raw[0][:]))
+        nc.vector.tensor_copy(*weave_views(pw_woven[0][:, PACK * SHARE :], pw_raw[0][:, :, SHARE:]))
         quantize(dvr[0], slice(0, P), turned[0], E5M2)
         quantize(pw_mx, half(0), pw_woven[0], E4M3)
 
@@ -135,16 +139,16 @@ def tile_attend_gsoftc_kernel(tc, cT, dvT, pm, pw, offs, out_0, out_1):
         quantize(dvr[1], slice(0, P), turned[1], E5M2)
         b = bank([P, HALF], "dc_bank10", 4)
         product(b[:], dvr[1], 0, pw_mx, half(0))
-        dc10 = copied("dc10", b[:], nc.scalar.copy)
+        scatter(1, 0, copied("dc10", b[:], nc.vector.tensor_copy)[:])
         quantize(pw_mx, half(1), pw_woven[1], E4M3)
-        second = []
         for j, copy in enumerate((nc.scalar.copy, nc.vector.tensor_copy)):
             b = bank([P, HALF], "dc_bank%d1" % j, (5, 0)[j])
             product(b[:], dvr[j], 0, pw_mx, half(1))
-            second.append(copied("dc%d1" % j, b[:], copy))
-        scatter(1, 0, dc10[:])
+            scatter(j, 1, copied("dc%d1" % j, b[:], copy)[:])
+        quantize(dvr[2], slice(0, 2 * P), turned23, E5M2)
+        banks = [bank([P, SLOTS], "dc_bank%d" % (2 + j), 6 + j) for j in range(2)]
         for j in range(2):
-            scatter(j, 1, second[j][:])
+            product(banks[j][:], dvr[2], j, pw_mx, slice(0, SLOTS))
 
         dvd = [mx_tiles("dvd0", 2 * P)]
 
@@ -153,31 +157,22 @@ def tile_attend_gsoftc_kernel(tc, cT, dvT, pm, pw, offs, out_0, out_1):
                                   rounded[:].rearrange("p (j w q e) -> p w q j e", j=PACK, w=2, e=2)[:, w, :, :, :])
             return woven
 
-        round_dv(2, 2, dv_raw[1][:], nc.vector.tensor_copy)
-        turned_bank = transpose_words(2, 2, 2)
-        dvd_woven = weave_dvd(0, tile([P, 2 * R], BF16, "dvd_woven")[:])
-        turned23 = weave_turned(tile([P, 2 * R], BF16, "turned2")[:], turned_bank, nc.vector.tensor_copy)
+        dvd_woven = weave_dvd(0, tile([P, 2 * R], BF16, "dvd_woven", "pw_woven1")[:])
         quantize(dvd[0], slice(0, 2 * P), dvd_woven, E5M2)
-        quantize(dvr[2], slice(0, 2 * P), turned23, E5M2)
-        banks = [bank([P, SLOTS], "dc_bank%d" % (2 + j), 6 + j) for j in range(2)]
-        for j in range(2):
-            product(banks[j][:], dvr[2], j, pw_mx, slice(0, SLOTS))
         dvd_woven = weave_dvd(1, tile([P, 2 * R], BF16, "dvd_woven1", "turned2")[:])
 
-        gathered = tile([P, PACK * SLOTS], F32, "gathered", "dvd_woven")
+        gathered = tile([P, PACK * SLOTS], F32, "gathered", "rounded")
         picked = gathered[:].rearrange("p (j i) -> p j i", j=PACK)
         dc2 = gathered[:, 11 * SLOTS // 4 : 15 * SLOTS // 4]
         nc.vector.tensor_copy(dc2, banks[0][:])
-        windows.append(tile([P, T], F32, "window3", "rounded"))
+        dc3 = copied("dc3", banks[1][:], nc.vector.tensor_copy)
+        windows.append(tile([P, T], F32, "window3", "pw_woven1"))
         nc.gpsimd.memset(windows[3][:].bitcast(I32), 0)
         nc.vector.tensor_copy(windows[2][:].indirect(offsets[:]), dc2)
         nc.sync.dma_start(out1_rows[:, 2, :], windows[2][:])
         for j in range(2):
             scalar_move(picked[:, j, :], c_raw[0][:, j, :].indirect(offsets[:]))
         nc.vector.tensor_copy(picked[:, 2, :], c_raw[1][:, 0, :].indirect(offsets[:]))
-        dc3 = tile([P, SLOTS], F32, "dc3", "c_raw0")
-        for h in range(2):
-            nc.scalar.copy(dc3[:, half(h)], banks[1][:, half(h)])
         for h in range(2):
             scatter(3, h, dc3[:, half(h)])
         for h in range(2):

@@ -85,7 +85,7 @@ def tile_attend_gsoftc_kernel(tc, cT, dvT, pm, pw, offs, out_0, out_1):
 
         rounded = tile([P, PACK * R], BF16, "rounded")
         pw_woven = [dv_raw[:, :R].bitcast(BF16), tile([P, PACK * HALF], BF16, "pw_woven1")[:]]
-        turned_places = (pw_woven[1][:, :R], tile([P, R], BF16, "turned1")[:])
+        turned_places = (pw_woven[1][:, :R], pw_woven[1][:, R:])
 
         def round_dv(first, planes, raw, copy):
             copy(rounded[:, first * R : (first + planes) * R].rearrange("p (j w q e) -> p j w q e", j=planes, w=2, e=2),
@@ -132,20 +132,21 @@ def tile_attend_gsoftc_kernel(tc, cT, dvT, pm, pw, offs, out_0, out_1):
         quantize(dvr[0], slice(0, P), turned[0], E5M2)
         quantize(pw_mx, half(0), pw_woven[0], E4M3)
 
-        b = bank([P, HALF], "dc_bank00", 3)
-        product(b[:], dvr[0], 0, pw_mx, half(0))
-        scatter(0, 0, copied("dc00", b[:], nc.scalar.copy)[:])
-        nc.vector.tensor_copy(*weave_views(pw_woven[1], pw_raw[1][:]))
         quantize(dvr[1], slice(0, P), turned[1], E5M2)
-        b = bank([P, HALF], "dc_bank10", 4)
-        product(b[:], dvr[1], 0, pw_mx, half(0))
-        scatter(1, 0, copied("dc10", b[:], nc.vector.tensor_copy)[:])
-        quantize(pw_mx, half(1), pw_woven[1], E4M3)
-        for j, copy in enumerate((nc.scalar.copy, nc.vector.tensor_copy)):
-            b = bank([P, HALF], "dc_bank%d1" % j, (5, 0)[j])
-            product(b[:], dvr[j], 0, pw_mx, half(1))
-            scatter(j, 1, copied("dc%d1" % j, b[:], copy)[:])
+
+        first = []
+        for j in range(2):
+            b = bank([P, HALF], "dc_bank%d0" % j, 3 + j)
+            product(b[:], dvr[j], 0, pw_mx, half(0))
+            first.append(copied("dc%d0" % j, b[:], nc.scalar.copy))
+        for j in range(2):
+            scatter(j, 0, first[j][:])
+        nc.vector.tensor_copy(*weave_views(pw_woven[1], pw_raw[1][:]))
         quantize(dvr[2], slice(0, 2 * P), turned23, E5M2)
+        quantize(pw_mx, half(1), pw_woven[1], E4M3)
+        second_bank = bank([P, 2, HALF], "dc_bank01", 5)
+        for j in range(2):
+            product(second_bank[:, 1 - j, :], dvr[j], 0, pw_mx, half(1))
         banks = [bank([P, SLOTS], "dc_bank%d" % (2 + j), 6 + j) for j in range(2)]
         for j in range(2):
             product(banks[j][:], dvr[2], j, pw_mx, slice(0, SLOTS))
@@ -161,22 +162,29 @@ def tile_attend_gsoftc_kernel(tc, cT, dvT, pm, pw, offs, out_0, out_1):
         quantize(dvd[0], slice(0, 2 * P), dvd_woven, E5M2)
         dvd_woven = weave_dvd(1, tile([P, 2 * R], BF16, "dvd_woven1", "turned2")[:])
 
-        gathered = tile([P, PACK * SLOTS], F32, "gathered", "rounded")
+        gathered = tile([P, PACK * SLOTS], F32, "gathered")
         picked = gathered[:].rearrange("p (j i) -> p j i", j=PACK)
-        dc2 = gathered[:, 11 * SLOTS // 4 : 15 * SLOTS // 4]
+        second = gathered[:, SLOTS // 4 : 9 * SLOTS // 4].rearrange("p (j i) -> p j i", j=2)[:, :, :HALF]
+        dc2 = gathered[:, 9 * SLOTS // 4 : 13 * SLOTS // 4]
         nc.vector.tensor_copy(dc2, banks[0][:])
+        nc.vector.tensor_copy(second, second_bank[:])
+        for j in range(2):
+            scatter(j, 1, second[:, 1 - j, :])
         dc3 = copied("dc3", banks[1][:], nc.vector.tensor_copy)
         windows.append(tile([P, T], F32, "window3", "pw_woven1"))
         nc.gpsimd.memset(windows[3][:].bitcast(I32), 0)
         nc.vector.tensor_copy(windows[2][:].indirect(offsets[:]), dc2)
         nc.sync.dma_start(out1_rows[:, 2, :], windows[2][:])
-        for j in range(2):
-            scalar_move(picked[:, j, :], c_raw[0][:, j, :].indirect(offsets[:]))
-        nc.vector.tensor_copy(picked[:, 2, :], c_raw[1][:, 0, :].indirect(offsets[:]))
+
+        def gather(j, first, last, move):
+            move(picked[:, j, first:last], c_raw[j // 2][:, j % 2, :].indirect(offsets[:, first // 16 : last // 16]))
+
+        for j, last in ((1, HALF), (0, SLOTS), (2, HALF)):
+            gather(j, 0, last, scalar_move)
+        for j, start in ((1, HALF), (3, 0), (2, HALF)):
+            gather(j, start, SLOTS, nc.vector.tensor_copy)
         for h in range(2):
             scatter(3, h, dc3[:, half(h)])
-        for h in range(2):
-            nc.vector.tensor_copy(picked[:, 3, half(h)], c_raw[1][:, 1, :].indirect(offsets[:, h * HALF // 16 : (h + 1) * HALF // 16]))
         c_woven = [tile([P, PACK * HALF], BF16, "c_woven%d" % h)[:] for h in range(2)]
         c_mx = mx_tiles("c", SLOTS)
         for h in range(2):

from contextlib import ExitStack

import concourse.mybir as mybir
from concourse.masks import make_identity

D, R, SLOTS, T = 512, 512, 512, 2048
FLOPS = 2 * 2 * D * R * SLOTS

F32 = mybir.dt.float32
BF16 = mybir.dt.bfloat16
I32 = mybir.dt.int32
U32 = mybir.dt.uint32
U16 = mybir.dt.uint16
U8 = mybir.dt.uint8
E4M3 = mybir.dt.float8_e4m3fn_x4
E5M2 = mybir.dt.float8_e5m2_x4
COPY = mybir.ActivationFunctionType.Copy
MULT = mybir.AluOpType.mult
ADD = mybir.AluOpType.add
IDENTITY = mybir.ActivationFunctionType.Identity

P = 128
PACK = 4
HALF = SLOTS // 2
SHARE = 64
ALIGN = 256


def weave_views(dst, src):
    return dst.rearrange("p (c i t) -> p c t i", i=4, t=PACK), src.rearrange("p t (c i) -> p c t i", i=4)


def tile_attend_gsoftc_kernel(tc, cT, dvT, pm, pw, offs, out_0, out_1):
    nc = tc.nc
    with ExitStack() as ctx:
        sb = ctx.enter_context(tc.tile_pool(name="sb", bufs=1))
        psum = ctx.enter_context(tc.psum_pool(name="psum", bufs=1))

        def tile(shape, dtype, name, tag=None):
            return sb.tile(shape, dtype, name=name, tag=tag or name, align_bytes=ALIGN)

        def bank(shape, name, nr):
            return psum.tile(shape, F32, name=name, tag="bank%d" % nr)

        def half(h):
            return slice(h * HALF, (h + 1) * HALF)

        offsets = sb.tile([P, SLOTS // 16], U16, name="offsets")
        pw_raw = [tile([P, PACK, HALF], F32, "pw_raw%d" % h) for h in range(2)]
        dv_raw = tile([P, PACK * R], F32, "dv_raw")
        c_raw = [tile([P, 2, T], F32, "c_raw%d" % u) for u in range(2)]
        pm_sb = tile([P, PACK, SLOTS], F32, "pm_sb")

        dv_rows = dvT.rearrange("(p j) r -> p (j r)", j=PACK)
        pw_rows = pw.rearrange("(p t) i -> p t i", t=PACK)
        c_rows = cT.rearrange("(p j) t -> p j t", j=PACK)
        nc.sync.dma_start(dv_raw[:], dv_rows)
        for h in range(2):
            nc.sync.dma_start(pw_raw[h][:], pw_rows[:, :, half(h)])
        nc.sync.dma_start(offsets[:], offs)
        for u in range(2):
            nc.sync.dma_start(c_raw[u][:], c_rows[:, 2 * u : 2 * u + 2, :])
        nc.sync.dma_start(pm_sb[:], pm.rearrange("(q t) i -> q t i", t=PACK))

        ident = tile([P, P], F32, "ident")
        make_identity(nc, ident[:])
        windows = [tile([P, T], F32, "window%d" % w) for w in range(3)]
        for words in (windows[0][:].bitcast(I32), windows[2][:, : T // 2].bitcast(I32)):
            cut = words.shape[1] // 2 - 1
            nc.vector.memset(words[:, :cut], 0)
            nc.vector.memset(words[:, cut:], 0)
        for words in (windows[1][:].bitcast(I32), windows[2][:, T // 2 :].bitcast(I32)):
            nc.gpsimd.memset(words, 0)

        def mx_tiles(name, width):
            return tile([P, width], U32, name + "_codes"), tile([P, width], U8, name + "_scales")

        def quantize(mx, cols, woven, fmt):
            nc.vector.quantize_mx(out=mx[0][:, cols].bitcast(fmt), scales=mx[1][:, cols], in_=woven)

        def product(out, dv_mx, block, mx, cols):
            rows = slice(block * P, (block + 1) * P)
            nc.tensor.matmul_mx(out=out, lhsT=dv_mx[0][:, rows].bitcast(E5M2), lhsT_scale=dv_mx[1][:, rows],
                                rhs=mx[0][:, cols].bitcast(E4M3), rhs_scale=mx[1][:, cols], start=True, stop=True)

        rounded = tile([P, PACK * R], BF16, "rounded")
        pw_woven = [dv_raw[:, :R].bitcast(BF16), tile([P, PACK * HALF], BF16, "pw_woven1")[:]]
        turned_places = (pw_woven[1][:, :R], pw_woven[1][:, R:])

        def round_dv(first, planes, raw, copy):
            copy(rounded[:, first * R : (first + planes) * R].rearrange("p (j w q e) -> p j w q e", j=planes, w=2, e=2),
                 raw.rearrange("p (j q w e) -> p j w q e", j=planes, w=2, e=2))

        def transpose_words(first, planes, nr):
            turned = bank([P, planes, 2, P], "turned_bank%d" % first, nr)
            words = rounded[:, first * R : (first + planes) * R].bitcast(F32)
            for j in range(planes):
                for w in range(2):
                    start = (2 * j + w) * P
                    nc.tensor.transpose(turned[:, j, w, :], words[:, start : start + P], ident[:])
            return turned

        def weave_turned(woven, turned, copy):
            copy(woven.bitcast(F32).rearrange("q (j p w) -> q j p w", p=P, w=2), turned[:].rearrange("q j w p -> q j p w"))
            return woven

        out1_rows = out_1.rearrange("(p j) t -> p j t", j=PACK)

        def scalar_move(out, in_):
            nc.scalar.activation(out, in_, COPY)

        def scatter(j, h, dc):
            scalar_move(windows[j][:].indirect(offsets[:, h * HALF // 16 : (h + 1) * HALF // 16]), dc)
            if h == 1:
                nc.sync.dma_start(out1_rows[:, j, :], windows[j][:])

        def copied(name, src, copy, tag=None):
            dc = tile(list(src.shape), F32, name, tag)
            copy(dc[:], src)
            return dc

        round_dv(0, 1, dv_raw[:, :R], nc.vector.tensor_copy)
        round_dv(1, 1, dv_raw[:, R : 2 * R], nc.scalar.copy)
        round_dv(2, 2, dv_raw[:, 2 * R :], nc.vector.tensor_copy)
        turned = [weave_turned(turned_places[0], transpose_words(0, 1, 0), nc.scalar.copy)]
        nc.scalar.copy(*weave_views(pw_woven[0][:, : PACK * SHARE], pw_raw[0][:, :, :SHARE]))
        turned.append(weave_turned(turned_places[1], transpose_words(1, 1, 1), nc.scalar.copy))
        turned23 = weave_turned(tile([P, 2 * R], BF16, "turned2")[:], transpose_words(2, 2, 2), nc.scalar.copy)
        dvr = [mx_tiles("dvr0", P), mx_tiles("dvr1", P), mx_tiles("dvr23", 2 * P)]
        pw_mx = mx_tiles("pw", SLOTS)
        nc.vector.tensor_copy(*weave_views(pw_woven[0][:, PACK * SHARE :], pw_raw[0][:, :, SHARE:]))
        quantize(dvr[0], slice(0, P), turned[0], E5M2)
        quantize(pw_mx, half(0), pw_woven[0], E4M3)

        quantize(dvr[1], slice(0, P), turned[1], E5M2)

        first = []
        for j in range(2):
            b = bank([P, HALF], "dc_bank%d0" % j, 3 + j)
            product(b[:], dvr[j], 0, pw_mx, half(0))
            first.append(copied("dc%d0" % j, b[:], nc.scalar.copy))
        for j in range(2):
            scatter(j, 0, first[j][:])
        nc.vector.tensor_copy(*weave_views(pw_woven[1], pw_raw[1][:]))
        quantize(dvr[2], slice(0, 2 * P), turned23, E5M2)
        quantize(pw_mx, half(1), pw_woven[1], E4M3)
        second_bank = bank([P, 2, HALF], "dc_bank01", 5)
        for j in range(2):
            product(second_bank[:, 1 - j, :], dvr[j], 0, pw_mx, half(1))
        banks = [bank([P, SLOTS], "dc_bank%d" % (2 + j), 6 + j) for j in range(2)]
        for j in range(2):
            product(banks[j][:], dvr[2], j, pw_mx, slice(0, SLOTS))

        dvd = [mx_tiles("dvd0", 2 * P)]

        def weave_dvd(w, woven):
            nc.vector.tensor_copy(woven.rearrange("p (e q j) -> p q j e", e=2, j=PACK),
                                  rounded[:].rearrange("p (j w q e) -> p w q j e", j=PACK, w=2, e=2)[:, w, :, :, :])
            return woven

        dvd_woven = weave_dvd(0, tile([P, 2 * R], BF16, "dvd_woven", "pw_woven1")[:])
        quantize(dvd[0], slice(0, 2 * P), dvd_woven, E5M2)
        dvd_woven = weave_dvd(1, tile([P, 2 * R], BF16, "dvd_woven1", "turned2")[:])

        gathered = tile([P, PACK * SLOTS], F32, "gathered")
        picked = gathered[:].rearrange("p (j i) -> p j i", j=PACK)
        second = gathered[:, SLOTS // 4 : 9 * SLOTS // 4].rearrange("p (j i) -> p j i", j=2)[:, :, :HALF]
        dc2 = gathered[:, 9 * SLOTS // 4 : 13 * SLOTS // 4]
        nc.vector.tensor_copy(dc2, banks[0][:])
        nc.vector.tensor_copy(second, second_bank[:])
        for j in range(2):
            scatter(j, 1, second[:, 1 - j, :])
        dc3 = copied("dc3", banks[1][:], nc.vector.tensor_copy)
        windows.append(tile([P, T], F32, "window3", "pw_woven1"))
        nc.gpsimd.memset(windows[3][:].bitcast(I32), 0)
        nc.vector.tensor_copy(windows[2][:].indirect(offsets[:]), dc2)
        nc.sync.dma_start(out1_rows[:, 2, :], windows[2][:])

        def gather(j, first, last, move):
            move(picked[:, j, first:last], c_raw[j // 2][:, j % 2, :].indirect(offsets[:, first // 16 : last // 16]))

        for j, last in ((1, HALF), (0, SLOTS), (2, HALF)):
            gather(j, 0, last, scalar_move)
        for j, start in ((1, HALF), (3, 0), (2, HALF)):
            gather(j, start, SLOTS, nc.vector.tensor_copy)
        for h in range(2):
            scatter(3, h, dc3[:, half(h)])
        c_woven = [tile([P, PACK * HALF], BF16, "c_woven%d" % h)[:] for h in range(2)]
        c_mx = mx_tiles("c", SLOTS)
        for h in range(2):
            nc.vector.tensor_copy(*weave_views(c_woven[h], picked[:, :, half(h)]))
        for h in range(2):
            quantize(c_mx, half(h), c_woven[h], E4M3)
        dvd.append((tile([P, 2 * P], U32, "dvd1_codes", "c_woven0"), tile([P, 2 * P], U8, "dvd1_scales")))
        quantize(dvd[1], slice(0, 2 * P), dvd_woven, E5M2)

        out0_rows = out_0.rearrange("(q t) i -> q t i", t=PACK)
        dp = [bank([P, SLOTS], "dp%d" % t, 1 + t) for t in range(PACK)]
        for h in range(2):
            product(dp[0][:, half(h)], dvd[0], 0, c_mx, half(h))
        for t in range(1, PACK):
            product(dp[t][:], dvd[t // 2], t % 2, c_mx, slice(0, SLOTS))
        weighted = [tile([P, SLOTS], F32, "weighted%d" % t) for t in range(PACK)]
        minus_s = [tile([P, 1], F32, "minus_s%d" % t) for t in range(PACK)]
        pairs = [tile([P, 2, SLOTS], F32, "result%d" % u) for u in range(2)]
        result = [pairs[t // 2][:, t % 2, :] for t in range(PACK)]
        centred = tile([P, SLOTS], F32, "centred")

        def finish_aside(t, cols):
            nc.scalar.activation(centred[:, cols], dp[t][:, cols], IDENTITY, bias=minus_s[t][:])
            nc.gpsimd.tensor_tensor(result[t][:, cols], centred[:, cols], pm_sb[:, t, cols], MULT)

        def finish(t, cols):
            nc.vector.scalar_tensor_tensor(result[t][:, cols], dp[t][:, cols], minus_s[t][:], pm_sb[:, t, cols], ADD, MULT)

        for t in range(PACK):
            nc.vector.scalar_tensor_tensor(weighted[t][:], dp[t][:], -1.0, pm_sb[:, t, :], MULT, MULT, accum_out=minus_s[t][:])
            if t == 0:
                for h in range(2):
                    finish_aside(t, half(h))
            else:
                finish(t, slice(0, SLOTS))
            if t % 2:
                nc.sync.dma_start(out0_rows[:, t - 1 : t + 1, :], pairs[t // 2][:])
